import numpy as np, ml_dtypes
CORES = [113,118,241,246]
N = 4
BF = ml_dtypes.bfloat16
def f(rng, *shape):
    return (rng.standard_normal(shape, dtype=np.float32) * np.exp2(rng.integers(-2, 3, shape[:-1] + (1,)))).astype(BF)
def wide(rng, *shape):
    v = f(rng, *shape).astype(np.float32); k = shape[:-2] + (1, shape[-1])
    return (v * np.exp2(rng.integers(-6, 7, k)) * (rng.random(k) > 0.0625)).astype(BF)
def entries(a):
    return np.ascontiguousarray(a.T).reshape(-1)
def table(e):
    return np.ascontiguousarray(np.reshape(e, (-1, 16)).T).astype(np.int32)
K, V, A, R = 4096, 6144, 6144, 256
CAP, U, HS, AS = 96, 112, 2, 5
TM = 1048576
def fine(rng, v):
    return v.astype(np.float32) * (1 + rng.random(v.shape, dtype=np.float32))
def moments(rng, uneven, *shape):
    return np.floor(np.exp2(rng.random(shape) * 20)).astype(np.int64) - 1 if uneven else rng.integers(0, TM, shape)
def owners(rng, without=-1):
    return np.stack([rng.permutation(np.repeat(np.array([q for q in range(N) if q != without]), CAP))[:R] for r in range(N)])
def full(rng):
    o = []
    for r in range(N):
        a, b = (r + 1) % N, (r + 2) % N
        rest = rng.permutation(np.repeat(np.array([q for q in range(N) if q != a and q != b]), CAP))[:R - 2 * CAP]
        o.append(rng.permutation(np.concatenate([np.repeat(np.array([a, b]), CAP), rest])))
    return np.stack(o)
def make(rng, own, key, fall=True, share=False, edge=False, low=None, uneven=False):
    tt = moments(rng, uneven, N, 8, K, HS + AS)
    if fall: tt = -np.sort(-tt, axis=3)
    if low is not None: tt = tt // 2; tt[..., :HS] += TM // 2
    h = rng.integers(0, HS + 1, (N, 8, K))
    if edge: h = HS * rng.integers(0, 2, (N, 8, K)); h[:, :, :2] = HS
    ch = rng.integers(0, K, (N, 8, K)) if share else np.zeros((N, 8, K), np.int64) + np.arange(K)
    col, s = rng.integers(0, 8, (N, R)), rng.integers(0, HS + AS, (N, R)); tie = tt[own, col, ch[own, col, key], s]; u = rng.random((N, R))
    if edge: t = np.where(u < 0.2, 0, np.where(u < 0.4, TM - 1, np.where(u < 0.7, tie, np.maximum(tie - 1, 0))))
    else: t = np.where(u < 0.25, tie, moments(rng, uneven, N, R))
    if low is not None: t = np.where(low, rng.integers(0, TM // 2, (N, R)), t)
    M = min(3 * K // 4, 2 * A // (AS + 1))
    hd = np.zeros((N, 8, K), np.int32); vt = moments(rng, uneven, N, 8, V).astype(np.int32); at = moments(rng, uneven, N, 8, A).astype(np.int32)
    vp = rng.integers(0, V + A + 1, (N, 8, V)).astype(np.int32); ap = rng.integers(0, A + 1, (N, 8, A)).astype(np.int32)
    for q in range(N):
        got = own == q; kk, tk, z = key[got], t[got], (q + 1) % N
        for c in range(8):
            x = tt[q, c]; e = np.arange(HS)[:, None] < h[q, c]; no = np.cumsum(e.reshape(-1)).reshape(HS, K) - 1; e = e & (no < V); n = np.sum(e, axis=0)
            ln = rng.integers(1, AS + 1, M)
            if edge: ln = np.where(rng.integers(0, 2, M) > 0, AS, 1); ln[:2] = AS
            e2 = np.arange(AS)[:, None] < ln; no2 = np.cumsum(e2.reshape(-1)).reshape(AS, M) - 1; e2 = e2 & (no2 < A)
            sl, sl2 = rng.permutation(V), rng.permutation(A)
            if edge:
                sl, sl2 = np.arange(V), np.arange(A); sl[1], sl[V - 1] = V - 1, 1; sl2[1], sl2[A - 1] = A - 1, 1
            m = np.where(e2, sl2[np.minimum(no2, A - 1)], A)
            want = np.array([0, 1]) if edge else rng.permutation(kk[low[got]]) if low is not None else np.zeros(0, np.int64)
            p = rng.permutation(K); o = np.concatenate([want, p[~np.isin(p, want)]])[:M]
            cont = np.full(K, A); cont[o] = m[0][np.arange(M) // 2 if share else np.arange(M)]
            ci = ch[q, c][kk]; un = ~np.any((x[ci, :HS] <= tk[:, None]) & (np.arange(HS) < n[ci][:, None]), axis=1)
            w = np.bincount(ci[un], minlength=K); most = U if low is not None else int(rng.integers(U // 2, U + 1)); tot = 0
            for j in o[w[o] > 0].tolist():
                if tot + int(w[j]) <= most: tot += int(w[j])
                else: cont[j] = A
            nx = np.where(e, sl[np.minimum(no, V - 1)], V + cont)
            hd[q, c] = nx[0][ch[q, c]]; vp[q, c][nx[e]] = np.concatenate([nx[1:], (V + cont)[None]])[e]; vt[q, c][nx[e]] = x.T[:HS][e]
            ap[z, c][m[e2]] = np.concatenate([m[1:], np.full((1, M), A)])[e2]; at[z, c][m[e2]] = x[o, HS:].T[e2]
    vv, av = (fine(rng, wide(rng, N, 8, V)), fine(rng, wide(rng, N, 8, A))) if uneven else (fine(rng, f(rng, N, 8, V)), fine(rng, f(rng, N, 8, A)))
    return {"hd": hd, "vt": vt, "vp": vp, "vv": vv, "at": at, "ap": ap, "av": av, "rk": np.stack([table(own[r] * K + key[r]) for r in range(N)]), "rt": np.stack([table(t[r]) for r in range(N)])}
def setup_inputs(rng):
    return make(rng, owners(rng), rng.integers(0, K, (N, R)))
def setup_inputs_caps(rng):
    own = full(rng); key = np.zeros((N, R), np.int64)
    for q in range(N): key[own == q] = rng.permutation(K)[:np.count_nonzero(own == q)]
    far = (own - np.arange(N)[:, None]) % N
    return make(rng, own, key, low=(far == 1) | (far == 2))
def setup_inputs_few(rng):
    own = owners(rng, int(rng.integers(0, N))); pool = np.stack([rng.permutation(K)[:16] for q in range(N)])
    return make(rng, own, pool[own, rng.integers(0, 16, (N, R))])
def setup_inputs_edge(rng):
    pool = np.stack([np.concatenate([np.array([0, 1, K - 1]), 2 + rng.permutation(K - 3)[:29]]) for q in range(N)]); own = owners(rng)
    return make(rng, own, pool[own, rng.integers(0, 32, (N, R))], edge=True)
def setup_inputs_mixed(rng):
    return make(rng, owners(rng), rng.integers(0, K, (N, R)), fall=False, share=True)
def setup_inputs_spread(rng):
    return make(rng, owners(rng), rng.integers(0, K, (N, R)), uneven=True)
def check_inputs(d):
    bad = []
    for a, top in (("hd", V + A + 1), ("vt", TM), ("vp", V + A + 1), ("at", TM), ("ap", A + 1), ("rk", N * K), ("rt", TM)):
        if np.min(d[a]) < 0 or np.max(d[a]) >= top: bad.append(a + "_range")
    for a in ("vv", "av"):
        if not np.isfinite(d[a]).all(): bad.append(a + "_finite")
    if bad: return bad
    hd, vt, vp, n = d["hd"], d["vt"], d["vp"], d["hd"].astype(np.int64); ap = np.roll(d["ap"], -1, axis=0)
    for s in range(HS): n = np.where(n < V, np.take_along_axis(vp, np.minimum(n, V - 1), 2), n)
    if (n < V).any(): bad.append("chain_in_the_heap")
    n = np.maximum(n - V, 0)
    for s in range(AS): n = np.where(n < A, np.take_along_axis(ap, np.minimum(n, A - 1), 2), n)
    if (n < A).any(): bad.append("chain_in_the_archive")
    c = np.arange(8)[:, None]; un = np.zeros((N, 8), np.int64); most = 0
    for r in range(N):
        key, t = entries(d["rk"][r]), entries(d["rt"][r]); q = key // K; most = max(most, int(np.max(np.bincount(q, minlength=N)))); n = hd[q, c, key % K]
        for s in range(HS):
            i = np.minimum(n, V - 1); n = np.where(n < V, np.where(vt[q, c, i] <= t, V + A, vp[q, c, i]), n)
        for g in range(8): un[:, g] += np.bincount(q[(n[g] >= V) & (n[g] < V + A)], minlength=N)
    if most > CAP: bad.append("reads_of_a_pair")
    if np.max(un) > U: bad.append("unfinished_walks")
    return bad
def reference(hd, vt, vp, vv, at, ap, av, rk, rt):
    y = np.zeros((N, 8, R), np.float32); c = np.arange(8)[:, None]
    for r in range(N):
        key, t = entries(rk[r]), entries(rt[r]); q = key // K; z = (q + 1) % N
        n = hd[q, c, key % K]
        for s in range(HS):
            i = np.minimum(n, V - 1); hit = (n < V) & (vt[q, c, i] <= t)
            y[r] = np.where(hit, vv[q, c, i], y[r]); n = np.where(hit, V + A, np.where(n < V, vp[q, c, i], n))
        n = n - V
        for s in range(AS):
            i = np.minimum(n, A - 1); hit = (n < A) & (at[z, c, i] <= t)
            y[r] = np.where(hit, av[z, c, i], y[r]); n = np.where(hit, A, np.where(n < A, ap[z, c, i], n))
    return {"y": y}

@@ -1,0 +1,457 @@
+from concourse.bass import DstId, RemoteDMATransfer
+from concourse.mybir import AluOpType, AxisListType, ActivationFunctionType
+
+V = 6144
+W = 6152
+KEYS = 4096
+SEL = {"SHD": 0, "SVP": 1, "SAP": 2, "H2": 3, "H1": 4, "A0": 5, "A1": 6, "A2": 7, "A3": 8, "A4": 9}
+
+_f, _b, _i, _u = "float32", "bfloat16", "int32", "uint16"
+
+
+def _bufs():
+    s = {}
+
+    def sb(name, n, t):
+        s[name] = ("sbuf", [128, n], t)
+    sb("WH", KEYS, _b); sb("WP", W, _b); sb("W32", W, _f); sb("Z", 1024, _b)
+    sb("HC", 256, _i); sb("VC", 384, _i); sb("AC", 384, _i); sb("VTC", 384, _i); sb("ATC", 384, _i)
+    sb("HHI", 256, _b); sb("HLO", 256, _b); sb("VHI", 384, _b); sb("VLO", 384, _b); sb("AHI", 384, _b); sb("ALO", 384, _b)
+    sb("VTF", 384, _f); sb("ATF", 384, _f)
+    sb("I256", 256, _b); sb("ZI", 128, _b); sb("MOD16", 128, _b); sb("OFF", 8, _b); sb("PC", 1, _i); sb("PAT", 8, _i)
+    sb("PATI", 8, _i); sb("X", 128, _i); sb("XH", 128, _i); sb("Y", 192, _i); sb("Y15", 192, _i); sb("C1", 192, _f); sb("C", 192, _f)
+    sb("US", 128, _b); sb("UI", 128, _b); sb("IB", 128, _b); sb("IF", 128, _f); sb("S", 1280, _b)
+    sb("PINT", 8, _i); sb("COL", 4, _f); sb("COLP1", 4, _f); sb("EV1", 4, _f)
+    sb("RK", 2, _i); sb("RT", 2, _i); sb("OWNI", 2, _i); sb("OWNF", 2, _f); sb("KI", 4, _i); sb("KF", 4, _f); sb("TF", 2, _f)
+    sb("O", 8, _b); sb("PR", 8, _f); sb("WI", 2, _i); sb("AB", 4, _i); sb("ABF", 4, _f); sb("LH", 256, _b); sb("RH", 128, _b)
+    sb("LSTU", 32, _u); sb("SI", 2, _i); sb("SF", 2, _f); sb("SH", 256, _f); sb("RTT", 16, _f); sb("TS", 8, _f)
+    for r in range(4):
+        sb("LI%d" % r, 6, _u); sb("TC%d" % r, 2, _f)
+    sb("G", 384 * 7, _b); sb("SC", 384 * 9, _f); sb("L", 24 * 9, _u); sb("N", 24 * 4, _f); sb("E0", 24, _f); sb("E1", 24, _f)
+    sb("M0", 24, _u); sb("ALV", 24, _f); sb("ALS", 24, _f)
+    sb("TB", 1024, _f); sb("TH", 384, _f); sb("TA", 384, _f); sb("HIT", 384 * 7, _b)
+    sb("HN", 72, _f); sb("HD", 48, _f); sb("HI", 48, _f); sb("HP", 48, _f); sb("HX", 24, _f); sb("HCL", 24, _f)
+    sb("HV", 384, _f); sb("HT", 384, _f); sb("PKH", 32, _f)
+    sb("MF", 144, _f); sb("AD", 120, _f); sb("AI", 120, _f); sb("AP", 120, _f); sb("AX", 48, _f); sb("AY", 24, _f); sb("AZ", 24, _f)
+    sb("AW", 24, _f); sb("ACL", 24, _f); sb("AV", 384, _f); sb("AT", 384, _f); sb("PKA", 32, _f)
+    sb("LANDH", 32, _f); sb("LANDA", 32, _f); sb("LS", 32, _f); sb("WIN", 32, _f)
+    sb("FI", 4, _i); sb("FF", 4, _f); sb("FR", 32, _b); sb("C8", 128, _b); sb("FL", 16, _u); sb("QB", 256, _b); sb("JS", 512, _b)
+    sb("PF", 8, _f); sb("MASK", 256, _f); sb("R0", 128, _f)
+    sb("GM", 256, _f); sb("TR", 256, _f); sb("SCF", 256, _f); sb("OT", 32, _f); sb("YT", 32, _f)
+    for k in range(8):
+        s["P%d" % k] = ("psum", [128, 512], "float32")
+    return s
+
+
+SCRATCH = _bufs()
+LOADS = ["rk", "rt", "hd", "vp", "ap", "vt", "at", "hh", "hl", "vh", "vl", "ah", "al", "vv", "av", "vtr", "atr", "y0", "y1", "y2", "y3"]
+SEMAPHORES = (["sv", "ss", "st", "sg"] + ["d_" + x for x in LOADS]
+              + ["r%s%d" % (k, r) for k in "LTHA" for r in range(4)] + ["rMA", "rMB", "rAL"]
+              + ["xL", "xT", "xMA", "xMB", "xAL", "xH", "xA"])
+NE = 4
+
+
+def rank_program(g, core, T, topo):
+    me = T.rank_of(core)
+    if me is None:
+        return
+    OP, ACT, X = AluOpType, ActivationFunctionType, AxisListType.X
+    n_ranks = len(T.cores)
+    nxt, prv = (me + 1) % n_ranks, (me - 1) % n_ranks
+    eng = {"v": g.vector, "s": g.scalar, "t": g.tensor, "g": g, "y": g.sync}
+    semof = {"v": "sv", "s": "ss", "t": "st", "g": "sg"}
+    cnt = {"sv": 0, "ss": 0, "st": 0, "sg": 0}
+    seen = {q: {} for q in eng}
+    vec, act, pe = g.vector, g.scalar, g.tensor
+
+    def wait(q, toks):
+        need = {}
+        for s, n in toks:
+            need[s] = max(need.get(s, 0), n)
+        for s in need:
+            if seen[q].get(s, 0) < need[s]:
+                eng[q].wait_ge(T.sem[s], need[s])
+                seen[q][s] = need[s]
+
+    def run(q, fn, toks=()):
+        wait(q, toks)
+        ins = fn()
+        s = semof[q]
+        ins.then_inc(T.sem[s], 1)
+        cnt[s] += 1
+        return (s, cnt[s])
+
+    def dma(q, out, in_, name, toks=()):
+        wait(q, toks)
+        eng[q].dma_start(out, in_).then_inc(T.sem["d_" + name], 16)
+        return ("d_" + name, 16)
+
+    def ts(out, in0, s1, s2, op0, op1=None, toks=()):
+        if op1 is None:
+            return run("v", lambda: vec.tensor_scalar(out, in0, s1, None, op0), toks)
+        return run("v", lambda: vec.tensor_scalar(out, in0, s1, s2, op0, op1), toks)
+
+    def tt(out, a, b, op, toks=()):
+        return run("v", lambda: vec.tensor_tensor(out, a, b, op), toks)
+
+    def cp(out, in_, toks=()):
+        return run("v", lambda: vec.tensor_copy(out, in_), toks)
+
+    def tr(out, in_, toks=()):
+        return run("v", lambda: vec.transpose(out, in_), toks)
+
+    def ms(ap, c, toks=()):
+        return run("v", lambda: vec.memset(ap, c), toks)
+
+    def mm(out, l, r, start, stop, toks=()):
+        return run("t", lambda: pe.matmul(out, l, r, start, stop), toks)
+
+    def copy_s(out, in_, toks=()):
+        return run("s", lambda: act.activation(out, in_, ACT.Copy), toks)
+
+    def iota(out, pattern, base, cm, toks=(), flag=True):
+        if flag:
+            return run("g", lambda: g.iota(out, pattern, base, cm, allow_small_or_imprecise_dtypes=True), toks)
+        return run("g", lambda: g.iota(out, pattern, base, cm), toks)
+
+    final = []
+
+    def fused(pairs, sem, local):
+        free, tl, tot = list(range(16)), [], 0
+        for d, src, dst in sorted(pairs, key=lambda x: len(topo.engines(core, T.cores[x[0]]))):
+            es = [e for e in topo.engines(core, T.cores[d]) if e in free][:NE]
+            free = [e for e in free if e not in es]
+            rid, pid = topo.addr(T.cores[d], core)
+            tl.append(RemoteDMATransfer(dst_ids=[DstId(rid=rid, pnc=pid)], dma_engine_mask=sum(1 << e for e in es),
+                                        remote_sem=T.sem[sem], srcs=[src], dsts=[dst]))
+            tot += len(es)
+        g.remote_dma_fused(tl, local_sem=T.sem[local])
+        final.append((local, tot))
+
+    def send(d, src, dst, sem, local, part):
+        es = topo.engines(core, T.cores[d])[NE * part:NE * part + NE]
+        rid, pid = topo.addr(T.cores[d], core)
+        g.remote_dma(dst, src, T.sem[sem], T.sem[local], pid, rid, sum(1 << e for e in es))
+        final.append((local, NE))
+
+    others = [(me + k) % n_ranks for k in range(1, n_ranks)]
+
+    d_rk = dma("y", T.RK[:], T.rk[:], "rk")
+    d_rt = dma("s", T.RT[:], T.rt[:], "rt")
+    d_hd = dma("y", T.HC[:], T.hd[:], "hd")
+    d_vp = dma("s", T.VC[:], T.vp[:], "vp")
+    d_ap = dma("y", T.AC[:], T.ap[:], "ap")
+    d_vt = dma("y", T.VTC[:], T.vt[:], "vt")
+    d_at = dma("y", T.ATC[:], T.at[:], "at")
+
+    c_zi = iota(T.ZI[:], [[1, 128]], 0, -1)
+    c_i = iota(T.I256[:], [[1, 256]], 0, 0)
+    c_off = iota(T.OFF[:], [[0, 2], [128, 4]], 0, 0)
+    c_mod = iota(T.MOD16[:], [[0, 8], [1, 16]], 0, 0)
+    c_x = iota(T.X[:], [[-16, 8], [0, 16]], 0, 1, flag=False)
+    c_y = iota(T.Y[:], [[0, 12], [1, 16]], 0, -1, flag=False)
+    c_pc = iota(T.PC[:], [[0, 1]], 0, 1, flag=False)
+    c_pat = iota(T.PAT[:], [[1, 4], [-1, 2]], 0, 0, flag=False)
+    fill = [iota(T.W32[:, 0:1024], [[0, 1024]], 0, 0)]
+
+    z = ms(T.Z[:], 0.0)
+    wh = ms(T.WH[:], 0.0)
+    wpf = [copy_s(T.WP[:, a:a + 1024], T.Z[:], [z]) for a in range(0, V, 1024)]
+    fill += [copy_s(T.W32[:, a:a + 1024], T.Z[:], [z]) for a in (3072, 4096)]
+
+    us = ts(T.US[:], T.ZI[:], 0.0, None, OP.is_gt, toks=[c_zi])
+    ui = ts(T.UI[:], T.ZI[:], 0.0, None, OP.is_ge)
+    ib = ts(T.IB[:], T.ZI[:], 0.0, None, OP.is_equal)
+    owni = ts(T.OWNI[:], T.RK[:], 12, None, OP.arith_shift_right, toks=[d_rk])
+    k1 = ts(T.KI[:, 0:2], T.RK[:], 4032, None, OP.bitwise_and)
+    k2 = ts(T.KI[:, 2:4], T.RK[:], 63, None, OP.bitwise_and)
+    ownf = cp(T.OWNF[:], T.OWNI[:], [owni])
+    kf = cp(T.KF[:], T.KI[:], [k2])
+    o0 = ts(T.O[:, 0:4], T.I256[:, 0:4], T.OWNF[:, 0:1], None, OP.is_equal, toks=[ownf, c_i])
+    o1 = ts(T.O[:, 4:8], T.I256[:, 0:4], T.OWNF[:, 1:2], None, OP.is_equal)
+    p = T.P0[:, 0:4]
+    mm(p, T.IB[:], T.OFF[:, 0:4], True, False, [ib, c_off])
+    mm(p, T.US[:], T.O[:, 0:4], False, False, [o0])
+    mm(p, T.US[:], T.O[:, 4:8], False, True, [o1])
+    p = T.P0[:, 4:8]
+    mm(p, T.IB[:], T.OFF[:, 4:8], True, False)
+    mm(p, T.UI[:], T.O[:, 0:4], False, False)
+    pos = mm(p, T.US[:], T.O[:, 4:8], False, True)
+    hh = cp(T.HHI[:], T.HC[:], [d_hd])
+    hl = tt(T.HLO[:], T.HC[:], T.HHI[:], OP.subtract, [hh])
+    pr = tt(T.PR[:], T.P0[:, 0:8], T.O[:], OP.mult, [pos, o1])
+    run("v", lambda: vec.tensor_reduce(T.WI[:, 0:1], T.PR[:, 0:4], X, OP.max), [pr])
+    wi = run("v", lambda: vec.tensor_reduce(T.WI[:, 1:2], T.PR[:, 4:8], X, OP.max))
+    ts(T.AB[:, 0:2], T.WI[:], 15, None, OP.bitwise_and, toks=[wi])
+    ab = ts(T.AB[:, 2:4], T.WI[:], 4, None, OP.arith_shift_right)
+    abf = cp(T.ABF[:], T.AB[:], [ab])
+    lt = []
+    for h in range(2):
+        ts(T.LH[:, 128 * h:128 * h + 128], T.MOD16[:], T.ABF[:, h:h + 1], None, OP.is_equal, toks=[abf, c_mod, kf])
+        for e in range(2):
+            k = 64 * h + 32 * e
+            lt.append(ts(T.RH[:, k:k + 32], T.I256[:, 0:32], T.ABF[:, 2 + h:3 + h], T.KF[:, 2 * e + h:2 * e + h + 1],
+                         OP.is_equal, OP.mult))
+    for i in range(4):
+        h = i // 2
+        lst = mm(T.P7[:, 0:32], T.LH[:, 128 * h:128 * h + 128], T.RH[:, 32 * i:32 * i + 32], i == 0, i == 3, [lt[i]])
+    y15 = ts(T.Y15[:], T.Y[:], 15, None, OP.bitwise_and, toks=[c_y])
+    xh = ts(T.XH[:], T.X[:], 1, None, OP.arith_shift_right, toks=[c_x])
+    lu = cp(T.LSTU[:], T.P7[:, 0:32], [lst])
+    wait("g", [lu])
+    fused([(d, T.LSTU[:, 8 * d:8 * d + 6], T["LI%d" % me][:]) for d in others], "rL%d" % me, "xL")
+    fill.append(iota(T.W32[:, 1024:2048], [[0, 1024]], 0, 0))
+
+    d_hh = dma("y", T.WH[4:128:16, :], T.HHI[:], "hh", [hl, wh])
+    d_hl = dma("y", T.WH[5:128:16, :], T.HLO[:], "hl")
+    vh = cp(T.VHI[:], T.VC[:], [d_vp])
+    vl = tt(T.VLO[:], T.VC[:], T.VHI[:], OP.subtract, [vh])
+    d_vh = dma("y", T.WP[0:128:16, 0:V], T.VHI[:], "vh", [vl] + wpf)
+    d_vl = dma("y", T.WP[1:128:16, 0:V], T.VLO[:], "vl")
+    ah = cp(T.AHI[:], T.AC[:], [d_ap])
+    al = tt(T.ALO[:], T.AC[:], T.AHI[:], OP.subtract, [ah])
+    d_ah = dma("y", T.WP[2:128:16, 0:V], T.AHI[:], "ah", [al])
+    d_al = dma("y", T.WP[3:128:16, 0:V], T.ALO[:], "al")
+
+    ts(T.SI[:], T.WI[:], 127, None, OP.bitwise_and)
+    tf = cp(T.TF[:], T.RT[:], [d_rt])
+    pati = ts(T.PATI[:], T.PAT[:], 3, None, OP.bitwise_and, toks=[c_pat])
+    sf = cp(T.SF[:], T.SI[:], [tf])
+    tl = []
+    for h in range(2):
+        ts(T.SH[:, 128 * h:128 * h + 128], T.I256[:, 0:128], T.SF[:, h:h + 1], None, OP.is_equal, toks=[sf, pati])
+        tl.append(ts(T.RTT[:, 8 * h:8 * h + 8], T.PATI[:], T.OWNF[:, h:h + 1], T.TF[:, h:h + 1], OP.is_equal, OP.mult))
+    mm(T.P0[:, 16:24], T.SH[:, 0:128], T.RTT[:, 0:8], True, False, [tl[0], pr])
+    tm = mm(T.P0[:, 16:24], T.SH[:, 128:256], T.RTT[:, 8:16], False, True, [tl[1]])
+    pint = ts(T.PINT[:, 0:1], T.PC[:], 15, None, OP.bitwise_and, toks=[c_pc])
+    ev = ts(T.PINT[:, 1:2], T.PC[:], 1, None, OP.bitwise_and)
+    c1 = ts(T.C1[:], T.Y15[:], 1.0, 0.96875, OP.min, OP.subtract, toks=[y15])
+    xhd = ts(T.S[:, 0:128], T.XH[:], 2.0, None, OP.is_equal, toks=[xh])
+    ts_tok = cp(T.TS[:], T.P0[:, 16:24], [tm])
+    wait("g", [ts_tok])
+    fused([(d, T.TS[:, 2 * d:2 * d + 2], T["TC%d" % me][:]) for d in others], "rT%d" % me, "xT")
+    fill.append(iota(T.W32[:, 2048:3072], [[0, 1024]], 0, 0))
+    cc = ts(T.C[:], T.C1[:], 524288.0, None, OP.mult, toks=[c1])
+    col = ts(T.COL[:, 0:1], T.PINT[:, 0:1], -16384.0, 245760.0, OP.mult, OP.add, toks=[pint])
+    e1 = ts(T.EV1[:, 0:1], T.PINT[:, 1:2], 0.0, 6144.0, OP.is_equal, OP.mult, toks=[ev])
+    e2 = ts(T.EV1[:, 1:2], T.PINT[:, 1:2], 0.0, 1048576.0, OP.is_equal, OP.mult)
+    cp1 = ts(T.COLP1[:, 0:1], T.COL[:, 0:1], 6144.0, None, OP.add, toks=[col])
+    cp2 = ts(T.COLP1[:, 1:2], T.COL[:, 0:1], 12288.0, None, OP.add)
+    w1 = ts(T.WP[:, V:W], T.Z[:, 0:8], T.EV1[:, 0:1], None, OP.add, toks=[e1])
+    w2 = ts(T.W32[:, V:W], T.Z[:, 0:8], T.EV1[:, 1:2], None, OP.add, toks=[e2])
+    xvp = ts(T.S[:, 128:256], T.XH[:], 0.0, None, OP.is_equal)
+
+    WHT = [wh, d_hh, d_hl]
+    WPT = wpf + [w1, d_vh, d_vl, d_ah, d_al]
+    banks = [T.P2[:, 0:192], T.P3[:, 0:192]]
+    codes = [T.P4[:, 0:192], T.P5[:, 0:192]]
+
+    def S(name):
+        return T.S[:, 128 * SEL[name]:128 * SEL[name] + 128]
+
+    def G(i, half):
+        return T.G[:, 384 * i + 192 * half:384 * i + 192 * half + 192]
+
+    def Ls(i, half):
+        return T.L[:, 24 * i + 12 * half:24 * i + 12 * half + 12]
+
+    def scan(i, half, src, tok):
+        o = 384 * i + 192 * half
+        t = run("v", lambda: vec.tensor_tensor_scan(T.SC[:, o:o + 192], T.C[:], src, 0.0, OP.add, OP.max), [tok, cc])
+        return t, T.SC[:, o + 15:o + 192:16]
+
+    hg = []
+    for r in [me] + others:
+        src = T.LSTU[:, 8 * me:8 * me + 6] if r == me else T["LI%d" % r][:]
+        tok = lu if r == me else ("rL%d" % r, NE)
+        hg.append(copy_s(T.G[:, 96 * r:96 * r + 96], T.WH[:, 0:KEYS].indirect(src), WHT + [tok]))
+    fill.append(copy_s(T.W32[:, 5120:6144], T.Z[:], [z]))
+    m = [mm(banks[h], S("SHD"), G(0, h), True, True, [xhd, hg[-1]]) for h in range(2)]
+    l0, e0 = [], []
+    hs = []
+    for h in range(2):
+        t, pk = scan(0, h, banks[h], m[h])
+        l0.append(ts(Ls(0, h), pk, T.COL[:, 0:1], 6144.0, OP.subtract, OP.min, toks=[t, col]))
+        hs.append((t, pk))
+    ga = copy_s(G(1, 0), T.WP[:, 0:W].indirect(Ls(0, 0)), WPT + [l0[0]])
+    gb = cp(G(1, 1), T.WP[:, 0:W].indirect(Ls(0, 1)), WPT + [l0[1]])
+    for h in range(2):
+        a = ts(T.N[:, 12 * h:12 * h + 12], hs[h][1], T.COL[:, 0:1], 6144.0, OP.subtract, OP.max)
+        e0.append(ts(T.E0[:, 12 * h:12 * h + 12], T.N[:, 12 * h:12 * h + 12], T.COLP1[:, 0:1], None, OP.subtract, toks=[a, cp2]))
+    m = [mm(banks[0], S("SVP"), G(1, 0), True, True, [xvp, ga, hs[0][0]]), mm(banks[1], S("SVP"), G(1, 1), True, True, [gb, hs[1][0]])]
+    def tcol(r, e):
+        return (T.TS[:, 2 * me + e:2 * me + e + 1], ts_tok) if r == me else (T["TC%d" % r][:, e:e + 1], ("rT%d" % r, NE))
+    l1, e1t, sct = [], [], []
+    for h in range(2):
+        t, pk = scan(1, h, banks[h], m[h])
+        n1 = T.N[:, 24 + 12 * h:36 + 12 * h]
+        a = tt(n1, pk, T.E0[:, 12 * h:12 * h + 12], OP.add, [t, e0[h]])
+        l1.append(ts(Ls(1, h), n1, 6144.0, None, OP.min, toks=[a]))
+        e1t.append(a)
+        sct.append(t)
+    ga = copy_s(G(2, 0), T.WP[:, 0:W].indirect(Ls(1, 0)), [l1[0]])
+    gb = cp(G(2, 1), T.WP[:, 0:W].indirect(Ls(1, 1)), [l1[1]])
+    e1v = [ts(T.E1[:, 12 * h:12 * h + 12], T.N[:, 24 + 12 * h:36 + 12 * h], 6144.0, T.COLP1[:, 1:2], OP.max, OP.subtract) for h in range(2)]
+    idf = ts(T.IF[:], T.ZI[:], 0.0, None, OP.is_equal)
+    m = [mm(banks[0], S("SVP"), G(2, 0), True, True, [ga, sct[0]]), mm(banks[1], S("SVP"), G(2, 1), True, True, [gb, sct[1]])]
+
+    def bcast(r, e):
+        c, tok = tcol(r, e)
+        return run("s", lambda: act.activation(T.TB[:, 512 * e + 128 * r:512 * e + 128 * r + 128], T.Z[:, 0:128], ACT.Identity, bias=c), [tok, z])
+
+    def tmm(r, e, tok):
+        b = T.P1 if e == 0 else T.P6
+        return mm(b[:, 96 * r:96 * r + 96], T.TB[:, 512 * e + 128 * r:512 * e + 128 * r + 128], T.IF[:, 0:96], True, True, [tok, idf])
+    bt = [bcast(r, 0) for r in range(4)]
+    th = [tmm(r, 0, bt[r]) for r in range(4)]
+    tht = copy_s(T.TH[:], T.P1[:, 0:384], [th[3]])
+    l2, sc2 = [], []
+    for h in range(2):
+        t, pk = scan(2, h, banks[h], m[h])
+        n2 = T.N[:, 48 + 12 * h:60 + 12 * h]
+        a = tt(n2, pk, T.E1[:, 12 * h:12 * h + 12], OP.add, [t, e1v[h]])
+        l2.append(cp(Ls(3, h), n2, [a]))
+        sc2.append(t)
+        wait("g", [l2[h]])
+        send(nxt, Ls(3, h), T.M0[:, 12 * h:12 * h + 12], "rMA" if h == 0 else "rMB", "xMA" if h == 0 else "xMB", h)
+    bt = [bcast(r, 1) for r in range(4)]
+
+    tv = cp(T.VTF[:], T.VTC[:], [d_vt])
+    ta_ = cp(T.ATF[:], T.ATC[:], [d_at])
+    d_vv = dma("y", T.W32[1:128:16, 0:V], T.vv[:], "vv", fill)
+    d_av = dma("y", T.W32[3:128:16, 0:V], T.av[:], "av")
+    d_vtr = dma("y", T.W32[0:128:16, 0:V], T.VTF[:], "vtr", [tv])
+    d_atr = dma("y", T.W32[2:128:16, 0:V], T.ATF[:], "atr", [ta_])
+    W32T = fill + [w2, d_vv, d_av, d_vtr, d_atr]
+    for name, src, v, wgt in (("SAP", T.XH, 1.0, None), ("H2", T.X, 0.0, 2.0), ("H1", T.X, 0.0, None), ("A0", T.X, 2.0, 16.0),
+                              ("A1", T.X, 2.0, 8.0), ("A2", T.X, 2.0, 4.0), ("A3", T.X, 2.0, 2.0), ("A4", T.X, 2.0, None)):
+        if wgt is None:
+            smat = ts(S(name), src[:], v, None, OP.is_equal)
+        else:
+            smat = ts(S(name), src[:], v, wgt, OP.is_equal, OP.mult)
+    n0f = cp(T.HN[:, 0:24], T.L[:, 0:24], [l0[1]])
+    n1f = cp(T.HN[:, 24:48], T.L[:, 24:48], [l1[1]])
+    hc = ms(T.HN[:, 48:72], 6144.0)
+    mf5 = ms(T.MF[:, 120:144], 6144.0)
+    hd_ = tt(T.HD[:], T.HN[:, 0:48], T.HN[:, 24:72], OP.subtract, [hc])
+    pkh0 = ms(T.PKH[:, 24:32], 0.0)
+    pka0 = ms(T.PKA[:, 24:32], 0.0)
+
+    def test(i, h, lst, times, toks):
+        o = 384 * i + 192 * h
+        return run("v", lambda: vec.tensor_tensor(T.HIT[:, o:o + 192], T.W32[:, 0:W].indirect(lst), times[:, 192 * h:192 * h + 192], OP.is_le), toks)
+
+    def hitc(i, h):
+        return T.HIT[:, 384 * i + 192 * h:384 * i + 192 * h + 192]
+
+    h0 = [test(0, h, Ls(0, h), T.TH, W32T + [tht]) for h in range(2)]
+    h1 = [test(1, h, Ls(1, h), T.TH, []) for h in range(2)]
+    for h in range(2):
+        mm(codes[h], S("H2"), hitc(0, h), True, False, [h0[h], smat])
+    tam = [tmm(r, 1, bt[r]) for r in range(2)]
+    hcode = [mm(codes[h], S("H1"), hitc(1, h), False, True, [h1[h]]) for h in range(2)]
+    tam += [tmm(r, 1, bt[r]) for r in range(2, 4)]
+    tat = copy_s(T.TA[:], T.P6[:, 0:384], [tam[3]])
+    hsc = []
+    for h in range(2):
+        t, pk = scan(3, h, codes[h], hcode[h])
+        hcl = ts(T.HCL[:, 12 * h:12 * h + 12], pk, T.COL[:, 0:1], None, OP.subtract, toks=[t])
+        hsc.append(t)
+    ts(T.HI[:, 0:24], T.HCL[:], 2.0, None, OP.is_ge, toks=[hcl])
+    hi = ts(T.HI[:, 24:48], T.HCL[:], 1.0, None, OP.is_ge)
+    als = ts(T.ALS[:], T.HCL[:], 0.0, None, OP.is_equal)
+    wait("g", [als])
+    send(nxt, T.ALS[:], T.ALV[:], "rAL", "xAL", 0)
+    hp = tt(T.HP[:], T.HI[:], T.HD[:], OP.mult, [hi, hd_])
+    hx = tt(T.HX[:], T.HP[:, 0:24], T.HP[:, 24:48], OP.add, [hp])
+    hsel = ts(T.L[:, 48:72], T.HX[:], 6144.0, None, OP.add, toks=[hx])
+
+    def values(buf, tbuf, pick, row, lst, sel):
+        a = copy_s(buf[:, 0:192], T.W32[:, 0:W].indirect(lst[:, 0:12]), W32T + [sel])
+        b = cp(buf[:, 192:384], T.W32[:, 0:W].indirect(lst[:, 12:24]), [sel])
+        t0 = tr(tbuf[:, 0:192], buf[:, 0:192], [a])
+        t1 = tr(tbuf[:, 192:384], buf[:, 192:384], [b])
+        return cp(pick[:, 0:24], tbuf[:, row::16], [t0, t1])
+    ph = values(T.HV, T.HT, T.PKH, 1, T.L[:, 48:72], hsel)
+    wait("g", [ph, pkh0])
+    fused([(d, T.PKH[:, 6 * d:6 * d + 8], T.LANDH[:, 8 * me:8 * me + 8]) for d in others], "rH%d" % me, "xH")
+    ownh = cp(T.LANDH[:, 8 * me:8 * me + 8], T.PKH[:, 6 * me:6 * me + 8], [ph])
+
+    lists = [[T.M0[:, 12 * h:12 * h + 12] for h in range(2)]]
+    toks = [[("rMA", NE), ("rMB", NE)]]
+    prev = sc2
+    for k in range(4):
+        gk = [copy_s(G(3 + k, h), T.WP[:, 0:W].indirect(lists[k][h]), [toks[k][h]]) for h in range(2)]
+        hk = [test(2 + k, h, lists[k][h], T.TA, [toks[k][h], tat]) for h in range(2)]
+        if k == 0:
+            cp(T.MF[:, 0:24], T.M0[:])
+        else:
+            cp(T.MF[:, 24 * k:24 * k + 24], T.L[:, 24 * (3 + k):24 * (4 + k)], [toks[k][1]])
+        m = [mm(banks[h], S("SAP"), G(3 + k, h), True, True, [gk[h], prev[h]]) for h in range(2)]
+        for h in range(2):
+            mm(codes[h], S("A%d" % k), hitc(2 + k, h), k == 0, False, [hk[h], hsc[h]])
+        nl, prev = [], []
+        for h in range(2):
+            t, pk = scan(4 + k, h, banks[h], m[h])
+            nl.append(ts(Ls(4 + k, h), pk, T.COL[:, 0:1], None, OP.subtract, toks=[t]))
+            prev.append(t)
+        lists.append([Ls(4 + k, h) for h in range(2)])
+        toks.append(nl)
+    hk = [test(6, h, lists[4][h], T.TA, [toks[4][h]]) for h in range(2)]
+    mf = cp(T.MF[:, 96:120], T.L[:, 24 * 7:24 * 8])
+    acode = [mm(codes[h], S("A4"), hitc(6, h), False, True, [hk[h]]) for h in range(2)]
+    ad = tt(T.AD[:], T.MF[:, 0:120], T.MF[:, 24:144], OP.subtract, [mf, mf5])
+    for h in range(2):
+        t, pk = scan(8, h, codes[h], acode[h])
+        acl = ts(T.ACL[:, 12 * h:12 * h + 12], pk, T.COL[:, 0:1], None, OP.subtract, toks=[t])
+    for k in range(5):
+        ai = ts(T.AI[:, 24 * k:24 * k + 24], T.ACL[:], float(2 ** (4 - k)), None, OP.is_ge, toks=[acl])
+    a = tt(T.AP[:], T.AI[:], T.AD[:], OP.mult, [ai, ad])
+    a = tt(T.AX[:], T.AP[:, 0:48], T.AP[:, 48:96], OP.add, [a])
+    a = tt(T.AY[:], T.AX[:, 0:24], T.AX[:, 24:48], OP.add, [a])
+    a = tt(T.AZ[:], T.AY[:], T.AP[:, 96:120], OP.add, [a])
+    a = tt(T.AW[:], T.AZ[:], T.ALV[:], OP.mult, [a, ("rAL", NE)])
+    asel = ts(T.L[:, 192:216], T.AW[:], 6144.0, None, OP.add, toks=[a])
+    pa = values(T.AV, T.AT, T.PKA, 3, T.L[:, 192:216], asel)
+    wait("g", [pa, pka0])
+    fused([(d, T.PKA[:, 6 * d:6 * d + 8], T.LANDA[:, 8 * prv:8 * prv + 8]) for d in others], "rA%d" % prv, "xA")
+    owna = cp(T.LANDA[:, 8 * prv:8 * prv + 8], T.PKA[:, 6 * me:6 * me + 8], [pa])
+
+    ts(T.FI[:, 0:2], T.WI[:], 31, None, OP.bitwise_and)
+    fi = ts(T.FI[:, 2:4], T.WI[:], 5, None, OP.arith_shift_right)
+    ts(T.PINT[:, 2:3], T.PC[:], 7, None, OP.bitwise_and)
+    ts(T.PINT[:, 3:4], T.PC[:], 3, None, OP.arith_shift_right)
+    pi = ts(T.PINT[:, 4:5], T.PC[:], 31, 1, OP.bitwise_and, OP.arith_shift_right)
+    ff = cp(T.FF[:], T.FI[:], [fi])
+    pf = cp(T.PF[:, 0:3], T.PINT[:, 2:5], [pi])
+    ts(T.PF[:, 3:4], T.PF[:, 0:1], 2.0, None, OP.mult, toks=[pf])
+    ts(T.PF[:, 4:5], T.PF[:, 0:1], 2.0, 1.0, OP.mult, OP.add)
+    a = ts(T.PF[:, 5:6], T.PF[:, 0:1], 32.0, T.PF[:, 1:2], OP.mult, OP.add)
+    a = ts(T.PF[:, 6:7], T.PF[:, 5:6], 16.0, None, OP.add, toks=[a, ff])
+    ts(T.C8[:], T.MOD16[:], T.PF[:, 1:2], None, OP.is_equal, toks=[a])
+    for h in range(2):
+        fr = ts(T.FR[:, 16 * h:16 * h + 16], T.I256[:, 0:16], T.PF[:, 3 + h:4 + h], T.FF[:, h:h + 1], OP.is_equal, OP.mult)
+    for h in range(2):
+        fl = mm(T.P7[:, 64:80], T.C8[:], T.FR[:, 16 * h:16 * h + 16], h == 0, h == 1, [fr])
+    for h in range(2):
+        ts(T.QB[:, 128 * h:128 * h + 128], T.I256[:, 0:128], 0.0, T.FF[:, 2 + h:3 + h], OP.mult, OP.add)
+        js = ts(T.JS[:, 256 * h:256 * h + 256], T.I256[:], T.PF[:, 5 + h:6 + h], None, OP.is_equal)
+    for h in range(2):
+        mk = mm(T.P0[:, 256:512], T.QB[:, 128 * h:128 * h + 128], T.JS[:, 256 * h:256 * h + 256], h == 0, h == 1, [js])
+    r0 = ts(T.R0[:], T.MOD16[:], 0.0, None, OP.not_equal)
+    flu = cp(T.FL[:], T.P7[:, 64:80], [fl])
+    mask = ts(T.MASK[:], T.P0[:, 256:512], T.PF[:, 2:3], None, OP.is_equal, toks=[mk])
+
+    arr = [("rH%d" % q, NE) for q in range(n_ranks) if q != me] + [("rA%d" % q, NE) for q in range(n_ranks) if (q + 1) % n_ranks != me]
+    ls = tt(T.LS[:], T.LANDH[:], T.LANDA[:], OP.add, arr + [ownh, owna])
+    wn = tr(T.WIN[:], T.LS[:], [ls])
+    gm = run("v", lambda: vec.tensor_tensor(T.GM[:], T.WIN[:, 0:32].indirect(T.FL[:]), T.MASK[:], OP.mult), [wn, flu, mask])
+    ot0 = ms(T.OT[:], 0.0)
+    t2 = tr(T.TR[:], T.GM[:], [gm])
+    for h in range(2):
+        sc = run("v", lambda: vec.tensor_tensor_scan(T.SCF[:, 128 * h:128 * h + 128], T.R0[:], T.TR[:, h::2], 0.0, OP.mult, OP.add), [t2, r0])
+    o = cp(T.OT[:, 0:16], T.SCF[:, 15::16], [sc, ot0])
+    yt = tr(T.YT[:], T.OT[:], [o])
+    for a in range(4):
+        final.append(dma("y" if a % 2 == 0 else "s", T.y[2 * a:2 * a + 2, :], T.YT[32 * a:32 * a + 16, :], "y%d" % a, [yt]))
+    wait("g", final + [(s, n) for s, n in cnt.items()])

@@ -21,7 +21,7 @@ def _bufs():
     sb("I256", 256, _b); sb("ZI", 128, _b); sb("MOD16", 128, _b); sb("OFF", 8, _b); sb("PC", 1, _i); sb("PAT", 8, _i)
     sb("PATI", 8, _i); sb("X", 128, _i); sb("XH", 128, _i); sb("Y", 192, _i); sb("Y15", 192, _i); sb("C1", 192, _f); sb("C", 192, _f)
     sb("US", 128, _b); sb("UI", 128, _b); sb("IB", 128, _b); sb("IF", 128, _f); sb("S", 1280, _b)
-    sb("PINT", 8, _i); sb("COL", 4, _f); sb("COLP1", 4, _f); sb("EV1", 4, _f)
+    sb("PINT", 8, _i); sb("COL", 12, _f); sb("EV1", 4, _f)
     sb("RK", 2, _i); sb("RT", 2, _i); sb("OWNI", 2, _i); sb("OWNF", 2, _f); sb("KI", 4, _i); sb("KF", 4, _f); sb("TF", 2, _f)
     sb("O", 8, _b); sb("PR", 8, _f); sb("WI", 2, _i); sb("AB", 4, _i); sb("ABF", 4, _f); sb("LH", 256, _b); sb("RH", 128, _b)
     sb("LSTU", 32, _u); sb("SI", 2, _i); sb("SF", 2, _f); sb("SH", 256, _f); sb("RTT", 16, _f); sb("TS", 8, _f)
@@ -29,11 +29,11 @@ def _bufs():
         sb("LI%d" % r, 6, _u); sb("TC%d" % r, 2, _f)
     sb("G", 384 * 7, _b); sb("SC", 384 * 9, _f); sb("L", 24 * 9, _u); sb("N", 24 * 4, _f); sb("E0", 24, _f); sb("E1", 24, _f)
     sb("M0", 24, _u); sb("ALV", 24, _f); sb("ALS", 24, _f)
-    sb("TB", 1024, _f); sb("TH", 384, _f); sb("TA", 384, _f); sb("HIT", 384 * 7, _b)
-    sb("HN", 72, _f); sb("HD", 48, _f); sb("HI", 48, _f); sb("HP", 48, _f); sb("HX", 24, _f); sb("HCL", 24, _f)
+    sb("TB", 512, _f); sb("TH", 384, _f); sb("HIT", 384 * 7, _b)
+    sb("HN", 72, _f); sb("HD", 48, _f); sb("HI", 48, _f); sb("HP", 48, _f); sb("HX", 24, _f)
     sb("HV", 384, _f); sb("HT", 384, _f); sb("PKH", 32, _f)
     sb("MF", 144, _f); sb("AD", 120, _f); sb("AI", 120, _f); sb("AP", 120, _f); sb("AX", 48, _f); sb("AY", 24, _f); sb("AZ", 24, _f)
-    sb("AW", 24, _f); sb("ACL", 24, _f); sb("AV", 384, _f); sb("AT", 384, _f); sb("PKA", 32, _f)
+    sb("AW", 24, _f); sb("AV", 384, _f); sb("AT", 384, _f); sb("PKA", 32, _f)
     sb("LANDH", 32, _f); sb("LANDA", 32, _f); sb("LS", 32, _f); sb("WIN", 32, _f)
     sb("FI", 4, _i); sb("FF", 4, _f); sb("FR", 32, _b); sb("C8", 128, _b); sb("FL", 16, _u); sb("QB", 256, _b); sb("JS", 512, _b)
     sb("PF", 8, _f); sb("MASK", 256, _f); sb("R0", 128, _f)
@@ -154,10 +154,14 @@ def rank_program(g, core, T, topo):
     c_pat = iota(T.PAT[:], [[1, 4], [-1, 2]], 0, 0, flag=False)
     fill = [iota(T.W32[:, 0:1024], [[0, 1024]], 0, 0)]
 
+    def zeros_s(a, b):
+        fill.append(copy_s(T.W32[:, a:b], T.Z[:, 0:b - a], [z]))
+
     z = ms(T.Z[:], 0.0)
-    wh = ms(T.WH[:], 0.0)
+    ms(T.WH[:, 0:3072], 0.0)
     wpf = [copy_s(T.WP[:, a:a + 1024], T.Z[:], [z]) for a in range(0, V, 1024)]
-    fill += [copy_s(T.W32[:, a:a + 1024], T.Z[:], [z]) for a in (3072, 4096)]
+    zeros_s(5120, 6144)
+    zeros_s(4352, 5120)
 
     us = ts(T.US[:], T.ZI[:], 0.0, None, OP.is_gt, toks=[c_zi])
     ui = ts(T.UI[:], T.ZI[:], 0.0, None, OP.is_ge)
@@ -178,7 +182,7 @@ def rank_program(g, core, T, topo):
     mm(p, T.UI[:], T.O[:, 0:4], False, False)
     pos = mm(p, T.US[:], T.O[:, 4:8], False, True)
     hh = cp(T.HHI[:], T.HC[:], [d_hd])
-    hl = tt(T.HLO[:], T.HC[:], T.HHI[:], OP.subtract, [hh])
+    wh = ms(T.WH[:, 3072:4096], 0.0)
     pr = tt(T.PR[:], T.P0[:, 0:8], T.O[:], OP.mult, [pos, o1])
     run("v", lambda: vec.tensor_reduce(T.WI[:, 0:1], T.PR[:, 0:4], X, OP.max), [pr])
     wi = run("v", lambda: vec.tensor_reduce(T.WI[:, 1:2], T.PR[:, 4:8], X, OP.max))
@@ -195,12 +199,11 @@ def rank_program(g, core, T, topo):
     for i in range(4):
         h = i // 2
         lst = mm(T.P7[:, 0:32], T.LH[:, 128 * h:128 * h + 128], T.RH[:, 32 * i:32 * i + 32], i == 0, i == 3, [lt[i]])
-    y15 = ts(T.Y15[:], T.Y[:], 15, None, OP.bitwise_and, toks=[c_y])
-    xh = ts(T.XH[:], T.X[:], 1, None, OP.arith_shift_right, toks=[c_x])
+    hl = tt(T.HLO[:], T.HC[:], T.HHI[:], OP.subtract, [hh])
     lu = cp(T.LSTU[:], T.P7[:, 0:32], [lst])
     wait("g", [lu])
     fused([(d, T.LSTU[:, 8 * d:8 * d + 6], T["LI%d" % me][:]) for d in others], "rL%d" % me, "xL")
-    fill.append(iota(T.W32[:, 1024:2048], [[0, 1024]], 0, 0))
+    fill.append(iota(T.W32[:, 1024:2304], [[0, 1280]], 0, 0))
 
     d_hh = dma("y", T.WH[4:128:16, :], T.HHI[:], "hh", [hl, wh])
     d_hl = dma("y", T.WH[5:128:16, :], T.HLO[:], "hl")
@@ -223,6 +226,8 @@ def rank_program(g, core, T, topo):
         tl.append(ts(T.RTT[:, 8 * h:8 * h + 8], T.PATI[:], T.OWNF[:, h:h + 1], T.TF[:, h:h + 1], OP.is_equal, OP.mult))
     mm(T.P0[:, 16:24], T.SH[:, 0:128], T.RTT[:, 0:8], True, False, [tl[0], pr])
     tm = mm(T.P0[:, 16:24], T.SH[:, 128:256], T.RTT[:, 8:16], False, True, [tl[1]])
+    y15 = ts(T.Y15[:], T.Y[:], 15, None, OP.bitwise_and, toks=[c_y])
+    xh = ts(T.XH[:], T.X[:], 1, None, OP.arith_shift_right, toks=[c_x])
     pint = ts(T.PINT[:, 0:1], T.PC[:], 15, None, OP.bitwise_and, toks=[c_pc])
     ev = ts(T.PINT[:, 1:2], T.PC[:], 1, None, OP.bitwise_and)
     c1 = ts(T.C1[:], T.Y15[:], 1.0, 0.96875, OP.min, OP.subtract, toks=[y15])
@@ -230,15 +235,11 @@ def rank_program(g, core, T, topo):
     ts_tok = cp(T.TS[:], T.P0[:, 16:24], [tm])
     wait("g", [ts_tok])
     fused([(d, T.TS[:, 2 * d:2 * d + 2], T["TC%d" % me][:]) for d in others], "rT%d" % me, "xT")
-    fill.append(iota(T.W32[:, 2048:3072], [[0, 1024]], 0, 0))
+    fill.append(iota(T.W32[:, 2304:2816], [[0, 512]], 0, 0))
     cc = ts(T.C[:], T.C1[:], 524288.0, None, OP.mult, toks=[c1])
     col = ts(T.COL[:, 0:1], T.PINT[:, 0:1], -16384.0, 245760.0, OP.mult, OP.add, toks=[pint])
     e1 = ts(T.EV1[:, 0:1], T.PINT[:, 1:2], 0.0, 6144.0, OP.is_equal, OP.mult, toks=[ev])
-    e2 = ts(T.EV1[:, 1:2], T.PINT[:, 1:2], 0.0, 1048576.0, OP.is_equal, OP.mult)
-    cp1 = ts(T.COLP1[:, 0:1], T.COL[:, 0:1], 6144.0, None, OP.add, toks=[col])
-    cp2 = ts(T.COLP1[:, 1:2], T.COL[:, 0:1], 12288.0, None, OP.add)
     w1 = ts(T.WP[:, V:W], T.Z[:, 0:8], T.EV1[:, 0:1], None, OP.add, toks=[e1])
-    w2 = ts(T.W32[:, V:W], T.Z[:, 0:8], T.EV1[:, 1:2], None, OP.add, toks=[e2])
     xvp = ts(T.S[:, 128:256], T.XH[:], 0.0, None, OP.is_equal)
 
     WHT = [wh, d_hh, d_hl]
@@ -260,12 +261,22 @@ def rank_program(g, core, T, topo):
         t = run("v", lambda: vec.tensor_tensor_scan(T.SC[:, o:o + 192], T.C[:], src, 0.0, OP.add, OP.max), [tok, cc])
         return t, T.SC[:, o + 15:o + 192:16]
 
+    smat = {}
+
+    def weights(*names):
+        for name, src, v, wgt in names:
+            if wgt is None:
+                smat[name] = ts(S(name), src[:], v, None, OP.is_equal)
+            else:
+                smat[name] = ts(S(name), src[:], v, wgt, OP.is_equal, OP.mult)
+
     hg = []
     for r in [me] + others:
         src = T.LSTU[:, 8 * me:8 * me + 6] if r == me else T["LI%d" % r][:]
         tok = lu if r == me else ("rL%d" % r, NE)
         hg.append(copy_s(T.G[:, 96 * r:96 * r + 96], T.WH[:, 0:KEYS].indirect(src), WHT + [tok]))
-    fill.append(copy_s(T.W32[:, 5120:6144], T.Z[:], [z]))
+    zeros_s(3328, 4352)
+    fill.append(ms(T.W32[:, 2816:3328], 0.0))
     m = [mm(banks[h], S("SHD"), G(0, h), True, True, [xhd, hg[-1]]) for h in range(2)]
     l0, e0 = [], []
     hs = []
@@ -275,35 +286,36 @@ def rank_program(g, core, T, topo):
         hs.append((t, pk))
     ga = copy_s(G(1, 0), T.WP[:, 0:W].indirect(Ls(0, 0)), WPT + [l0[0]])
     gb = cp(G(1, 1), T.WP[:, 0:W].indirect(Ls(0, 1)), WPT + [l0[1]])
+    ts(T.COL[:, 1:2], T.COL[:, 0:1], 6144.0, None, OP.add)
+    cp2 = ts(T.COL[:, 2:3], T.COL[:, 0:1], 12288.0, None, OP.add)
     for h in range(2):
         a = ts(T.N[:, 12 * h:12 * h + 12], hs[h][1], T.COL[:, 0:1], 6144.0, OP.subtract, OP.max)
-        e0.append(ts(T.E0[:, 12 * h:12 * h + 12], T.N[:, 12 * h:12 * h + 12], T.COLP1[:, 0:1], None, OP.subtract, toks=[a, cp2]))
+        e0.append(ts(T.E0[:, 12 * h:12 * h + 12], T.N[:, 12 * h:12 * h + 12], T.COL[:, 1:2], None, OP.subtract, toks=[a, cp2]))
     m = [mm(banks[0], S("SVP"), G(1, 0), True, True, [xvp, ga, hs[0][0]]), mm(banks[1], S("SVP"), G(1, 1), True, True, [gb, hs[1][0]])]
-    def tcol(r, e):
-        return (T.TS[:, 2 * me + e:2 * me + e + 1], ts_tok) if r == me else (T["TC%d" % r][:, e:e + 1], ("rT%d" % r, NE))
-    l1, e1t, sct = [], [], []
+    tv = cp(T.VTF[:], T.VTC[:], [d_vt])
+    ta_ = cp(T.ATF[:], T.ATC[:], [d_at])
+    l1, sct = [], []
     for h in range(2):
         t, pk = scan(1, h, banks[h], m[h])
         n1 = T.N[:, 24 + 12 * h:36 + 12 * h]
         a = tt(n1, pk, T.E0[:, 12 * h:12 * h + 12], OP.add, [t, e0[h]])
         l1.append(ts(Ls(1, h), n1, 6144.0, None, OP.min, toks=[a]))
-        e1t.append(a)
         sct.append(t)
     ga = copy_s(G(2, 0), T.WP[:, 0:W].indirect(Ls(1, 0)), [l1[0]])
     gb = cp(G(2, 1), T.WP[:, 0:W].indirect(Ls(1, 1)), [l1[1]])
-    e1v = [ts(T.E1[:, 12 * h:12 * h + 12], T.N[:, 24 + 12 * h:36 + 12 * h], 6144.0, T.COLP1[:, 1:2], OP.max, OP.subtract) for h in range(2)]
+    e1v = [ts(T.E1[:, 12 * h:12 * h + 12], T.N[:, 24 + 12 * h:36 + 12 * h], 6144.0, T.COL[:, 2:3], OP.max, OP.subtract) for h in range(2)]
     idf = ts(T.IF[:], T.ZI[:], 0.0, None, OP.is_equal)
     m = [mm(banks[0], S("SVP"), G(2, 0), True, True, [ga, sct[0]]), mm(banks[1], S("SVP"), G(2, 1), True, True, [gb, sct[1]])]
 
-    def bcast(r, e):
-        c, tok = tcol(r, e)
-        return run("s", lambda: act.activation(T.TB[:, 512 * e + 128 * r:512 * e + 128 * r + 128], T.Z[:, 0:128], ACT.Identity, bias=c), [tok, z])
+    def bcast(r):
+        c, tok = (T.TS[:, 2 * me:2 * me + 2], ts_tok) if r == me else (T["TC%d" % r][:], ("rT%d" % r, NE))
+        x = run("s", lambda: act.activation(T.TB[:, 128 * r:128 * r + 128], T.Z[:, 0:128], ACT.Identity, bias=c[:, 0:1]), [tok, z])
+        return run("s", lambda: act.activation(T.TB[:, 128 * r + 2:128 * r + 128:16], T.Z[:, 0:8], ACT.Identity, bias=c[:, 1:2]), [x])
 
-    def tmm(r, e, tok):
-        b = T.P1 if e == 0 else T.P6
-        return mm(b[:, 96 * r:96 * r + 96], T.TB[:, 512 * e + 128 * r:512 * e + 128 * r + 128], T.IF[:, 0:96], True, True, [tok, idf])
-    bt = [bcast(r, 0) for r in range(4)]
-    th = [tmm(r, 0, bt[r]) for r in range(4)]
+    def tmm(r, tok):
+        return mm(T.P1[:, 96 * r:96 * r + 96], T.TB[:, 128 * r:128 * r + 128], T.IF[:, 0:96], True, True, [tok, idf])
+    bt = [bcast(r) for r in range(4)]
+    th = [tmm(r, bt[r]) for r in range(4)]
     tht = copy_s(T.TH[:], T.P1[:, 0:384], [th[3]])
     l2, sc2 = [], []
     for h in range(2):
@@ -314,21 +326,14 @@ def rank_program(g, core, T, topo):
         sc2.append(t)
         wait("g", [l2[h]])
         send(nxt, Ls(3, h), T.M0[:, 12 * h:12 * h + 12], "rMA" if h == 0 else "rMB", "xMA" if h == 0 else "xMB", h)
-    bt = [bcast(r, 1) for r in range(4)]
 
-    tv = cp(T.VTF[:], T.VTC[:], [d_vt])
-    ta_ = cp(T.ATF[:], T.ATC[:], [d_at])
     d_vv = dma("y", T.W32[1:128:16, 0:V], T.vv[:], "vv", fill)
     d_av = dma("y", T.W32[3:128:16, 0:V], T.av[:], "av")
     d_vtr = dma("y", T.W32[0:128:16, 0:V], T.VTF[:], "vtr", [tv])
     d_atr = dma("y", T.W32[2:128:16, 0:V], T.ATF[:], "atr", [ta_])
+    e2 = ts(T.EV1[:, 1:2], T.PINT[:, 1:2], 0.0, 1048576.0, OP.is_equal, OP.mult)
+    w2 = ts(T.W32[:, V:W], T.Z[:, 0:8], T.EV1[:, 1:2], None, OP.add, toks=[e2])
     W32T = fill + [w2, d_vv, d_av, d_vtr, d_atr]
-    for name, src, v, wgt in (("SAP", T.XH, 1.0, None), ("H2", T.X, 0.0, 2.0), ("H1", T.X, 0.0, None), ("A0", T.X, 2.0, 16.0),
-                              ("A1", T.X, 2.0, 8.0), ("A2", T.X, 2.0, 4.0), ("A3", T.X, 2.0, 2.0), ("A4", T.X, 2.0, None)):
-        if wgt is None:
-            smat = ts(S(name), src[:], v, None, OP.is_equal)
-        else:
-            smat = ts(S(name), src[:], v, wgt, OP.is_equal, OP.mult)
     n0f = cp(T.HN[:, 0:24], T.L[:, 0:24], [l0[1]])
     n1f = cp(T.HN[:, 24:48], T.L[:, 24:48], [l1[1]])
     hc = ms(T.HN[:, 48:72], 6144.0)
@@ -336,53 +341,47 @@ def rank_program(g, core, T, topo):
     hd_ = tt(T.HD[:], T.HN[:, 0:48], T.HN[:, 24:72], OP.subtract, [hc])
     pkh0 = ms(T.PKH[:, 24:32], 0.0)
     pka0 = ms(T.PKA[:, 24:32], 0.0)
+    for k in range(5):
+        colt = ts(T.COL[:, 4 + k:5 + k], T.COL[:, 0:1], float(2 ** k), None, OP.add)
+    weights(("H2", T.X, 0.0, 2.0), ("H1", T.X, 0.0, None), ("SAP", T.XH, 1.0, None), ("A0", T.X, 2.0, 16.0),
+            ("A1", T.X, 2.0, 8.0), ("A2", T.X, 2.0, 4.0), ("A3", T.X, 2.0, 2.0), ("A4", T.X, 2.0, None))
 
-    def test(i, h, lst, times, toks):
+    def test(i, h, lst, toks):
         o = 384 * i + 192 * h
-        return run("v", lambda: vec.tensor_tensor(T.HIT[:, o:o + 192], T.W32[:, 0:W].indirect(lst), times[:, 192 * h:192 * h + 192], OP.is_le), toks)
+        return run("v", lambda: vec.tensor_tensor(T.HIT[:, o:o + 192], T.W32[:, 0:W].indirect(lst), T.TH[:, 192 * h:192 * h + 192], OP.is_le), toks)
 
     def hitc(i, h):
         return T.HIT[:, 384 * i + 192 * h:384 * i + 192 * h + 192]
 
-    h0 = [test(0, h, Ls(0, h), T.TH, W32T + [tht]) for h in range(2)]
-    h1 = [test(1, h, Ls(1, h), T.TH, []) for h in range(2)]
+    h0 = [test(0, h, Ls(0, h), W32T + [tht]) for h in range(2)]
+    h1 = [test(1, h, Ls(1, h), []) for h in range(2)]
     for h in range(2):
-        mm(codes[h], S("H2"), hitc(0, h), True, False, [h0[h], smat])
-    tam = [tmm(r, 1, bt[r]) for r in range(2)]
+        mm(codes[h], S("H2"), hitc(0, h), True, False, [h0[h], smat["A4"]])
     hcode = [mm(codes[h], S("H1"), hitc(1, h), False, True, [h1[h]]) for h in range(2)]
-    tam += [tmm(r, 1, bt[r]) for r in range(2, 4)]
-    tat = copy_s(T.TA[:], T.P6[:, 0:384], [tam[3]])
-    hsc = []
-    for h in range(2):
-        t, pk = scan(3, h, codes[h], hcode[h])
-        hcl = ts(T.HCL[:, 12 * h:12 * h + 12], pk, T.COL[:, 0:1], None, OP.subtract, toks=[t])
-        hsc.append(t)
-    ts(T.HI[:, 0:24], T.HCL[:], 2.0, None, OP.is_ge, toks=[hcl])
-    hi = ts(T.HI[:, 24:48], T.HCL[:], 1.0, None, OP.is_ge)
-    als = ts(T.ALS[:], T.HCL[:], 0.0, None, OP.is_equal)
+    hsc = [scan(3, h, codes[h], hcode[h])[0] for h in range(2)]
+    hpk = T.SC[:, 384 * 3 + 15:384 * 4:16]
+    ts(T.HI[:, 0:24], hpk, T.COL[:, 5:6], None, OP.is_ge, toks=[hsc[1], colt])
+    hi = ts(T.HI[:, 24:48], hpk, T.COL[:, 4:5], None, OP.is_ge)
+    als = ts(T.ALS[:], hpk, T.COL[:, 0:1], None, OP.is_equal)
     wait("g", [als])
     send(nxt, T.ALS[:], T.ALV[:], "rAL", "xAL", 0)
     hp = tt(T.HP[:], T.HI[:], T.HD[:], OP.mult, [hi, hd_])
     hx = tt(T.HX[:], T.HP[:, 0:24], T.HP[:, 24:48], OP.add, [hp])
     hsel = ts(T.L[:, 48:72], T.HX[:], 6144.0, None, OP.add, toks=[hx])
 
-    def values(buf, tbuf, pick, row, lst, sel):
-        a = copy_s(buf[:, 0:192], T.W32[:, 0:W].indirect(lst[:, 0:12]), W32T + [sel])
-        b = cp(buf[:, 192:384], T.W32[:, 0:W].indirect(lst[:, 12:24]), [sel])
-        t0 = tr(tbuf[:, 0:192], buf[:, 0:192], [a])
-        t1 = tr(tbuf[:, 192:384], buf[:, 192:384], [b])
+    def compact(buf, tbuf, pick, row, ab):
+        t0 = tr(tbuf[:, 0:192], buf[:, 0:192], [ab[0]])
+        t1 = tr(tbuf[:, 192:384], buf[:, 192:384], [ab[1]])
         return cp(pick[:, 0:24], tbuf[:, row::16], [t0, t1])
-    ph = values(T.HV, T.HT, T.PKH, 1, T.L[:, 48:72], hsel)
-    wait("g", [ph, pkh0])
-    fused([(d, T.PKH[:, 6 * d:6 * d + 8], T.LANDH[:, 8 * me:8 * me + 8]) for d in others], "rH%d" % me, "xH")
-    ownh = cp(T.LANDH[:, 8 * me:8 * me + 8], T.PKH[:, 6 * me:6 * me + 8], [ph])
 
     lists = [[T.M0[:, 12 * h:12 * h + 12] for h in range(2)]]
     toks = [[("rMA", NE), ("rMB", NE)]]
     prev = sc2
     for k in range(4):
         gk = [copy_s(G(3 + k, h), T.WP[:, 0:W].indirect(lists[k][h]), [toks[k][h]]) for h in range(2)]
-        hk = [test(2 + k, h, lists[k][h], T.TA, [toks[k][h], tat]) for h in range(2)]
+        if k == 0:
+            hv = [copy_s(T.HV[:, 192 * h:192 * h + 192], T.W32[:, 0:W].indirect(Ls(2, h)), W32T + [hsel]) for h in range(2)]
+        hk = [test(2 + k, h, lists[k][h], [toks[k][h]]) for h in range(2)]
         if k == 0:
             cp(T.MF[:, 0:24], T.M0[:])
         else:
@@ -397,24 +396,29 @@ def rank_program(g, core, T, topo):
             prev.append(t)
         lists.append([Ls(4 + k, h) for h in range(2)])
         toks.append(nl)
-    hk = [test(6, h, lists[4][h], T.TA, [toks[4][h]]) for h in range(2)]
+    hk = [test(6, h, lists[4][h], [toks[4][h]]) for h in range(2)]
     mf = cp(T.MF[:, 96:120], T.L[:, 24 * 7:24 * 8])
     acode = [mm(codes[h], S("A4"), hitc(6, h), False, True, [hk[h]]) for h in range(2)]
     ad = tt(T.AD[:], T.MF[:, 0:120], T.MF[:, 24:144], OP.subtract, [mf, mf5])
-    for h in range(2):
-        t, pk = scan(8, h, codes[h], acode[h])
-        acl = ts(T.ACL[:, 12 * h:12 * h + 12], pk, T.COL[:, 0:1], None, OP.subtract, toks=[t])
+    ph = compact(T.HV, T.HT, T.PKH, 1, hv)
+    wait("g", [ph, pkh0])
+    fused([(d, T.PKH[:, 6 * d:6 * d + 8], T.LANDH[:, 8 * me:8 * me + 8]) for d in others], "rH%d" % me, "xH")
+    asc = [scan(8, h, codes[h], acode[h])[0] for h in range(2)]
+    apk = T.SC[:, 384 * 8 + 15:384 * 9:16]
     for k in range(5):
-        ai = ts(T.AI[:, 24 * k:24 * k + 24], T.ACL[:], float(2 ** (4 - k)), None, OP.is_ge, toks=[acl])
+        ai = ts(T.AI[:, 24 * k:24 * k + 24], apk, T.COL[:, 8 - k:9 - k], None, OP.is_ge, toks=[asc[1]])
     a = tt(T.AP[:], T.AI[:], T.AD[:], OP.mult, [ai, ad])
     a = tt(T.AX[:], T.AP[:, 0:48], T.AP[:, 48:96], OP.add, [a])
     a = tt(T.AY[:], T.AX[:, 0:24], T.AX[:, 24:48], OP.add, [a])
     a = tt(T.AZ[:], T.AY[:], T.AP[:, 96:120], OP.add, [a])
     a = tt(T.AW[:], T.AZ[:], T.ALV[:], OP.mult, [a, ("rAL", NE)])
     asel = ts(T.L[:, 192:216], T.AW[:], 6144.0, None, OP.add, toks=[a])
-    pa = values(T.AV, T.AT, T.PKA, 3, T.L[:, 192:216], asel)
+    va = copy_s(T.AV[:, 0:192], T.W32[:, 0:W].indirect(Ls(8, 0)), [asel])
+    vb = cp(T.AV[:, 192:384], T.W32[:, 0:W].indirect(Ls(8, 1)), [asel])
+    pa = compact(T.AV, T.AT, T.PKA, 3, [va, vb])
     wait("g", [pa, pka0])
     fused([(d, T.PKA[:, 6 * d:6 * d + 8], T.LANDA[:, 8 * prv:8 * prv + 8]) for d in others], "rA%d" % prv, "xA")
+    ownh = cp(T.LANDH[:, 8 * me:8 * me + 8], T.PKH[:, 6 * me:6 * me + 8], [ph])
     owna = cp(T.LANDA[:, 8 * prv:8 * prv + 8], T.PKA[:, 6 * me:6 * me + 8], [pa])
 
     ts(T.FI[:, 0:2], T.WI[:], 31, None, OP.bitwise_and)
@@ -441,12 +445,12 @@ def rank_program(g, core, T, topo):
     r0 = ts(T.R0[:], T.MOD16[:], 0.0, None, OP.not_equal)
     flu = cp(T.FL[:], T.P7[:, 64:80], [fl])
     mask = ts(T.MASK[:], T.P0[:, 256:512], T.PF[:, 2:3], None, OP.is_equal, toks=[mk])
+    ot0 = ms(T.OT[:], 0.0)
 
     arr = [("rH%d" % q, NE) for q in range(n_ranks) if q != me] + [("rA%d" % q, NE) for q in range(n_ranks) if (q + 1) % n_ranks != me]
     ls = tt(T.LS[:], T.LANDH[:], T.LANDA[:], OP.add, arr + [ownh, owna])
     wn = tr(T.WIN[:], T.LS[:], [ls])
     gm = run("v", lambda: vec.tensor_tensor(T.GM[:], T.WIN[:, 0:32].indirect(T.FL[:]), T.MASK[:], OP.mult), [wn, flu, mask])
-    ot0 = ms(T.OT[:], 0.0)
     t2 = tr(T.TR[:], T.GM[:], [gm])
     for h in range(2):
         sc = run("v", lambda: vec.tensor_tensor_scan(T.SCF[:, 128 * h:128 * h + 128], T.R0[:], T.TR[:, h::2], 0.0, OP.mult, OP.add), [t2, r0])

@@ -4,7 +4,7 @@ from concourse.mybir import AluOpType, AxisListType, ActivationFunctionType
 V = 6144
 W = 6152
 KEYS = 4096
-SEL = {"SHD": 0, "SVP": 1, "SAP": 2, "H2": 3, "H1": 4, "A0": 5, "A1": 6, "A2": 7, "A3": 8, "A4": 9}
+SEL = {"SVP": 0, "SHD": 1, "H2": 2, "H1": 3, "HIT": 4, "SAP": 5}
 
 _f, _b, _i, _u = "float32", "bfloat16", "int32", "uint16"
 
@@ -14,13 +14,14 @@ def _bufs():
 
     def sb(name, n, t):
         s[name] = ("sbuf", [128, n], t)
-    sb("WH", KEYS, _b); sb("WP", W, _b); sb("W32", W, _f); sb("Z", 1024, _b)
+    sb("WP", W, _b); sb("WV", W, _f); sb("Z", 1024, _b)
     sb("HC", 256, _i); sb("VC", 384, _i); sb("AC", 384, _i); sb("VTC", 384, _i); sb("ATC", 384, _i)
     sb("HHI", 256, _b); sb("HLO", 256, _b); sb("VHI", 384, _b); sb("VLO", 384, _b); sb("AHI", 384, _b); sb("ALO", 384, _b)
     sb("VTF", 384, _f); sb("ATF", 384, _f)
-    sb("I256", 256, _b); sb("ZI", 128, _b); sb("MOD16", 128, _b); sb("OFF", 8, _b); sb("PC", 1, _i); sb("PAT", 8, _i)
-    sb("PATI", 8, _i); sb("X", 128, _i); sb("XH", 128, _i); sb("Y", 192, _i); sb("Y15", 192, _i); sb("C1", 192, _f); sb("C", 192, _f)
-    sb("US", 128, _b); sb("UI", 128, _b); sb("IB", 128, _b); sb("IF", 128, _f); sb("S", 1280, _b)
+    sb("I128", 128, _b); sb("I256", 256, _b); sb("ZI", 128, _b); sb("MOD16", 192, _b); sb("XB", 128, _b); sb("OFF", 8, _b)
+    sb("PC", 1, _i); sb("PAT", 8, _i)
+    sb("PATI", 8, _i); sb("X", 128, _i); sb("XH", 128, _i); sb("C1", 192, _f); sb("C", 192, _f)
+    sb("US", 128, _b); sb("UI", 128, _b); sb("IB", 128, _b); sb("IF", 128, _f); sb("S", 768, _b); sb("IND", 128, _b)
     sb("PINT", 8, _i); sb("COL", 12, _f); sb("EV1", 4, _f)
     sb("RK", 2, _i); sb("RT", 2, _i); sb("OWNI", 2, _i); sb("OWNF", 2, _f); sb("KI", 4, _i); sb("KF", 4, _f); sb("TF", 2, _f)
     sb("O", 8, _b); sb("PR", 8, _f); sb("WI", 2, _i); sb("AB", 4, _i); sb("ABF", 4, _f); sb("LH", 256, _b); sb("RH", 128, _b)
@@ -31,10 +32,10 @@ def _bufs():
     sb("M0", 24, _u); sb("ALV", 24, _f); sb("ALS", 24, _f)
     sb("TB", 512, _f); sb("TH", 384, _f); sb("HIT", 384 * 7, _b)
     sb("HN", 72, _f); sb("HD", 48, _f); sb("HI", 48, _f); sb("HP", 48, _f); sb("HX", 24, _f)
-    sb("HV", 384, _f); sb("HT", 384, _f); sb("PKH", 32, _f)
-    sb("MF", 144, _f); sb("AD", 120, _f); sb("AI", 120, _f); sb("AP", 120, _f); sb("AX", 48, _f); sb("AY", 24, _f); sb("AZ", 24, _f)
-    sb("AW", 24, _f); sb("AV", 384, _f); sb("AT", 384, _f); sb("PKA", 32, _f)
-    sb("LANDH", 32, _f); sb("LANDA", 32, _f); sb("LS", 32, _f); sb("WIN", 32, _f)
+    sb("HV", 384, _f); sb("HT", 384, _f); sb("PK", 56, _f)
+    sb("MF", 120, _f); sb("AI", 120, _f); sb("AP", 96, _f); sb("AX", 48, _f); sb("AY", 24, _f); sb("AZ", 24, _f)
+    sb("D4", 24, _f); sb("AQ", 24, _f); sb("AW", 24, _f); sb("AV", 384, _f); sb("AT", 384, _f)
+    sb("LAND", 64, _f); sb("LS", 32, _f); sb("WIN", 32, _f)
     sb("FI", 4, _i); sb("FF", 4, _f); sb("FR", 32, _b); sb("C8", 128, _b); sb("FL", 16, _u); sb("QB", 256, _b); sb("JS", 512, _b)
     sb("PF", 8, _f); sb("MASK", 256, _f); sb("R0", 128, _f)
     sb("GM", 256, _f); sb("TR", 256, _f); sb("SCF", 256, _f); sb("OT", 32, _f); sb("YT", 32, _f)
@@ -46,9 +47,13 @@ def _bufs():
 SCRATCH = _bufs()
 LOADS = ["rk", "rt", "hd", "vp", "ap", "vt", "at", "hh", "hl", "vh", "vl", "ah", "al", "vv", "av", "vtr", "atr", "y0", "y1", "y2", "y3"]
 SEMAPHORES = (["sv", "ss", "st", "sg"] + ["d_" + x for x in LOADS]
-              + ["r%s%d" % (k, r) for k in "LTHA" for r in range(4)] + ["rMA", "rMB", "rAL"]
-              + ["xL", "xT", "xMA", "xMB", "xAL", "xH", "xA"])
+              + ["r%s%d" % (k, r) for k in "LTA" for r in range(4)] + ["rM", "rAL"]
+              + ["xL", "xT", "xM", "xAL", "xA"])
 NE = 4
+NS = 8
+VP = (1024, 1536, 2048)
+GV = (1152, 1920)
+SV = 5632
 
 
 def rank_program(g, core, T, topo):
@@ -57,7 +62,7 @@ def rank_program(g, core, T, topo):
         return
     OP, ACT, X = AluOpType, ActivationFunctionType, AxisListType.X
     n_ranks = len(T.cores)
-    nxt, prv = (me + 1) % n_ranks, (me - 1) % n_ranks
+    nxt = (me + 1) % n_ranks
     eng = {"v": g.vector, "s": g.scalar, "t": g.tensor, "g": g, "y": g.sync}
     semof = {"v": "sv", "s": "ss", "t": "st", "g": "sg"}
     cnt = {"sv": 0, "ss": 0, "st": 0, "sg": 0}
@@ -128,11 +133,11 @@ def rank_program(g, core, T, topo):
         g.remote_dma_fused(tl, local_sem=T.sem[local])
         final.append((local, tot))
 
-    def send(d, src, dst, sem, local, part):
-        es = topo.engines(core, T.cores[d])[NE * part:NE * part + NE]
+    def send(d, src, dst, sem, local):
+        es = topo.engines(core, T.cores[d])[:NS]
         rid, pid = topo.addr(T.cores[d], core)
         g.remote_dma(dst, src, T.sem[sem], T.sem[local], pid, rid, sum(1 << e for e in es))
-        final.append((local, NE))
+        final.append((local, NS))
 
     others = [(me + k) % n_ranks for k in range(1, n_ranks)]
 
@@ -140,28 +145,52 @@ def rank_program(g, core, T, topo):
     d_rt = dma("s", T.RT[:], T.rt[:], "rt")
     d_hd = dma("y", T.HC[:], T.hd[:], "hd")
     d_vp = dma("s", T.VC[:], T.vp[:], "vp")
-    d_ap = dma("y", T.AC[:], T.ap[:], "ap")
+    d_ap = dma("s", T.AC[:], T.ap[:], "ap")
     d_vt = dma("y", T.VTC[:], T.vt[:], "vt")
     d_at = dma("y", T.ATC[:], T.at[:], "at")
 
-    c_zi = iota(T.ZI[:], [[1, 128]], 0, -1)
-    c_i = iota(T.I256[:], [[1, 256]], 0, 0)
-    c_off = iota(T.OFF[:], [[0, 2], [128, 4]], 0, 0)
-    c_mod = iota(T.MOD16[:], [[0, 8], [1, 16]], 0, 0)
-    c_x = iota(T.X[:], [[-16, 8], [0, 16]], 0, 1, flag=False)
-    c_y = iota(T.Y[:], [[0, 12], [1, 16]], 0, -1, flag=False)
     c_pc = iota(T.PC[:], [[0, 1]], 0, 1, flag=False)
+    c_x = iota(T.X[:], [[-16, 8], [0, 16]], 0, 1, flag=False)
+    c_zi = iota(T.ZI[:], [[1, 128]], 0, -1)
+    c_i = iota(T.I128[:], [[1, 128]], 0, 0)
+    c_off = iota(T.OFF[:], [[0, 2], [128, 4]], 0, 0)
+    c_mod = iota(T.MOD16[:], [[0, 12], [1, 16]], 0, 0)
     c_pat = iota(T.PAT[:], [[1, 4], [-1, 2]], 0, 0, flag=False)
-    fill = [iota(T.W32[:, 0:1024], [[0, 1024]], 0, 0)]
+    c_xb = iota(T.XB[:], [[-16, 8], [0, 16]], 0, 1)
+    wpf, vfill = [], []
 
-    def zeros_s(a, b):
-        fill.append(copy_s(T.W32[:, a:b], T.Z[:, 0:b - a], [z]))
+    def zeros_g(win, l, a, b):
+        l.append(iota(win[:, a:b], [[0, b - a]], 0, 0))
+
+    def zeros_s(win, l, a, b):
+        for i in range(a, b, 1024):
+            n = min(1024, b - i)
+            l.append(copy_s(win[:, i:i + n], T.Z[:, 0:n], [z]))
+
+    zeros_g(T.WV, vfill, 0, GV[0])
 
     z = ms(T.Z[:], 0.0)
-    ms(T.WH[:, 0:3072], 0.0)
-    wpf = [copy_s(T.WP[:, a:a + 1024], T.Z[:], [z]) for a in range(0, V, 1024)]
-    zeros_s(5120, 6144)
-    zeros_s(4352, 5120)
+    zeros_s(T.WP, wpf, VP[2], V)
+    zeros_s(T.WV, vfill, GV[1], SV)
+    pint = ts(T.PINT[:, 0:1], T.PC[:], 15, None, OP.bitwise_and, toks=[c_pc])
+    ev = ts(T.PINT[:, 1:2], T.PC[:], 1, None, OP.bitwise_and)
+    col = ts(T.COL[:, 0:1], T.PINT[:, 0:1], -16384.0, 245760.0, OP.mult, OP.add, toks=[pint])
+    e1 = ts(T.EV1[:, 0:1], T.PINT[:, 1:2], 0.0, 6144.0, OP.is_equal, OP.mult, toks=[ev])
+    e2 = ts(T.EV1[:, 1:2], T.PINT[:, 1:2], 0.0, 1048576.0, OP.is_equal, OP.mult)
+    p16 = cp(T.COL[:, 3:4], T.PINT[:, 0:1])
+    wpf.append(ms(T.WP[:, 0:VP[0]], 0.0))
+    w1 = ts(T.WP[:, V:W], T.Z[:, 0:8], T.EV1[:, 0:1], None, OP.add, toks=[e1])
+    w2 = ts(T.WV[:, V:W], T.Z[:, 0:8], T.EV1[:, 1:2], None, OP.add, toks=[e2])
+    smat = {}
+
+    def S(name):
+        return T.S[:, 128 * SEL[name]:128 * SEL[name] + 128]
+
+    def weight(name, src, v, wgt=None, toks=()):
+        if wgt is None:
+            smat[name] = ts(S(name), src[:], v, None, OP.is_equal, toks=toks)
+        else:
+            smat[name] = ts(S(name), src[:], v, wgt, OP.is_equal, OP.mult, toks=toks)
 
     us = ts(T.US[:], T.ZI[:], 0.0, None, OP.is_gt, toks=[c_zi])
     ui = ts(T.UI[:], T.ZI[:], 0.0, None, OP.is_ge)
@@ -171,50 +200,55 @@ def rank_program(g, core, T, topo):
     k2 = ts(T.KI[:, 2:4], T.RK[:], 63, None, OP.bitwise_and)
     ownf = cp(T.OWNF[:], T.OWNI[:], [owni])
     kf = cp(T.KF[:], T.KI[:], [k2])
-    o0 = ts(T.O[:, 0:4], T.I256[:, 0:4], T.OWNF[:, 0:1], None, OP.is_equal, toks=[ownf, c_i])
-    o1 = ts(T.O[:, 4:8], T.I256[:, 0:4], T.OWNF[:, 1:2], None, OP.is_equal)
-    p = T.P0[:, 0:4]
+    o0 = ts(T.O[:, 0:4], T.I128[:, 0:4], T.OWNF[:, 0:1], None, OP.is_equal, toks=[ownf, c_i])
+    o1 = ts(T.O[:, 4:8], T.I128[:, 0:4], T.OWNF[:, 1:2], None, OP.is_equal)
+    p, q = T.P0[:, 0:4], T.P1[:, 0:4]
     mm(p, T.IB[:], T.OFF[:, 0:4], True, False, [ib, c_off])
+    mm(q, T.IB[:], T.OFF[:, 4:8], True, False)
     mm(p, T.US[:], T.O[:, 0:4], False, False, [o0])
+    mm(q, T.UI[:], T.O[:, 0:4], False, False)
     mm(p, T.US[:], T.O[:, 4:8], False, True, [o1])
-    p = T.P0[:, 4:8]
-    mm(p, T.IB[:], T.OFF[:, 4:8], True, False)
-    mm(p, T.UI[:], T.O[:, 0:4], False, False)
-    pos = mm(p, T.US[:], T.O[:, 4:8], False, True)
-    hh = cp(T.HHI[:], T.HC[:], [d_hd])
-    wh = ms(T.WH[:, 3072:4096], 0.0)
-    pr = tt(T.PR[:], T.P0[:, 0:8], T.O[:], OP.mult, [pos, o1])
+    pos = mm(q, T.US[:], T.O[:, 4:8], False, True)
+    wpf.append(ms(T.WP[:, VP[0]:VP[1]], 0.0))
+    tt(T.PR[:, 0:4], T.P0[:, 0:4], T.O[:, 0:4], OP.mult, [pos, o1])
+    pr = tt(T.PR[:, 4:8], T.P1[:, 0:4], T.O[:, 4:8], OP.mult)
+    xh = ts(T.XH[:], T.X[:], 1, None, OP.arith_shift_right, toks=[c_x])
     run("v", lambda: vec.tensor_reduce(T.WI[:, 0:1], T.PR[:, 0:4], X, OP.max), [pr])
     wi = run("v", lambda: vec.tensor_reduce(T.WI[:, 1:2], T.PR[:, 4:8], X, OP.max))
+    weight("SVP", T.XH, 0.0, toks=[xh])
     ts(T.AB[:, 0:2], T.WI[:], 15, None, OP.bitwise_and, toks=[wi])
     ab = ts(T.AB[:, 2:4], T.WI[:], 4, None, OP.arith_shift_right)
+    weight("SHD", T.XH, 1.0)
     abf = cp(T.ABF[:], T.AB[:], [ab])
+    weight("SAP", T.XH, 2.0)
     lt = []
     for h in range(2):
-        ts(T.LH[:, 128 * h:128 * h + 128], T.MOD16[:], T.ABF[:, h:h + 1], None, OP.is_equal, toks=[abf, c_mod, kf])
+        ts(T.LH[:, 128 * h:128 * h + 128], T.MOD16[:, 0:128], T.ABF[:, h:h + 1], None, OP.is_equal, toks=[abf, c_mod, kf])
         for e in range(2):
             k = 64 * h + 32 * e
-            lt.append(ts(T.RH[:, k:k + 32], T.I256[:, 0:32], T.ABF[:, 2 + h:3 + h], T.KF[:, 2 * e + h:2 * e + h + 1],
+            lt.append(ts(T.RH[:, k:k + 32], T.I128[:, 0:32], T.ABF[:, 2 + h:3 + h], T.KF[:, 2 * e + h:2 * e + h + 1],
                          OP.is_equal, OP.mult))
     for i in range(4):
         h = i // 2
         lst = mm(T.P7[:, 0:32], T.LH[:, 128 * h:128 * h + 128], T.RH[:, 32 * i:32 * i + 32], i == 0, i == 3, [lt[i]])
-    hl = tt(T.HLO[:], T.HC[:], T.HHI[:], OP.subtract, [hh])
+    wpf.append(ms(T.WP[:, VP[1]:VP[2]], 0.0))
     lu = cp(T.LSTU[:], T.P7[:, 0:32], [lst])
     wait("g", [lu])
     fused([(d, T.LSTU[:, 8 * d:8 * d + 6], T["LI%d" % me][:]) for d in others], "rL%d" % me, "xL")
-    fill.append(iota(T.W32[:, 1024:2304], [[0, 1280]], 0, 0))
 
-    d_hh = dma("y", T.WH[4:128:16, :], T.HHI[:], "hh", [hl, wh])
-    d_hl = dma("y", T.WH[5:128:16, :], T.HLO[:], "hl")
+    hh = cp(T.HHI[:], T.HC[:], [d_hd])
+    th_ = mm(T.P4[:, 0:256], T.IB[:], T.HHI[:], True, True, [hh])
+    d_hh = dma("y", T.WP[2:128:16, 0:KEYS], T.HHI[:], "hh", [hh] + wpf)
     vh = cp(T.VHI[:], T.VC[:], [d_vp])
-    vl = tt(T.VLO[:], T.VC[:], T.VHI[:], OP.subtract, [vh])
-    d_vh = dma("y", T.WP[0:128:16, 0:V], T.VHI[:], "vh", [vl] + wpf)
-    d_vl = dma("y", T.WP[1:128:16, 0:V], T.VLO[:], "vl")
+    tv_ = mm(T.P5[:, 0:384], T.IB[:], T.VHI[:], True, True, [vh])
+    d_vh = dma("y", T.WP[0:128:16, 0:V], T.VHI[:], "vh", [vh])
     ah = cp(T.AHI[:], T.AC[:], [d_ap])
-    al = tt(T.ALO[:], T.AC[:], T.AHI[:], OP.subtract, [ah])
-    d_ah = dma("y", T.WP[2:128:16, 0:V], T.AHI[:], "ah", [al])
-    d_al = dma("y", T.WP[3:128:16, 0:V], T.ALO[:], "al")
+    tah = mm(T.P6[:, 0:384], T.IB[:], T.AHI[:], True, True, [ah])
+    d_ah = dma("y", T.WP[4:128:16, 0:V], T.AHI[:], "ah", [ah])
+    hl = tt(T.HLO[:], T.HC[:], T.P4[:, 0:256], OP.subtract, [th_])
+    d_hl = dma("y", T.WP[3:128:16, 0:KEYS], T.HLO[:], "hl", [hl])
+    vl = tt(T.VLO[:], T.VC[:], T.P5[:, 0:384], OP.subtract, [tv_])
+    d_vl = dma("y", T.WP[1:128:16, 0:V], T.VLO[:], "vl", [vl])
 
     ts(T.SI[:], T.WI[:], 127, None, OP.bitwise_and)
     tf = cp(T.TF[:], T.RT[:], [d_rt])
@@ -222,33 +256,29 @@ def rank_program(g, core, T, topo):
     sf = cp(T.SF[:], T.SI[:], [tf])
     tl = []
     for h in range(2):
-        ts(T.SH[:, 128 * h:128 * h + 128], T.I256[:, 0:128], T.SF[:, h:h + 1], None, OP.is_equal, toks=[sf, pati])
+        ts(T.SH[:, 128 * h:128 * h + 128], T.I128[:], T.SF[:, h:h + 1], None, OP.is_equal, toks=[sf, pati])
         tl.append(ts(T.RTT[:, 8 * h:8 * h + 8], T.PATI[:], T.OWNF[:, h:h + 1], T.TF[:, h:h + 1], OP.is_equal, OP.mult))
     mm(T.P0[:, 16:24], T.SH[:, 0:128], T.RTT[:, 0:8], True, False, [tl[0], pr])
     tm = mm(T.P0[:, 16:24], T.SH[:, 128:256], T.RTT[:, 8:16], False, True, [tl[1]])
-    y15 = ts(T.Y15[:], T.Y[:], 15, None, OP.bitwise_and, toks=[c_y])
-    xh = ts(T.XH[:], T.X[:], 1, None, OP.arith_shift_right, toks=[c_x])
-    pint = ts(T.PINT[:, 0:1], T.PC[:], 15, None, OP.bitwise_and, toks=[c_pc])
-    ev = ts(T.PINT[:, 1:2], T.PC[:], 1, None, OP.bitwise_and)
-    c1 = ts(T.C1[:], T.Y15[:], 1.0, 0.96875, OP.min, OP.subtract, toks=[y15])
-    xhd = ts(T.S[:, 0:128], T.XH[:], 2.0, None, OP.is_equal, toks=[xh])
-    ts_tok = cp(T.TS[:], T.P0[:, 16:24], [tm])
+    al = tt(T.ALO[:], T.AC[:], T.P6[:, 0:384], OP.subtract, [tah])
+    d_al = dma("y", T.WP[5:128:16, 0:V], T.ALO[:], "al", [al])
+    tsa = cp(T.TS[:, 0:8:2], T.P0[:, 16:24:2], [tm])
+    ts_tok = tt(T.TS[:, 1:8:2], T.P0[:, 17:24:2], T.TS[:, 0:8:2], OP.subtract, [tsa])
     wait("g", [ts_tok])
     fused([(d, T.TS[:, 2 * d:2 * d + 2], T["TC%d" % me][:]) for d in others], "rT%d" % me, "xT")
-    fill.append(iota(T.W32[:, 2304:2816], [[0, 512]], 0, 0))
-    cc = ts(T.C[:], T.C1[:], 524288.0, None, OP.mult, toks=[c1])
-    col = ts(T.COL[:, 0:1], T.PINT[:, 0:1], -16384.0, 245760.0, OP.mult, OP.add, toks=[pint])
-    e1 = ts(T.EV1[:, 0:1], T.PINT[:, 1:2], 0.0, 6144.0, OP.is_equal, OP.mult, toks=[ev])
-    w1 = ts(T.WP[:, V:W], T.Z[:, 0:8], T.EV1[:, 0:1], None, OP.add, toks=[e1])
-    xvp = ts(T.S[:, 128:256], T.XH[:], 0.0, None, OP.is_equal)
 
-    WHT = [wh, d_hh, d_hl]
-    WPT = wpf + [w1, d_vh, d_vl, d_ah, d_al]
+    c1 = ts(T.C1[:], T.MOD16[:], T.COL[:, 3:4], -524288.0, OP.is_equal, OP.mult, toks=[p16, c_xb])
+    ind = ts(T.IND[:], T.MOD16[:, 0:128], 2.0, None, OP.is_equal)
+    idf = ts(T.IF[:], T.ZI[:], 0.0, None, OP.is_equal)
+    cc = ts(T.C[:], T.C1[:], 16384.0, None, OP.add, toks=[c1])
+    vfill.append(ms(T.WV[:, SV:V], 0.0))
+    tv = cp(T.VTF[:], T.VTC[:], [d_vt])
+    ta_ = cp(T.ATF[:], T.ATC[:], [d_at])
+    zeros_g(T.WV, vfill, GV[0], GV[1])
+
+    WPT = wpf + [w1, d_hh, d_hl, d_vh, d_vl, d_ah, d_al]
     banks = [T.P2[:, 0:192], T.P3[:, 0:192]]
     codes = [T.P4[:, 0:192], T.P5[:, 0:192]]
-
-    def S(name):
-        return T.S[:, 128 * SEL[name]:128 * SEL[name] + 128]
 
     def G(i, half):
         return T.G[:, 384 * i + 192 * half:384 * i + 192 * half + 192]
@@ -261,165 +291,160 @@ def rank_program(g, core, T, topo):
         t = run("v", lambda: vec.tensor_tensor_scan(T.SC[:, o:o + 192], T.C[:], src, 0.0, OP.add, OP.max), [tok, cc])
         return t, T.SC[:, o + 15:o + 192:16]
 
-    smat = {}
-
-    def weights(*names):
-        for name, src, v, wgt in names:
-            if wgt is None:
-                smat[name] = ts(S(name), src[:], v, None, OP.is_equal)
-            else:
-                smat[name] = ts(S(name), src[:], v, wgt, OP.is_equal, OP.mult)
+    def both(i):
+        return T.SC[:, 384 * i + 15:384 * i + 384:16]
 
     hg = []
     for r in [me] + others:
         src = T.LSTU[:, 8 * me:8 * me + 6] if r == me else T["LI%d" % r][:]
         tok = lu if r == me else ("rL%d" % r, NE)
-        hg.append(copy_s(T.G[:, 96 * r:96 * r + 96], T.WH[:, 0:KEYS].indirect(src), WHT + [tok]))
-    zeros_s(3328, 4352)
-    fill.append(ms(T.W32[:, 2816:3328], 0.0))
-    m = [mm(banks[h], S("SHD"), G(0, h), True, True, [xhd, hg[-1]]) for h in range(2)]
-    l0, e0 = [], []
-    hs = []
-    for h in range(2):
-        t, pk = scan(0, h, banks[h], m[h])
-        l0.append(ts(Ls(0, h), pk, T.COL[:, 0:1], 6144.0, OP.subtract, OP.min, toks=[t, col]))
-        hs.append((t, pk))
-    ga = copy_s(G(1, 0), T.WP[:, 0:W].indirect(Ls(0, 0)), WPT + [l0[0]])
-    gb = cp(G(1, 1), T.WP[:, 0:W].indirect(Ls(0, 1)), WPT + [l0[1]])
-    ts(T.COL[:, 1:2], T.COL[:, 0:1], 6144.0, None, OP.add)
-    cp2 = ts(T.COL[:, 2:3], T.COL[:, 0:1], 12288.0, None, OP.add)
-    for h in range(2):
-        a = ts(T.N[:, 12 * h:12 * h + 12], hs[h][1], T.COL[:, 0:1], 6144.0, OP.subtract, OP.max)
-        e0.append(ts(T.E0[:, 12 * h:12 * h + 12], T.N[:, 12 * h:12 * h + 12], T.COL[:, 1:2], None, OP.subtract, toks=[a, cp2]))
-    m = [mm(banks[0], S("SVP"), G(1, 0), True, True, [xvp, ga, hs[0][0]]), mm(banks[1], S("SVP"), G(1, 1), True, True, [gb, hs[1][0]])]
-    tv = cp(T.VTF[:], T.VTC[:], [d_vt])
-    ta_ = cp(T.ATF[:], T.ATC[:], [d_at])
-    l1, sct = [], []
-    for h in range(2):
-        t, pk = scan(1, h, banks[h], m[h])
-        n1 = T.N[:, 24 + 12 * h:36 + 12 * h]
-        a = tt(n1, pk, T.E0[:, 12 * h:12 * h + 12], OP.add, [t, e0[h]])
-        l1.append(ts(Ls(1, h), n1, 6144.0, None, OP.min, toks=[a]))
-        sct.append(t)
-    ga = copy_s(G(2, 0), T.WP[:, 0:W].indirect(Ls(1, 0)), [l1[0]])
-    gb = cp(G(2, 1), T.WP[:, 0:W].indirect(Ls(1, 1)), [l1[1]])
-    e1v = [ts(T.E1[:, 12 * h:12 * h + 12], T.N[:, 24 + 12 * h:36 + 12 * h], 6144.0, T.COL[:, 2:3], OP.max, OP.subtract) for h in range(2)]
-    idf = ts(T.IF[:], T.ZI[:], 0.0, None, OP.is_equal)
-    m = [mm(banks[0], S("SVP"), G(2, 0), True, True, [ga, sct[0]]), mm(banks[1], S("SVP"), G(2, 1), True, True, [gb, sct[1]])]
+        hg.append(copy_s(T.G[:, 96 * r:96 * r + 96], T.WP[:, 0:KEYS].indirect(src), WPT + [tok]))
+
+    order, thm = [me] + others, [None] * n_ranks
+    tbank = [T.P1, T.P6]
 
     def bcast(r):
         c, tok = (T.TS[:, 2 * me:2 * me + 2], ts_tok) if r == me else (T["TC%d" % r][:], ("rT%d" % r, NE))
-        x = run("s", lambda: act.activation(T.TB[:, 128 * r:128 * r + 128], T.Z[:, 0:128], ACT.Identity, bias=c[:, 0:1]), [tok, z])
-        return run("s", lambda: act.activation(T.TB[:, 128 * r + 2:128 * r + 128:16], T.Z[:, 0:8], ACT.Identity, bias=c[:, 1:2]), [x])
+        return run("s", lambda: act.activation(T.TB[:, 128 * r:128 * r + 128], T.IND[:], ACT.Identity, bias=c[:, 0:1], scale=c[:, 1:2]),
+                   [tok, ind])
 
     def tmm(r, tok):
-        return mm(T.P1[:, 96 * r:96 * r + 96], T.TB[:, 128 * r:128 * r + 128], T.IF[:, 0:96], True, True, [tok, idf])
-    bt = [bcast(r) for r in range(4)]
-    th = [tmm(r, bt[r]) for r in range(4)]
-    tht = copy_s(T.TH[:], T.P1[:, 0:384], [th[3]])
-    l2, sc2 = [], []
-    for h in range(2):
-        t, pk = scan(2, h, banks[h], m[h])
-        n2 = T.N[:, 48 + 12 * h:60 + 12 * h]
-        a = tt(n2, pk, T.E1[:, 12 * h:12 * h + 12], OP.add, [t, e1v[h]])
-        l2.append(cp(Ls(3, h), n2, [a]))
-        sc2.append(t)
-        wait("g", [l2[h]])
-        send(nxt, Ls(3, h), T.M0[:, 12 * h:12 * h + 12], "rMA" if h == 0 else "rMB", "xMA" if h == 0 else "xMB", h)
+        k = 96 * (r % 2)
+        thm[r] = mm(tbank[r // 2][:, k:k + 96], T.TB[:, 128 * r:128 * r + 128], T.IF[:, 0:96], True, True, [tok, idf, pr])
 
-    d_vv = dma("y", T.W32[1:128:16, 0:V], T.vv[:], "vv", fill)
-    d_av = dma("y", T.W32[3:128:16, 0:V], T.av[:], "av")
-    d_vtr = dma("y", T.W32[0:128:16, 0:V], T.VTF[:], "vtr", [tv])
-    d_atr = dma("y", T.W32[2:128:16, 0:V], T.ATF[:], "atr", [ta_])
-    e2 = ts(T.EV1[:, 1:2], T.PINT[:, 1:2], 0.0, 1048576.0, OP.is_equal, OP.mult)
-    w2 = ts(T.W32[:, V:W], T.Z[:, 0:8], T.EV1[:, 1:2], None, OP.add, toks=[e2])
-    W32T = fill + [w2, d_vv, d_av, d_vtr, d_atr]
-    n0f = cp(T.HN[:, 0:24], T.L[:, 0:24], [l0[1]])
-    n1f = cp(T.HN[:, 24:48], T.L[:, 24:48], [l1[1]])
+    bt = bcast(me)
+    m = [mm(banks[h], S("SHD"), G(0, h), True, True, [smat["SHD"], hg[-1]]) for h in range(2)]
+    tmm(me, bt)
+    ts(T.COL[:, 1:2], T.COL[:, 0:1], 6144.0, None, OP.add, toks=[col])
+    cp2 = ts(T.COL[:, 2:3], T.COL[:, 0:1], 12288.0, None, OP.add)
+    for k, v in ((4, 1.0), (5, 2.0), (6, 8192.0)):
+        colt = ts(T.COL[:, k:k + 1], T.COL[:, 0:1], v, None, OP.add)
+    ks = [scan(0, h, banks[h], m[h]) for h in range(2)]
+    l0 = [ts(Ls(0, h), ks[h][1], T.COL[:, 0:1], 6144.0, OP.subtract, OP.min, toks=[ks[h][0], col]) for h in range(2)]
+    ga = copy_s(G(1, 0), T.WP[:, 0:W].indirect(Ls(0, 0)), [l0[0]])
+    bt = [bcast(r) for r in others]
+    gb = cp(G(1, 1), T.WP[:, 0:W].indirect(Ls(0, 1)), WPT + [l0[1]])
+    a = ts(T.N[:, 0:24], both(0), T.COL[:, 0:1], 6144.0, OP.subtract, OP.max)
+    weight("H2", T.XB, 0.0, 2.0)
+    weight("H1", T.XB, 0.0)
+    e0 = ts(T.E0[:], T.N[:, 0:24], T.COL[:, 1:2], None, OP.subtract, toks=[a, cp2])
+    m = [mm(banks[0], S("SVP"), G(1, 0), True, True, [ga, ks[0][0]]), mm(banks[1], S("SVP"), G(1, 1), True, True, [gb, ks[1][0]])]
+    tmm(order[1], bt[0])
+    weight("HIT", T.XB, 2.0, 8192.0)
+    ks = [scan(1, h, banks[h], m[h]) for h in range(2)]
+    a = [tt(T.N[:, 24 + 12 * h:36 + 12 * h], ks[h][1], T.E0[:, 12 * h:12 * h + 12], OP.add, [ks[h][0], e0]) for h in range(2)]
+    l1 = [ts(Ls(1, h), T.N[:, 24 + 12 * h:36 + 12 * h], 6144.0, None, OP.min, toks=[a[h]]) for h in range(2)]
+    d_vtr = dma("y", T.WV[0:128:16, 0:V], T.VTF[:], "vtr", [tv] + vfill)
+    d_atr = dma("y", T.WV[2:128:16, 0:V], T.ATF[:], "atr", [ta_])
+    d_vv = dma("y", T.WV[1:128:16, 0:V], T.vv[:], "vv")
+    d_av = dma("y", T.WV[3:128:16, 0:V], T.av[:], "av")
+    WVT = vfill + [w2, d_vtr, d_atr, d_vv, d_av]
+    ga = copy_s(G(2, 0), T.WP[:, 0:W].indirect(Ls(1, 0)), [l1[0]])
+    gb = cp(G(2, 1), T.WP[:, 0:W].indirect(Ls(1, 1)), [l1[1]])
+    e1v = ts(T.E1[:], T.N[:, 24:48], 6144.0, T.COL[:, 2:3], OP.max, OP.subtract)
+    cp(T.HN[:, 0:24], T.L[:, 0:24], [l0[1]])
+    cp(T.HN[:, 24:48], T.L[:, 24:48], [l1[1]])
     hc = ms(T.HN[:, 48:72], 6144.0)
-    mf5 = ms(T.MF[:, 120:144], 6144.0)
+    pk0 = ms(T.PK[:, 48:56], 0.0)
+    m = [mm(banks[0], S("SVP"), G(2, 0), True, True, [ga, ks[0][0]]), mm(banks[1], S("SVP"), G(2, 1), True, True, [gb, ks[1][0]])]
+    for k in (2, 3):
+        tmm(order[k], bt[k - 1])
+    tht = [copy_s(T.TH[:, 192 * h:192 * h + 192], tbank[h][:, 0:192], [thm[2 * h], thm[2 * h + 1]]) for h in range(2)]
+    ks = [scan(2, h, banks[h], m[h]) for h in range(2)]
+    sc2 = [t for t, pk in ks]
+    a = [tt(T.N[:, 48 + 12 * h:60 + 12 * h], ks[h][1], T.E1[:, 12 * h:12 * h + 12], OP.add, [ks[h][0], e1v]) for h in range(2)]
+    l2 = [cp(Ls(3, h), T.N[:, 48 + 12 * h:60 + 12 * h], [a[h]]) for h in range(2)]
+    wait("g", l2)
+    send(nxt, T.L[:, 72:96], T.M0[:], "rM", "xM")
+    c_256 = iota(T.I256[:], [[1, 256]], 0, 0)
     hd_ = tt(T.HD[:], T.HN[:, 0:48], T.HN[:, 24:72], OP.subtract, [hc])
-    pkh0 = ms(T.PKH[:, 24:32], 0.0)
-    pka0 = ms(T.PKA[:, 24:32], 0.0)
-    for k in range(5):
-        colt = ts(T.COL[:, 4 + k:5 + k], T.COL[:, 0:1], float(2 ** k), None, OP.add)
-    weights(("H2", T.X, 0.0, 2.0), ("H1", T.X, 0.0, None), ("SAP", T.XH, 1.0, None), ("A0", T.X, 2.0, 16.0),
-            ("A1", T.X, 2.0, 8.0), ("A2", T.X, 2.0, 4.0), ("A3", T.X, 2.0, 2.0), ("A4", T.X, 2.0, None))
 
     def test(i, h, lst, toks):
         o = 384 * i + 192 * h
-        return run("v", lambda: vec.tensor_tensor(T.HIT[:, o:o + 192], T.W32[:, 0:W].indirect(lst), T.TH[:, 192 * h:192 * h + 192], OP.is_le), toks)
+        return run("v", lambda: vec.tensor_tensor(T.HIT[:, o:o + 192], T.WV[:, 0:W].indirect(lst), T.TH[:, 192 * h:192 * h + 192], OP.is_le), toks)
 
     def hitc(i, h):
         return T.HIT[:, 384 * i + 192 * h:384 * i + 192 * h + 192]
 
-    h0 = [test(0, h, Ls(0, h), W32T + [tht]) for h in range(2)]
+    h0 = [test(0, h, Ls(0, h), WVT + [tht[h]]) for h in range(2)]
     h1 = [test(1, h, Ls(1, h), []) for h in range(2)]
     for h in range(2):
-        mm(codes[h], S("H2"), hitc(0, h), True, False, [h0[h], smat["A4"]])
+        mm(codes[h], S("H2"), hitc(0, h), True, False, [h0[h], smat["HIT"]])
     hcode = [mm(codes[h], S("H1"), hitc(1, h), False, True, [h1[h]]) for h in range(2)]
     hsc = [scan(3, h, codes[h], hcode[h])[0] for h in range(2)]
-    hpk = T.SC[:, 384 * 3 + 15:384 * 4:16]
-    ts(T.HI[:, 0:24], hpk, T.COL[:, 5:6], None, OP.is_ge, toks=[hsc[1], colt])
-    hi = ts(T.HI[:, 24:48], hpk, T.COL[:, 4:5], None, OP.is_ge)
-    als = ts(T.ALS[:], hpk, T.COL[:, 0:1], None, OP.is_equal)
+    als = ts(T.ALS[:], both(3), T.COL[:, 0:1], None, OP.is_equal, toks=[hsc[1], colt])
+    ts(T.HI[:, 0:24], both(3), T.COL[:, 5:6], None, OP.is_ge)
+    hi = ts(T.HI[:, 24:48], both(3), T.COL[:, 4:5], None, OP.is_ge)
     wait("g", [als])
-    send(nxt, T.ALS[:], T.ALV[:], "rAL", "xAL", 0)
-    hp = tt(T.HP[:], T.HI[:], T.HD[:], OP.mult, [hi, hd_])
-    hx = tt(T.HX[:], T.HP[:, 0:24], T.HP[:, 24:48], OP.add, [hp])
-    hsel = ts(T.L[:, 48:72], T.HX[:], 6144.0, None, OP.add, toks=[hx])
+    send(nxt, T.ALS[:], T.ALV[:], "rAL", "xAL")
 
-    def compact(buf, tbuf, pick, row, ab):
+    def compact(buf, tbuf, row, k, ab):
         t0 = tr(tbuf[:, 0:192], buf[:, 0:192], [ab[0]])
         t1 = tr(tbuf[:, 192:384], buf[:, 192:384], [ab[1]])
-        return cp(pick[:, 0:24], tbuf[:, row::16], [t0, t1])
+        return cp(T.PK[:, k:48:2], tbuf[:, row::16], [t0, t1])
 
-    lists = [[T.M0[:, 12 * h:12 * h + 12] for h in range(2)]]
-    toks = [[("rMA", NE), ("rMB", NE)]]
+    lists = [T.M0[:, 12 * h:12 * h + 12] for h in range(2)]
+    arrived = [("rM", NS), ("rM", NS)]
+    hk = [test(2, h, lists[h], [arrived[h]]) for h in range(2)]
+    hs = {"m": ts(T.MF[:, 0:24], T.M0[:], 6144.0, None, OP.subtract, toks=[arrived[0]])}
     prev = sc2
-    for k in range(4):
-        gk = [copy_s(G(3 + k, h), T.WP[:, 0:W].indirect(lists[k][h]), [toks[k][h]]) for h in range(2)]
-        if k == 0:
-            hv = [copy_s(T.HV[:, 192 * h:192 * h + 192], T.W32[:, 0:W].indirect(Ls(2, h)), W32T + [hsel]) for h in range(2)]
-        hk = [test(2 + k, h, lists[k][h], [toks[k][h]]) for h in range(2)]
-        if k == 0:
-            cp(T.MF[:, 0:24], T.M0[:])
+
+    def part(k, j):
+        b = 24 * k
+        if j == 0:
+            if k == 0:
+                hs["p"] = tt(T.HP[:], T.HI[:], T.HD[:], OP.mult, [hi, hd_])
+            else:
+                hs["f"] = ts(T.AI[:, b - 24:b], both(3 + k), T.COL[:, 6:7], None, OP.is_ge)
+        elif j == 1:
+            if k == 0:
+                hs["x"] = tt(T.HX[:], T.HP[:, 0:24], T.HP[:, 24:48], OP.add, [hs["p"]])
+            else:
+                hs["a"] = tt(T.AP[:, b - 24:b], T.AI[:, b - 24:b], T.MF[:, b - 24:b], OP.mult, [hs["f"], hs["m"]])
         else:
-            cp(T.MF[:, 24 * k:24 * k + 24], T.L[:, 24 * (3 + k):24 * (4 + k)], [toks[k][1]])
-        m = [mm(banks[h], S("SAP"), G(3 + k, h), True, True, [gk[h], prev[h]]) for h in range(2)]
+            if k == 0:
+                hs["s"] = ts(T.L[:, 48:72], T.HX[:], 6144.0, None, OP.add, toks=[hs["x"]])
+            hs["m"] = ts(T.MF[:, b + 24:b + 48], T.L[:, 96 + b:120 + b], 6144.0, None, OP.subtract, toks=[arrived[1]])
+
+    for k in range(4):
+        gk = [copy_s(G(3 + k, h), T.WP[:, 0:W].indirect(lists[h]), [arrived[h]]) for h in range(2)]
+        m = []
         for h in range(2):
-            mm(codes[h], S("A%d" % k), hitc(2 + k, h), k == 0, False, [hk[h], hsc[h]])
-        nl, prev = [], []
-        for h in range(2):
-            t, pk = scan(4 + k, h, banks[h], m[h])
-            nl.append(ts(Ls(4 + k, h), pk, T.COL[:, 0:1], None, OP.subtract, toks=[t]))
-            prev.append(t)
-        lists.append([Ls(4 + k, h) for h in range(2)])
-        toks.append(nl)
-    hk = [test(6, h, lists[4][h], [toks[4][h]]) for h in range(2)]
-    mf = cp(T.MF[:, 96:120], T.L[:, 24 * 7:24 * 8])
-    acode = [mm(codes[h], S("A4"), hitc(6, h), False, True, [hk[h]]) for h in range(2)]
-    ad = tt(T.AD[:], T.MF[:, 0:120], T.MF[:, 24:144], OP.subtract, [mf, mf5])
-    ph = compact(T.HV, T.HT, T.PKH, 1, hv)
-    wait("g", [ph, pkh0])
-    fused([(d, T.PKH[:, 6 * d:6 * d + 8], T.LANDH[:, 8 * me:8 * me + 8]) for d in others], "rH%d" % me, "xH")
-    asc = [scan(8, h, codes[h], acode[h])[0] for h in range(2)]
-    apk = T.SC[:, 384 * 8 + 15:384 * 9:16]
-    for k in range(5):
-        ai = ts(T.AI[:, 24 * k:24 * k + 24], apk, T.COL[:, 8 - k:9 - k], None, OP.is_ge, toks=[asc[1]])
-    a = tt(T.AP[:], T.AI[:], T.AD[:], OP.mult, [ai, ad])
-    a = tt(T.AX[:], T.AP[:, 0:48], T.AP[:, 48:96], OP.add, [a])
-    a = tt(T.AY[:], T.AX[:, 0:24], T.AX[:, 24:48], OP.add, [a])
-    a = tt(T.AZ[:], T.AY[:], T.AP[:, 96:120], OP.add, [a])
-    a = tt(T.AW[:], T.AZ[:], T.ALV[:], OP.mult, [a, ("rAL", NE)])
+            mm(banks[h], S("HIT"), hitc(2 + k, h), True, False, [hk[h], prev[h]])
+            m.append(mm(banks[h], S("SAP"), G(3 + k, h), False, True, [gk[h]]))
+        lists = [Ls(4 + k, h) for h in range(2)]
+        part(k, 0)
+        t0, pk0_ = scan(4 + k, 0, banks[0], m[0])
+        part(k, 1)
+        a0 = ts(lists[0], pk0_, T.COL[:, 0:1], 6144.0, OP.subtract, OP.min, toks=[t0])
+        t1, pk1_ = scan(4 + k, 1, banks[1], m[1])
+        x0 = test(3 + k, 0, lists[0], [a0])
+        a1 = ts(lists[1], pk1_, T.COL[:, 0:1], 6144.0, OP.subtract, OP.min, toks=[t1])
+        arrived, prev = [a0, a1], [t0, t1]
+        part(k, 2)
+        hk = [x0, test(3 + k, 1, lists[1], [a1])]
+    acode = [mm(banks[h], S("HIT"), hitc(6, h), True, True, [hk[h], prev[h]]) for h in range(2)]
+    hv = [copy_s(T.HV[:, 192 * h:192 * h + 192], T.WV[:, 0:W].indirect(Ls(2, h)), WVT + [hs["s"]]) for h in range(2)]
+    part(4, 0)
+    d4 = tt(T.D4[:], T.MF[:, 96:120], T.ALV[:], OP.mult, [hs["m"], ("rAL", NS)])
+    a0 = tt(T.AX[:, 0:24], T.AP[:, 0:24], T.AP[:, 24:48], OP.add, [hs["a"]])
+    part(4, 1)
+    a1 = tt(T.AX[:, 24:48], T.AP[:, 48:72], T.AP[:, 72:96], OP.add, [hs["a"]])
+    a = tt(T.AY[:], T.AX[:, 0:24], T.AX[:, 24:48], OP.add, [a0, a1])
+    asc = [scan(8, 0, banks[0], acode[0])[0]]
+    az = tt(T.AZ[:], T.AY[:], T.ALV[:], OP.mult, [a])
+    asc.append(scan(8, 1, banks[1], acode[1])[0])
+    ai = ts(T.AI[:, 96:120], both(8), T.COL[:, 6:7], None, OP.is_ge, toks=[asc[1]])
+    a = tt(T.AQ[:], T.AI[:, 96:120], T.D4[:], OP.mult, [ai, d4])
+    a = tt(T.AW[:], T.AQ[:], T.AZ[:], OP.add, [a, az])
     asel = ts(T.L[:, 192:216], T.AW[:], 6144.0, None, OP.add, toks=[a])
-    va = copy_s(T.AV[:, 0:192], T.W32[:, 0:W].indirect(Ls(8, 0)), [asel])
-    vb = cp(T.AV[:, 192:384], T.W32[:, 0:W].indirect(Ls(8, 1)), [asel])
-    pa = compact(T.AV, T.AT, T.PKA, 3, [va, vb])
-    wait("g", [pa, pka0])
-    fused([(d, T.PKA[:, 6 * d:6 * d + 8], T.LANDA[:, 8 * prv:8 * prv + 8]) for d in others], "rA%d" % prv, "xA")
-    ownh = cp(T.LANDH[:, 8 * me:8 * me + 8], T.PKH[:, 6 * me:6 * me + 8], [ph])
-    owna = cp(T.LANDA[:, 8 * prv:8 * prv + 8], T.PKA[:, 6 * me:6 * me + 8], [pa])
+    va = copy_s(T.AV[:, 0:192], T.WV[:, 0:W].indirect(Ls(8, 0)), [asel])
+    vb = cp(T.AV[:, 192:384], T.WV[:, 0:W].indirect(Ls(8, 1)), [asel])
+    ph = compact(T.HV, T.HT, 1, 0, hv)
+    pa = compact(T.AV, T.AT, 3, 1, [va, vb])
+    wait("g", [ph, pa, pk0])
+    fused([(d, T.PK[:, 12 * d:12 * d + 16], T.LAND[:, 16 * me:16 * me + 16]) for d in others], "rA%d" % me, "xA")
+    own = cp(T.LAND[:, 16 * me:16 * me + 16], T.PK[:, 12 * me:12 * me + 16], [ph, pa])
 
     ts(T.FI[:, 0:2], T.WI[:], 31, None, OP.bitwise_and)
     fi = ts(T.FI[:, 2:4], T.WI[:], 5, None, OP.arith_shift_right)
@@ -432,23 +457,24 @@ def rank_program(g, core, T, topo):
     ts(T.PF[:, 4:5], T.PF[:, 0:1], 2.0, 1.0, OP.mult, OP.add)
     a = ts(T.PF[:, 5:6], T.PF[:, 0:1], 32.0, T.PF[:, 1:2], OP.mult, OP.add)
     a = ts(T.PF[:, 6:7], T.PF[:, 5:6], 16.0, None, OP.add, toks=[a, ff])
-    ts(T.C8[:], T.MOD16[:], T.PF[:, 1:2], None, OP.is_equal, toks=[a])
+    ts(T.C8[:], T.MOD16[:, 0:128], T.PF[:, 1:2], None, OP.is_equal, toks=[a])
     for h in range(2):
-        fr = ts(T.FR[:, 16 * h:16 * h + 16], T.I256[:, 0:16], T.PF[:, 3 + h:4 + h], T.FF[:, h:h + 1], OP.is_equal, OP.mult)
+        fr = ts(T.FR[:, 16 * h:16 * h + 16], T.I128[:, 0:16], T.PF[:, 3 + h:4 + h], T.FF[:, h:h + 1], OP.is_equal, OP.mult)
     for h in range(2):
         fl = mm(T.P7[:, 64:80], T.C8[:], T.FR[:, 16 * h:16 * h + 16], h == 0, h == 1, [fr])
     for h in range(2):
-        ts(T.QB[:, 128 * h:128 * h + 128], T.I256[:, 0:128], 0.0, T.FF[:, 2 + h:3 + h], OP.mult, OP.add)
-        js = ts(T.JS[:, 256 * h:256 * h + 256], T.I256[:], T.PF[:, 5 + h:6 + h], None, OP.is_equal)
+        ts(T.QB[:, 128 * h:128 * h + 128], T.I128[:], 0.0, T.FF[:, 2 + h:3 + h], OP.mult, OP.add)
+        js = ts(T.JS[:, 256 * h:256 * h + 256], T.I256[:], T.PF[:, 5 + h:6 + h], None, OP.is_equal, toks=[c_256])
     for h in range(2):
         mk = mm(T.P0[:, 256:512], T.QB[:, 128 * h:128 * h + 128], T.JS[:, 256 * h:256 * h + 256], h == 0, h == 1, [js])
-    r0 = ts(T.R0[:], T.MOD16[:], 0.0, None, OP.not_equal)
+    r0 = ts(T.R0[:], T.MOD16[:, 0:128], 0.0, None, OP.not_equal)
     flu = cp(T.FL[:], T.P7[:, 64:80], [fl])
     mask = ts(T.MASK[:], T.P0[:, 256:512], T.PF[:, 2:3], None, OP.is_equal, toks=[mk])
     ot0 = ms(T.OT[:], 0.0)
 
-    arr = [("rH%d" % q, NE) for q in range(n_ranks) if q != me] + [("rA%d" % q, NE) for q in range(n_ranks) if (q + 1) % n_ranks != me]
-    ls = tt(T.LS[:], T.LANDH[:], T.LANDA[:], OP.add, arr + [ownh, owna])
+    arr = [("rA%d" % r, NE) for r in others] + [own]
+    tt(T.LS[:, 0:24], T.LAND[:, 0:48:2], T.LAND[:, 17:64:2], OP.add, arr)
+    ls = tt(T.LS[:, 24:32], T.LAND[:, 48:64:2], T.LAND[:, 1:16:2], OP.add)
     wn = tr(T.WIN[:], T.LS[:], [ls])
     gm = run("v", lambda: vec.tensor_tensor(T.GM[:], T.WIN[:, 0:32].indirect(T.FL[:]), T.MASK[:], OP.mult), [wn, flu, mask])
     t2 = tr(T.TR[:], T.GM[:], [gm])

@@ -2,9 +2,10 @@ from concourse.bass import DstId, RemoteDMATransfer
 from concourse.mybir import AluOpType, AxisListType, ActivationFunctionType
 
 V = 6144
-W = 6152
+W = 6160
 KEYS = 4096
-SEL = {"SVP": 0, "SHD": 1, "H2": 2, "H1": 3, "HIT": 4, "SAP": 5}
+INC = 1179648.0
+TYP = {"P": 0, "HD": 1, "VT": 2, "AT": 3, "AP": 4}
 
 _f, _b, _i, _u = "float32", "bfloat16", "int32", "uint16"
 
@@ -14,27 +15,27 @@ def _bufs():
 
     def sb(name, n, t):
         s[name] = ("sbuf", [128, n], t)
-    sb("WP", W, _b); sb("WV", W, _f); sb("Z", 1024, _b)
+    sb("WA", W, _b); sb("WB", W, _b); sb("WV", W, _f); sb("Z8", 16, _b); sb("S0", 384, _b)
     sb("HC", 256, _i); sb("VC", 384, _i); sb("AC", 384, _i); sb("VTC", 384, _i); sb("ATC", 384, _i)
     sb("HHI", 256, _b); sb("HLO", 256, _b); sb("VHI", 384, _b); sb("VLO", 384, _b); sb("AHI", 384, _b); sb("ALO", 384, _b)
-    sb("VTF", 384, _f); sb("ATF", 384, _f)
-    sb("I128", 128, _b); sb("I256", 256, _b); sb("ZI", 128, _b); sb("MOD16", 192, _b); sb("XB", 128, _b); sb("OFF", 8, _b)
-    sb("PC", 1, _i); sb("PAT", 8, _i)
-    sb("PATI", 8, _i); sb("X", 128, _i); sb("XH", 128, _i); sb("C1", 192, _f); sb("C", 192, _f)
-    sb("US", 128, _b); sb("UI", 128, _b); sb("IB", 128, _b); sb("IF", 128, _f); sb("S", 768, _b); sb("IND", 128, _b)
-    sb("PINT", 8, _i); sb("COL", 12, _f); sb("EV1", 4, _f)
-    sb("RK", 2, _i); sb("RT", 2, _i); sb("OWNI", 2, _i); sb("OWNF", 2, _f); sb("KI", 4, _i); sb("KF", 4, _f); sb("TF", 2, _f)
-    sb("O", 8, _b); sb("PR", 8, _f); sb("WI", 2, _i); sb("AB", 4, _i); sb("ABF", 4, _f); sb("LH", 256, _b); sb("RH", 128, _b)
-    sb("LSTU", 32, _u); sb("SI", 2, _i); sb("SF", 2, _f); sb("SH", 256, _f); sb("RTT", 16, _f); sb("TS", 8, _f)
+    for x in ("VT", "AT"):
+        for k in range(3):
+            sb("%s%d" % (x, k), 384, _b)
+    sb("I128", 128, _b); sb("I256", 256, _b); sb("ZI", 128, _b); sb("MOD16", 128, _b); sb("MOD8", 192, _b); sb("OFF", 8, _b)
+    sb("XQ", 256, _b); sb("AQ", 256, _b); sb("PC", 1, _i); sb("C1", 192, _f); sb("C", 192, _f)
+    sb("US", 128, _b); sb("UI", 128, _b); sb("IB", 128, _b); sb("S", 1280, _b); sb("RW", 8, _f)
+    sb("PINT", 8, _i); sb("COL", 4, _f); sb("EV", 4, _f)
+    sb("RK", 2, _i); sb("RT", 2, _i); sb("OWNI", 2, _i); sb("OWNF", 2, _f); sb("KI", 2, _i); sb("KF", 2, _f); sb("TF", 2, _f)
+    sb("O", 8, _b); sb("PR", 8, _f); sb("WI", 2, _i); sb("AB", 4, _i); sb("ABF", 4, _f); sb("LHF", 256, _f); sb("RHF", 128, _f)
+    sb("LSTU", 32, _u); sb("TLF", 40, _f)
     for r in range(4):
-        sb("LI%d" % r, 6, _u); sb("TC%d" % r, 2, _f)
-    sb("G", 384 * 7, _b); sb("SC", 384 * 9, _f); sb("L", 24 * 9, _u); sb("N", 24 * 4, _f); sb("E0", 24, _f); sb("E1", 24, _f)
-    sb("M0", 24, _u); sb("ALV", 24, _f); sb("ALS", 24, _f)
-    sb("TB", 512, _f); sb("TH", 384, _f); sb("HIT", 384 * 7, _b)
-    sb("HN", 72, _f); sb("HD", 48, _f); sb("HI", 48, _f); sb("HP", 48, _f); sb("HX", 24, _f)
-    sb("HV", 384, _f); sb("HT", 384, _f); sb("PK", 56, _f)
-    sb("MF", 120, _f); sb("AI", 120, _f); sb("AP", 96, _f); sb("AX", 48, _f); sb("AY", 24, _f); sb("AZ", 24, _f)
-    sb("D4", 24, _f); sb("AQ", 24, _f); sb("AW", 24, _f); sb("AV", 384, _f); sb("AT", 384, _f)
+        sb("LI%d" % r, 6, _u); sb("TC%d" % r, 14, _f)
+    sb("TOC", 24, _f); sb("TAC", 24, _f)
+    sb("G", 384 * 10, _b); sb("SC", 192 * 14, _f); sb("L", 24 * 9, _u); sb("N", 72, _f); sb("E0", 24, _f); sb("E1", 24, _f)
+    sb("M0", 24, _u); sb("DWS", 24, _b); sb("DW", 24, _b)
+    sb("HN", 168, _f); sb("HIT", 168, _f); sb("CD", 168, _f); sb("ACC", 144, _f); sb("ACI", 48, _i); sb("SEL", 48, _i)
+    sb("NON", 24, _f); sb("HX", 48, _f); sb("HY", 48, _f); sb("FM", 48, _f); sb("FS", 48, _f); sb("FC", 48, _f)
+    sb("HV", 384, _f); sb("HT", 384, _f); sb("PK", 56, _f); sb("AV", 384, _f); sb("AVT", 384, _f)
     sb("LAND", 64, _f); sb("LS", 32, _f); sb("WIN", 32, _f)
     sb("FI", 4, _i); sb("FF", 4, _f); sb("FR", 32, _b); sb("C8", 128, _b); sb("FL", 16, _u); sb("QB", 256, _b); sb("JS", 512, _b)
     sb("PF", 8, _f); sb("MASK", 256, _f); sb("R0", 128, _f)
@@ -45,15 +46,16 @@ def _bufs():
 
 
 SCRATCH = _bufs()
-LOADS = ["rk", "rt", "hd", "vp", "ap", "vt", "at", "hh", "hl", "vh", "vl", "ah", "al", "vv", "av", "vtr", "atr", "y0", "y1", "y2", "y3"]
+LOADS = ["rk", "rt", "hd", "vp", "ap", "vt", "at", "hh", "hl", "vh", "vl", "ah", "al", "VT0", "VT1", "VT2", "AT0", "AT1", "AT2",
+         "vv", "av", "y0", "y1", "y2", "y3"]
 SEMAPHORES = (["sv", "ss", "st", "sg"] + ["d_" + x for x in LOADS]
               + ["r%s%d" % (k, r) for k in "LTA" for r in range(4)] + ["rM", "rAL"]
               + ["xL", "xT", "xM", "xAL", "xA"])
 NE = 4
 NS = 8
-VP = (1024, 1536, 2048)
-GV = (1152, 1920)
-SV = 5632
+FA = (768, 1536)
+GB, VB = (0, 384, 768), 3072
+GW = (0, 640, 1280, 1920, 2560, 3200, 3840)
 
 
 def rank_program(g, core, T, topo):
@@ -108,6 +110,9 @@ def rank_program(g, core, T, topo):
     def ms(ap, c, toks=()):
         return run("v", lambda: vec.memset(ap, c), toks)
 
+    def tscan(out, d0, d1, op0, op1, toks=()):
+        return run("v", lambda: vec.tensor_tensor_scan(out, d0, d1, 0.0, op0, op1), toks)
+
     def mm(out, l, r, start, stop, toks=()):
         return run("t", lambda: pe.matmul(out, l, r, start, stop), toks)
 
@@ -150,56 +155,56 @@ def rank_program(g, core, T, topo):
     d_at = dma("y", T.ATC[:], T.at[:], "at")
 
     c_pc = iota(T.PC[:], [[0, 1]], 0, 1, flag=False)
-    c_x = iota(T.X[:], [[-16, 8], [0, 16]], 0, 1, flag=False)
     c_zi = iota(T.ZI[:], [[1, 128]], 0, -1)
     c_i = iota(T.I128[:], [[1, 128]], 0, 0)
     c_off = iota(T.OFF[:], [[0, 2], [128, 4]], 0, 0)
-    c_mod = iota(T.MOD16[:], [[0, 12], [1, 16]], 0, 0)
-    c_pat = iota(T.PAT[:], [[1, 4], [-1, 2]], 0, 0, flag=False)
-    c_xb = iota(T.XB[:], [[-16, 8], [0, 16]], 0, 1)
-    wpf, vfill = [], []
+    c_xq = [iota(T.XQ[:, 128 * q:128 * q + 128], [[-16, 8], [0, 8], [512 - 1024 * q, 2]], 512 * q, 1) for q in range(2)]
+    c_m16 = iota(T.MOD16[:], [[0, 8], [1, 16]], 0, 0)
+    c_m8 = iota(T.MOD8[:], [[0, 24], [1, 8]], 0, 0)
 
-    def zeros_g(win, l, a, b):
-        l.append(iota(win[:, a:b], [[0, b - a]], 0, 0))
+    fa, fb, fv = [], [], []
+    tk, gpos, spos = {}, [0], [0]
+    gjobs = [(w, l, c[i], c[i + 1]) for w, l, c in ((T.WB, fb, GB), (T.WV, fv, GW)) for i in range(len(c) - 1)]
+    sjobs = []
+    for win, lst, a, step_ in ((T.WA, fa, FA[1], 768), (T.WB, fb, VB, 384), (T.WV, fv, GW[-1], 384)):
+        while a < V:
+            n = min(step_, V - a)
+            sjobs.append((win, lst, a, n))
+            a += n
 
-    def zeros_s(win, l, a, b):
-        for i in range(a, b, 1024):
-            n = min(1024, b - i)
-            l.append(copy_s(win[:, i:i + n], T.Z[:, 0:n], [z]))
+    def gfill(n):
+        for _ in range(n):
+            if gpos[0] < len(gjobs):
+                win, lst, a, b = gjobs[gpos[0]]
+                lst.append(iota(win[:, a:b], [[0, b - a]], 0, 0))
+                gpos[0] += 1
 
-    zeros_g(T.WV, vfill, 0, GV[0])
+    def sfill(n):
+        for _ in range(n):
+            if spos[0] < len(sjobs):
+                win, lst, a, k = sjobs[spos[0]]
+                if win is T.WA:
+                    lst.append(copy_s(win[:, a:a + k], T.WA[:, 0:k], [z]))
+                else:
+                    lst.append(copy_s(win[:, a:a + k], T.S0[:, 0:k], [s0]))
+                spos[0] += 1
 
-    z = ms(T.Z[:], 0.0)
-    zeros_s(T.WP, wpf, VP[2], V)
-    zeros_s(T.WV, vfill, GV[1], SV)
-    pint = ts(T.PINT[:, 0:1], T.PC[:], 15, None, OP.bitwise_and, toks=[c_pc])
-    ev = ts(T.PINT[:, 1:2], T.PC[:], 1, None, OP.bitwise_and)
-    col = ts(T.COL[:, 0:1], T.PINT[:, 0:1], -16384.0, 245760.0, OP.mult, OP.add, toks=[pint])
-    e1 = ts(T.EV1[:, 0:1], T.PINT[:, 1:2], 0.0, 6144.0, OP.is_equal, OP.mult, toks=[ev])
-    e2 = ts(T.EV1[:, 1:2], T.PINT[:, 1:2], 0.0, 1048576.0, OP.is_equal, OP.mult)
-    p16 = cp(T.COL[:, 3:4], T.PINT[:, 0:1])
-    wpf.append(ms(T.WP[:, 0:VP[0]], 0.0))
-    w1 = ts(T.WP[:, V:W], T.Z[:, 0:8], T.EV1[:, 0:1], None, OP.add, toks=[e1])
-    w2 = ts(T.WV[:, V:W], T.Z[:, 0:8], T.EV1[:, 1:2], None, OP.add, toks=[e2])
-    smat = {}
-
-    def S(name):
-        return T.S[:, 128 * SEL[name]:128 * SEL[name] + 128]
-
-    def weight(name, src, v, wgt=None, toks=()):
-        if wgt is None:
-            smat[name] = ts(S(name), src[:], v, None, OP.is_equal, toks=toks)
-        else:
-            smat[name] = ts(S(name), src[:], v, wgt, OP.is_equal, OP.mult, toks=toks)
+    z = ms(T.WA[:, 0:FA[0]], 0.0)
+    fa.append(z)
+    sfill(sum(1 for j in sjobs if j[0] is T.WA))
 
     us = ts(T.US[:], T.ZI[:], 0.0, None, OP.is_gt, toks=[c_zi])
     ui = ts(T.UI[:], T.ZI[:], 0.0, None, OP.is_ge)
     ib = ts(T.IB[:], T.ZI[:], 0.0, None, OP.is_equal)
     owni = ts(T.OWNI[:], T.RK[:], 12, None, OP.arith_shift_right, toks=[d_rk])
-    k1 = ts(T.KI[:, 0:2], T.RK[:], 4032, None, OP.bitwise_and)
-    k2 = ts(T.KI[:, 2:4], T.RK[:], 63, None, OP.bitwise_and)
+    k1 = ts(T.KI[:], T.RK[:], 4095, None, OP.bitwise_and)
+    ts(T.PINT[:, 0:1], T.PC[:], 15, None, OP.bitwise_and, toks=[c_pc])
+    for k in (1, 2):
+        ts(T.PINT[:, k:k + 1], T.PC[:], 15, k, OP.bitwise_and, OP.arith_shift_right)
     ownf = cp(T.OWNF[:], T.OWNI[:], [owni])
-    kf = cp(T.KF[:], T.KI[:], [k2])
+    kf = cp(T.KF[:], T.KI[:], [k1])
+    pi = ts(T.PINT[:, 3:4], T.PC[:], 3, None, OP.bitwise_and)
+    ts(T.PINT[:, 4:5], T.PC[:], 7, None, OP.bitwise_and)
     o0 = ts(T.O[:, 0:4], T.I128[:, 0:4], T.OWNF[:, 0:1], None, OP.is_equal, toks=[ownf, c_i])
     o1 = ts(T.O[:, 4:8], T.I128[:, 0:4], T.OWNF[:, 1:2], None, OP.is_equal)
     p, q = T.P0[:, 0:4], T.P1[:, 0:4]
@@ -209,278 +214,347 @@ def rank_program(g, core, T, topo):
     mm(q, T.UI[:], T.O[:, 0:4], False, False)
     mm(p, T.US[:], T.O[:, 4:8], False, True, [o1])
     pos = mm(q, T.US[:], T.O[:, 4:8], False, True)
-    wpf.append(ms(T.WP[:, VP[0]:VP[1]], 0.0))
+    ts(T.EV[:, 0:1], T.PINT[:, 3:4], 0.0, 6144.0, OP.is_equal, OP.mult, toks=[pi])
+    e3 = ts(T.EV[:, 1:2], T.PINT[:, 3:4], 3.0, 1048576.0, OP.is_equal, OP.mult)
+    tf = cp(T.TF[:], T.RT[:], [d_rt])
+    col = ts(T.COL[:, 0:1], T.PINT[:, 1:2], -INC, 7 * INC, OP.mult, OP.add)
+    p8 = cp(T.COL[:, 3:4], T.PINT[:, 1:2])
+    s0 = ms(T.S0[:], 0.0)
+    fa.append(ms(T.WA[:, FA[0]:FA[1]], 0.0))
+    smat = {}
+
+    def S(name, q):
+        k = 128 * (2 * TYP[name] + q)
+        return T.S[:, k:k + 128]
+
+    def weight(name):
+        for q in range(2):
+            smat[name] = ts(S(name, q), T.AQ[:, 128 * q:128 * q + 128], 8.0, T.RW[:, TYP[name]:TYP[name] + 1], OP.is_le, OP.mult, toks=[rw, aq[1]])
+
     tt(T.PR[:, 0:4], T.P0[:, 0:4], T.O[:, 0:4], OP.mult, [pos, o1])
     pr = tt(T.PR[:, 4:8], T.P1[:, 0:4], T.O[:, 4:8], OP.mult)
-    xh = ts(T.XH[:], T.X[:], 1, None, OP.arith_shift_right, toks=[c_x])
     run("v", lambda: vec.tensor_reduce(T.WI[:, 0:1], T.PR[:, 0:4], X, OP.max), [pr])
     wi = run("v", lambda: vec.tensor_reduce(T.WI[:, 1:2], T.PR[:, 4:8], X, OP.max))
-    weight("SVP", T.XH, 0.0, toks=[xh])
     ts(T.AB[:, 0:2], T.WI[:], 15, None, OP.bitwise_and, toks=[wi])
     ab = ts(T.AB[:, 2:4], T.WI[:], 4, None, OP.arith_shift_right)
-    weight("SHD", T.XH, 1.0)
-    abf = cp(T.ABF[:], T.AB[:], [ab])
-    weight("SAP", T.XH, 2.0)
-    lt = []
+    for k, (src, v) in enumerate(((1, 0.0), (1, 1.0), (2, 1.0), (2, 2.0), (1, 6.0))):
+        rw = ts(T.RW[:, k:k + 1], T.PINT[:, src:src + 1], v, None, OP.is_equal)
+        if k == 3:
+            abf = cp(T.ABF[:], T.AB[:], [ab])
+    c1 = ts(T.C1[:], T.MOD8[:], T.COL[:, 3:4], -16000000.0, OP.is_equal, OP.mult, toks=[p8, c_m8])
+    z8 = ms(T.Z8[:], 0.0)
+    eb = tt(T.EV[:, 2:3], T.EV[:, 0:1], T.EV[:, 1:2], OP.add, [e3])
     for h in range(2):
-        ts(T.LH[:, 128 * h:128 * h + 128], T.MOD16[:, 0:128], T.ABF[:, h:h + 1], None, OP.is_equal, toks=[abf, c_mod, kf])
-        for e in range(2):
+        for e, val in ((0, T.KF), (1, T.TF)):
             k = 64 * h + 32 * e
-            lt.append(ts(T.RH[:, k:k + 32], T.I128[:, 0:32], T.ABF[:, 2 + h:3 + h], T.KF[:, 2 * e + h:2 * e + h + 1],
-                         OP.is_equal, OP.mult))
-    for i in range(4):
-        h = i // 2
-        lst = mm(T.P7[:, 0:32], T.LH[:, 128 * h:128 * h + 128], T.RH[:, 32 * i:32 * i + 32], i == 0, i == 3, [lt[i]])
-    wpf.append(ms(T.WP[:, VP[1]:VP[2]], 0.0))
-    lu = cp(T.LSTU[:], T.P7[:, 0:32], [lst])
-    wait("g", [lu])
-    fused([(d, T.LSTU[:, 8 * d:8 * d + 6], T["LI%d" % me][:]) for d in others], "rL%d" % me, "xL")
-
+            ts(T.RHF[:, k:k + 32], T.I128[:, 0:32], T.ABF[:, 2 + h:3 + h], val[:, h:h + 1], OP.is_equal, OP.mult, toks=[abf, kf, tf])
+        lt = ts(T.LHF[:, 128 * h:128 * h + 128], T.MOD16[:], T.ABF[:, h:h + 1], None, OP.is_equal, toks=[c_m16])
+        lst = mm(T.P7[:, 0:64], T.LHF[:, 128 * h:128 * h + 128], T.RHF[:, 64 * h:64 * h + 64], h == 0, h == 1, [lt])
     hh = cp(T.HHI[:], T.HC[:], [d_hd])
     th_ = mm(T.P4[:, 0:256], T.IB[:], T.HHI[:], True, True, [hh])
-    d_hh = dma("y", T.WP[2:128:16, 0:KEYS], T.HHI[:], "hh", [hh] + wpf)
     vh = cp(T.VHI[:], T.VC[:], [d_vp])
     tv_ = mm(T.P5[:, 0:384], T.IB[:], T.VHI[:], True, True, [vh])
-    d_vh = dma("y", T.WP[0:128:16, 0:V], T.VHI[:], "vh", [vh])
-    ah = cp(T.AHI[:], T.AC[:], [d_ap])
-    tah = mm(T.P6[:, 0:384], T.IB[:], T.AHI[:], True, True, [ah])
-    d_ah = dma("y", T.WP[4:128:16, 0:V], T.AHI[:], "ah", [ah])
+    fa.append(ts(T.WA[:, V:W], T.Z8[:], T.EV[:, 2:3], None, OP.add, toks=[eb, z8]))
+    d_hh = dma("y", T.WA[2:128:16, 0:KEYS], T.HHI[:], "hh", [hh] + fa)
+    d_vh = dma("y", T.WA[0:128:16, 0:V], T.VHI[:], "vh", [vh])
+    lu = cp(T.LSTU[:], T.P7[:, 0:32], [lst])
+    tl0 = cp(T.TLF[:, 8:40], T.P7[:, 32:64])
+    tl1 = cp(T.TLF[:, 0:8], T.P7[:, 56:64])
     hl = tt(T.HLO[:], T.HC[:], T.P4[:, 0:256], OP.subtract, [th_])
-    d_hl = dma("y", T.WP[3:128:16, 0:KEYS], T.HLO[:], "hl", [hl])
+    d_hl = dma("y", T.WA[3:128:16, 0:KEYS], T.HLO[:], "hl", [hl])
     vl = tt(T.VLO[:], T.VC[:], T.P5[:, 0:384], OP.subtract, [tv_])
-    d_vl = dma("y", T.WP[1:128:16, 0:V], T.VLO[:], "vl", [vl])
+    d_vl = dma("y", T.WA[1:128:16, 0:V], T.VLO[:], "vl", [vl])
+    WAT = fa + [d_hh, d_hl, d_vh, d_vl]
+    tk["c256"] = iota(T.I256[:], [[1, 256]], 0, 0)
+    gfill(1)
+    wait("g", [lu])
+    fused([(d, T.LSTU[:, 8 * d:8 * d + 6], T["LI%d" % me][:]) for d in others], "rL%d" % me, "xL")
+    wait("g", [tl1])
+    fused([(d, T.TLF[:, 8 * d:8 * d + 14], T["TC%d" % me][:]) for d in others], "rT%d" % me, "xT")
+    gfill(5)
+    aq = [run("s", lambda q=q: act.activation(T.AQ[:, 128 * q:128 * q + 128], T.XQ[:, 128 * q:128 * q + 128], ACT.Abs, bias=-7.5), [c_xq[q]])
+          for q in range(2)]
+    cc = run("s", lambda: act.activation(T.C[:], T.C1[:], ACT.Copy, bias=INC), [c1])
+    weight("HD")
+    sfill(7)
+    weight("P")
+    ts(T.COL[:, 1:2], T.COL[:, 0:1], 6144.0, None, OP.add, toks=[col])
+    cp2 = ts(T.COL[:, 2:3], T.COL[:, 0:1], 12288.0, None, OP.add)
+    fb.append(ts(T.WB[:, V:W], T.Z8[:], T.EV[:, 2:3], None, OP.add))
+    tk["wv"] = ms(T.WV[:, V:W], 0.0)
+    for k, (m, s) in ((5, (127, 3)), (6, (31, 1))):
+        ts(T.PINT[:, k:k + 1], T.PC[:], m, s, OP.bitwise_and, OP.arith_shift_right)
 
-    ts(T.SI[:], T.WI[:], 127, None, OP.bitwise_and)
-    tf = cp(T.TF[:], T.RT[:], [d_rt])
-    pati = ts(T.PATI[:], T.PAT[:], 3, None, OP.bitwise_and, toks=[c_pat])
-    sf = cp(T.SF[:], T.SI[:], [tf])
-    tl = []
+    big, bg, wbt, WBT = [], [], [], []
+
+    def conv(fn, name, row, src):
+        t = fn()
+        tk[name] = t
+        wbt.append((name, row, src, t))
+
+    def aph():
+        conv(lambda: cp(T.AHI[:], T.AC[:], [d_ap]), "ah", 12, T.AHI)
+        tk["map"] = mm(T.P6[:, 0:384], T.IB[:], T.AHI[:], True, True, [tk["ah"]])
+
+    def first(x, src, bank, d, row):
+        conv(lambda: cp(T[x + "0"][:], src[:], [d]), x + "0", row, T[x + "0"])
+        tk["m" + x] = mm(bank[:, 0:384], T.IB[:], T[x + "0"][:], True, True, [tk[x + "0"], hl, vl])
+
+    def mid(x, src, bank, row):
+        conv(lambda: tt(T[x + "1"][:], src[:], bank[:, 0:384], OP.subtract, [tk["m" + x]]), x + "1", row + 1, T[x + "1"])
+        mm(bank[:, 0:384], T.IB[:], T[x + "0"][:], True, False, [tk[x + "1"]])
+        tk["n" + x] = mm(bank[:, 0:384], T.IB[:], T[x + "1"][:], False, True)
+
+    def last(x, src, bank, row):
+        conv(lambda: tt(T[x + "2"][:], src[:], bank[:, 0:384], OP.subtract, [tk["n" + x]]), x + "2", row + 2, T[x + "2"])
+
+    big += [aph, lambda: first("AT", T.ATC, T.P5, d_at, 8),
+            lambda: conv(lambda: tt(T.ALO[:], T.AC[:], T.P6[:, 0:384], OP.subtract, [tk["map"]]), "al", 13, T.ALO),
+            lambda: first("VT", T.VTC, T.P4, d_vt, 4), lambda: mid("AT", T.ATC, T.P5, 8), lambda: mid("VT", T.VTC, T.P4, 4),
+            lambda: last("AT", T.ATC, T.P5, 8), lambda: last("VT", T.VTC, T.P4, 4)]
+    for x in ("AP", "AT", "VT"):
+        bg.append(lambda x=x: weight(x))
+
+    def tadd(buf, r, off):
+        src = T.TLF[:, 8 * me + off:8 * me + off + 6] if r == me else T["TC%d" % r][:, off:off + 6]
+        tk["TO" if off else "TA"] = ts(buf[:, 6 * r:6 * r + 6], src, T.COL[:, 0:1], None, OP.add, toks=[tl1 if r == me else ("rT%d" % r, NE), col])
+    for off in (8, 0):
+        for r in [me] + others:
+            bg.append(lambda r=r, off=off: tadd(T.TOC if off else T.TAC, r, off))
+    bg.append(lambda: tk.update(fm0=ms(T.FM[:], 0.0)))
+    bg.append(lambda: tk.update(pk0=ms(T.PK[:, 48:56], 0.0)))
+    bg.append(lambda: ts(T.FI[:, 0:2], T.WI[:], 31, None, OP.bitwise_and))
+    bg.append(lambda: tk.update(fi=ts(T.FI[:, 2:4], T.WI[:], 5, None, OP.arith_shift_right)))
+    bg.append(lambda: tk.update(pf=cp(T.PF[:, 0:3], T.PINT[:, 4:7])))
+    bg.append(lambda: tk.update(ff=cp(T.FF[:], T.FI[:], [tk["fi"]])))
+    bg.append(lambda: ts(T.PF[:, 3:4], T.PF[:, 0:1], 2.0, None, OP.mult, toks=[tk["pf"]]))
+    bg.append(lambda: ts(T.PF[:, 4:5], T.PF[:, 0:1], 2.0, 1.0, OP.mult, OP.add))
+    bg.append(lambda: tk.update(p5=ts(T.PF[:, 5:6], T.PF[:, 0:1], 32.0, T.PF[:, 1:2], OP.mult, OP.add)))
+    bg.append(lambda: ts(T.C8[:], T.MOD16[:], T.PF[:, 1:2], None, OP.is_equal))
+    bg.append(lambda: tk.update(p6=ts(T.PF[:, 6:7], T.PF[:, 5:6], 16.0, None, OP.add, toks=[tk["p5"]])))
     for h in range(2):
-        ts(T.SH[:, 128 * h:128 * h + 128], T.I128[:], T.SF[:, h:h + 1], None, OP.is_equal, toks=[sf, pati])
-        tl.append(ts(T.RTT[:, 8 * h:8 * h + 8], T.PATI[:], T.OWNF[:, h:h + 1], T.TF[:, h:h + 1], OP.is_equal, OP.mult))
-    mm(T.P0[:, 16:24], T.SH[:, 0:128], T.RTT[:, 0:8], True, False, [tl[0], pr])
-    tm = mm(T.P0[:, 16:24], T.SH[:, 128:256], T.RTT[:, 8:16], False, True, [tl[1]])
-    al = tt(T.ALO[:], T.AC[:], T.P6[:, 0:384], OP.subtract, [tah])
-    d_al = dma("y", T.WP[5:128:16, 0:V], T.ALO[:], "al", [al])
-    tsa = cp(T.TS[:, 0:8:2], T.P0[:, 16:24:2], [tm])
-    ts_tok = tt(T.TS[:, 1:8:2], T.P0[:, 17:24:2], T.TS[:, 0:8:2], OP.subtract, [tsa])
-    wait("g", [ts_tok])
-    fused([(d, T.TS[:, 2 * d:2 * d + 2], T["TC%d" % me][:]) for d in others], "rT%d" % me, "xT")
+        bg.append(lambda h=h: tk.update(fr=ts(T.FR[:, 16 * h:16 * h + 16], T.I128[:, 0:16], T.PF[:, 3 + h:4 + h], T.FF[:, h:h + 1],
+                                              OP.is_equal, OP.mult, toks=[tk["p6"], tk["ff"]])))
+    for h in range(2):
+        bg.append(lambda h=h: ts(T.QB[:, 128 * h:128 * h + 128], T.I128[:], 0.0, T.FF[:, 2 + h:3 + h], OP.mult, OP.add))
+        bg.append(lambda h=h: tk.update(js=ts(T.JS[:, 256 * h:256 * h + 256], T.I256[:], T.PF[:, 5 + h:6 + h], None, OP.is_equal, toks=[tk["c256"]])))
 
-    c1 = ts(T.C1[:], T.MOD16[:], T.COL[:, 3:4], -524288.0, OP.is_equal, OP.mult, toks=[p16, c_xb])
-    ind = ts(T.IND[:], T.MOD16[:, 0:128], 2.0, None, OP.is_equal)
-    idf = ts(T.IF[:], T.ZI[:], 0.0, None, OP.is_equal)
-    cc = ts(T.C[:], T.C1[:], 16384.0, None, OP.add, toks=[c1])
-    vfill.append(ms(T.WV[:, SV:V], 0.0))
-    tv = cp(T.VTF[:], T.VTC[:], [d_vt])
-    ta_ = cp(T.ATF[:], T.ATC[:], [d_at])
-    zeros_g(T.WV, vfill, GV[0], GV[1])
+    def place():
+        for h in range(2):
+            tk["fl"] = mm(T.P7[:, 64:80], T.C8[:], T.FR[:, 16 * h:16 * h + 16], h == 0, h == 1, [tk["fr"], tl1])
+        for h in range(2):
+            tk["mk"] = mm(T.P0[:, 256:512], T.QB[:, 128 * h:128 * h + 128], T.JS[:, 256 * h:256 * h + 256], h == 0, h == 1, [tk["js"], pr])
+        tk["r0"] = ts(T.R0[:], T.MOD16[:], 0.0, None, OP.not_equal)
+    bg.append(place)
+    bg.append(lambda: tk.update(ot0=ms(T.OT[:], 0.0)))
+    bg.append(lambda: tk.update(flu=cp(T.FL[:], T.P7[:, 64:80], [tk["fl"]])))
+    bg.append(lambda: tk.update(mask=ts(T.MASK[:], T.P0[:, 256:512], T.PF[:, 2:3], None, OP.is_equal, toks=[tk["mk"]])))
 
-    WPT = wpf + [w1, d_hh, d_hl, d_vh, d_vl, d_ah, d_al]
-    banks = [T.P2[:, 0:192], T.P3[:, 0:192]]
-    codes = [T.P4[:, 0:192], T.P5[:, 0:192]]
+    def pop(jobs, n):
+        for _ in range(n):
+            if jobs:
+                jobs.pop(0)()
 
-    def G(i, half):
-        return T.G[:, 384 * i + 192 * half:384 * i + 192 * half + 192]
+    def land():
+        while wbt:
+            name, row, src, t = wbt.pop(0)
+            WBT.append(dma("y", T.WB[row:128:16, 0:V], src[:], name, [t] + fb))
+
+    banks = [T.P2, T.P3]
+
+    def gather(i, h, win, lst, toks, who="s"):
+        o = 384 * i + 192 * h
+        if who == "s":
+            return copy_s(T.G[:, o:o + 192], win.indirect(lst), toks)
+        return cp(T.G[:, o:o + 192], win.indirect(lst), toks)
+
+    def spread(bank, c, name, i, h, toks):
+        o = 384 * i + 192 * h
+        for q in range(2):
+            t = mm(bank[:, c:c + 96], S(name, q), T.G[:, o + q:o + 192:2], q == 0, q == 1, toks + [smat[name]])
+        return t
 
     def Ls(i, half):
         return T.L[:, 24 * i + 12 * half:24 * i + 12 * half + 12]
 
-    def scan(i, half, src, tok):
-        o = 384 * i + 192 * half
-        t = run("v", lambda: vec.tensor_tensor_scan(T.SC[:, o:o + 192], T.C[:], src, 0.0, OP.add, OP.max), [tok, cc])
-        return t, T.SC[:, o + 15:o + 192:16]
+    def scan(i, half, tok):
+        o = 192 * i + 96 * half
+        t = tscan(T.SC[:, o:o + 96], T.C[:, 0:96], banks[half][:, 0:96], OP.add, OP.max, [tok, cc])
+        return t, T.SC[:, o + 7:o + 96:8]
+
+    def scan2(i, src, tok):
+        return tscan(T.SC[:, 192 * i:192 * i + 192], T.C[:], src, OP.add, OP.max, [tok, cc])
 
     def both(i):
-        return T.SC[:, 384 * i + 15:384 * i + 384:16]
+        return T.SC[:, 192 * i + 7:192 * i + 192:8]
 
+    def step(i, m, lst):
+        ks, ls = [], []
+        for h in range(2):
+            t, pick = scan(i, h, m[h])
+            ks.append(t)
+            pop(bg, 1)
+            ls.append(lst(h, t, pick))
+        return ks, ls
+
+    fb.append(ms(T.WB[:, GB[-1]:VB], 0.0))
+    pop(big, 2)
     hg = []
-    for r in [me] + others:
+    for k, r in enumerate([me] + others):
         src = T.LSTU[:, 8 * me:8 * me + 6] if r == me else T["LI%d" % r][:]
         tok = lu if r == me else ("rL%d" % r, NE)
-        hg.append(copy_s(T.G[:, 96 * r:96 * r + 96], T.WP[:, 0:KEYS].indirect(src), WPT + [tok]))
-
-    order, thm = [me] + others, [None] * n_ranks
-    tbank = [T.P1, T.P6]
-
-    def bcast(r):
-        c, tok = (T.TS[:, 2 * me:2 * me + 2], ts_tok) if r == me else (T["TC%d" % r][:], ("rT%d" % r, NE))
-        return run("s", lambda: act.activation(T.TB[:, 128 * r:128 * r + 128], T.IND[:], ACT.Identity, bias=c[:, 0:1], scale=c[:, 1:2]),
-                   [tok, ind])
-
-    def tmm(r, tok):
-        k = 96 * (r % 2)
-        thm[r] = mm(tbank[r // 2][:, k:k + 96], T.TB[:, 128 * r:128 * r + 128], T.IF[:, 0:96], True, True, [tok, idf, pr])
-
-    bt = bcast(me)
-    m = [mm(banks[h], S("SHD"), G(0, h), True, True, [smat["SHD"], hg[-1]]) for h in range(2)]
-    tmm(me, bt)
-    ts(T.COL[:, 1:2], T.COL[:, 0:1], 6144.0, None, OP.add, toks=[col])
-    cp2 = ts(T.COL[:, 2:3], T.COL[:, 0:1], 12288.0, None, OP.add)
-    for k, v in ((4, 1.0), (5, 2.0), (6, 8192.0)):
-        colt = ts(T.COL[:, k:k + 1], T.COL[:, 0:1], v, None, OP.add)
-    ks = [scan(0, h, banks[h], m[h]) for h in range(2)]
-    l0 = [ts(Ls(0, h), ks[h][1], T.COL[:, 0:1], 6144.0, OP.subtract, OP.min, toks=[ks[h][0], col]) for h in range(2)]
-    ga = copy_s(G(1, 0), T.WP[:, 0:W].indirect(Ls(0, 0)), [l0[0]])
-    bt = [bcast(r) for r in others]
-    gb = cp(G(1, 1), T.WP[:, 0:W].indirect(Ls(0, 1)), WPT + [l0[1]])
+        out, inp = T.G[:, 96 * r:96 * r + 96], T.WA[:, 0:KEYS].indirect(src)
+        hg.append(cp(out, inp, WAT + [tok]) if k == 3 else copy_s(out, inp, WAT + [tok]))
+    m = [spread(banks[h], 0, "HD", 0, h, hg) for h in range(2)]
+    sfill(1)
+    pop(big, 2)
+    land()
+    ks, l0 = step(0, m, lambda h, t, pick: ts(Ls(0, h), pick, T.COL[:, 0:1], 6144.0, OP.subtract, OP.min, toks=[t, col]))
+    ga = [gather(1, h, T.WA[:], Ls(0, h), WAT + [l0[h]]) for h in range(2)]
+    m = [spread(banks[h], 0, "P", 1, h, [ga[h], ks[h]]) for h in range(2)]
     a = ts(T.N[:, 0:24], both(0), T.COL[:, 0:1], 6144.0, OP.subtract, OP.max)
-    weight("H2", T.XB, 0.0, 2.0)
-    weight("H1", T.XB, 0.0)
+    pop(big, 2)
     e0 = ts(T.E0[:], T.N[:, 0:24], T.COL[:, 1:2], None, OP.subtract, toks=[a, cp2])
-    m = [mm(banks[0], S("SVP"), G(1, 0), True, True, [ga, ks[0][0]]), mm(banks[1], S("SVP"), G(1, 1), True, True, [gb, ks[1][0]])]
-    tmm(order[1], bt[0])
-    weight("HIT", T.XB, 2.0, 8192.0)
-    ks = [scan(1, h, banks[h], m[h]) for h in range(2)]
-    a = [tt(T.N[:, 24 + 12 * h:36 + 12 * h], ks[h][1], T.E0[:, 12 * h:12 * h + 12], OP.add, [ks[h][0], e0]) for h in range(2)]
-    l1 = [ts(Ls(1, h), T.N[:, 24 + 12 * h:36 + 12 * h], 6144.0, None, OP.min, toks=[a[h]]) for h in range(2)]
-    d_vtr = dma("y", T.WV[0:128:16, 0:V], T.VTF[:], "vtr", [tv] + vfill)
-    d_atr = dma("y", T.WV[2:128:16, 0:V], T.ATF[:], "atr", [ta_])
-    d_vv = dma("y", T.WV[1:128:16, 0:V], T.vv[:], "vv")
-    d_av = dma("y", T.WV[3:128:16, 0:V], T.av[:], "av")
-    WVT = vfill + [w2, d_vtr, d_atr, d_vv, d_av]
-    ga = copy_s(G(2, 0), T.WP[:, 0:W].indirect(Ls(1, 0)), [l1[0]])
-    gb = cp(G(2, 1), T.WP[:, 0:W].indirect(Ls(1, 1)), [l1[1]])
+    land()
+
+    def l1_(h, t, pick):
+        a = tt(T.N[:, 24 + 12 * h:36 + 12 * h], pick, T.E0[:, 12 * h:12 * h + 12], OP.add, [t, e0])
+        pop(bg, 1)
+        return ts(Ls(1, h), T.N[:, 24 + 12 * h:36 + 12 * h], 6144.0, None, OP.min, toks=[a])
+    ks, l1 = step(1, m, l1_)
+    ga = [gather(2, h, T.WA[:], Ls(1, h), [l1[h]]) for h in range(2)]
+    m = [spread(banks[h], 0, "P", 2, h, [ga[h], ks[h]]) for h in range(2)]
     e1v = ts(T.E1[:], T.N[:, 24:48], 6144.0, T.COL[:, 2:3], OP.max, OP.subtract)
-    cp(T.HN[:, 0:24], T.L[:, 0:24], [l0[1]])
-    cp(T.HN[:, 24:48], T.L[:, 24:48], [l1[1]])
-    hc = ms(T.HN[:, 48:72], 6144.0)
-    pk0 = ms(T.PK[:, 48:56], 0.0)
-    m = [mm(banks[0], S("SVP"), G(2, 0), True, True, [ga, ks[0][0]]), mm(banks[1], S("SVP"), G(2, 1), True, True, [gb, ks[1][0]])]
-    for k in (2, 3):
-        tmm(order[k], bt[k - 1])
-    tht = [copy_s(T.TH[:, 192 * h:192 * h + 192], tbank[h][:, 0:192], [thm[2 * h], thm[2 * h + 1]]) for h in range(2)]
-    ks = [scan(2, h, banks[h], m[h]) for h in range(2)]
-    sc2 = [t for t, pk in ks]
-    a = [tt(T.N[:, 48 + 12 * h:60 + 12 * h], ks[h][1], T.E1[:, 12 * h:12 * h + 12], OP.add, [ks[h][0], e1v]) for h in range(2)]
-    l2 = [cp(Ls(3, h), T.N[:, 48 + 12 * h:60 + 12 * h], [a[h]]) for h in range(2)]
+    pop(big, 2)
+    land()
+
+    def l2_(h, t, pick):
+        a = tt(T.N[:, 48 + 12 * h:60 + 12 * h], pick, T.E1[:, 12 * h:12 * h + 12], OP.add, [t, e1v])
+        pop(bg, 1)
+        return cp(Ls(2, h), T.N[:, 48 + 12 * h:60 + 12 * h], [a])
+    prev, l2 = step(2, m, l2_)
     wait("g", l2)
-    send(nxt, T.L[:, 72:96], T.M0[:], "rM", "xM")
-    c_256 = iota(T.I256[:], [[1, 256]], 0, 0)
-    hd_ = tt(T.HD[:], T.HN[:, 0:48], T.HN[:, 24:72], OP.subtract, [hc])
+    send(nxt, T.L[:, 48:72], T.M0[:], "rM", "xM")
+    sfill(99)
+    gfill(99)
+    d_vv = dma("y", T.WV[1:128:16, 0:V], T.vv[:], "vv", fv)
+    d_av = dma("y", T.WV[2:128:16, 0:V], T.av[:], "av", fv)
+    WVT = fv + [d_vv, d_av, tk["wv"]]
+    pop(bg, 12)
+    nn = [ts(T.HN[:, 24 * i:24 * i + 24], T.L[:, 24 * i:24 * i + 24], 8192.0 * (2 - i), None, OP.add) for i in range(2)]
+    pop(bg, 2)
+    st = {}
 
-    def test(i, h, lst, toks):
-        o = 384 * i + 192 * h
-        return run("v", lambda: vec.tensor_tensor(T.HIT[:, o:o + 192], T.WV[:, 0:W].indirect(lst), T.TH[:, 192 * h:192 * h + 192], OP.is_le), toks)
+    def dead():
+        dw = ts(T.DWS[:], T.ACC[:, 0:24], 8192.0, 55296.0, OP.is_ge, OP.mult, toks=[st["ha"]])
+        wait("g", [dw])
+        send(nxt, T.DWS[:], T.DW[:], "rAL", "xAL")
+    hq = [lambda: st.update(x0=tt(T.HIT[:, 0:24], both(7), T.TOC[:], OP.is_le, [st["h0"], tk["TO"]])),
+          lambda: st.update(x1=tt(T.HIT[:, 24:48], both(8), T.TOC[:], OP.is_le, [st["h1"]])),
+          lambda: st.update(c0=tt(T.CD[:, 0:24], T.HIT[:, 0:24], T.HN[:, 0:24], OP.mult, [st["x0"], nn[0]])),
+          lambda: st.update(c1=tt(T.CD[:, 24:48], T.HIT[:, 24:48], T.HN[:, 24:48], OP.mult, [st["x1"], nn[1]])),
+          lambda: st.update(ha=tt(T.ACC[:, 0:24], T.CD[:, 0:24], T.CD[:, 24:48], OP.max, [st["c0"], st["c1"]])),
+          dead,
+          lambda: st.update(hm_=ts(T.ACI[:, 0:24], T.ACC[:, 0:24], 6144.0, None, OP.max)),
+          lambda: st.update(hs_=ts(T.SEL[:, 0:24], T.ACI[:, 0:24], 8191, None, OP.bitwise_and, toks=[st["hm_"]])),
+          lambda: st.update(hl_=cp(T.L[:, 168:192], T.SEL[:, 0:24], [st["hs_"]]))]
 
-    def hitc(i, h):
-        return T.HIT[:, 384 * i + 192 * h:384 * i + 192 * h + 192]
-
-    h0 = [test(0, h, Ls(0, h), WVT + [tht[h]]) for h in range(2)]
-    h1 = [test(1, h, Ls(1, h), []) for h in range(2)]
-    for h in range(2):
-        mm(codes[h], S("H2"), hitc(0, h), True, False, [h0[h], smat["HIT"]])
-    hcode = [mm(codes[h], S("H1"), hitc(1, h), False, True, [h1[h]]) for h in range(2)]
-    hsc = [scan(3, h, codes[h], hcode[h])[0] for h in range(2)]
-    als = ts(T.ALS[:], both(3), T.COL[:, 0:1], None, OP.is_equal, toks=[hsc[1], colt])
-    ts(T.HI[:, 0:24], both(3), T.COL[:, 5:6], None, OP.is_ge)
-    hi = ts(T.HI[:, 24:48], both(3), T.COL[:, 4:5], None, OP.is_ge)
-    wait("g", [als])
-    send(nxt, T.ALS[:], T.ALV[:], "rAL", "xAL")
-
-    def compact(buf, tbuf, row, k, ab):
-        t0 = tr(tbuf[:, 0:192], buf[:, 0:192], [ab[0]])
-        t1 = tr(tbuf[:, 192:384], buf[:, 192:384], [ab[1]])
-        return cp(T.PK[:, k:48:2], tbuf[:, row::16], [t0, t1])
+    def gap(n):
+        for _ in range(n):
+            pop(hq if hq and "h1" in st else bg, 1)
 
     lists = [T.M0[:, 12 * h:12 * h + 12] for h in range(2)]
-    arrived = [("rM", NS), ("rM", NS)]
-    hk = [test(2, h, lists[h], [arrived[h]]) for h in range(2)]
-    hs = {"m": ts(T.MF[:, 0:24], T.M0[:], 6144.0, None, OP.subtract, toks=[arrived[0]])}
-    prev = sc2
-
-    def part(k, j):
-        b = 24 * k
-        if j == 0:
-            if k == 0:
-                hs["p"] = tt(T.HP[:], T.HI[:], T.HD[:], OP.mult, [hi, hd_])
-            else:
-                hs["f"] = ts(T.AI[:, b - 24:b], both(3 + k), T.COL[:, 6:7], None, OP.is_ge)
-        elif j == 1:
-            if k == 0:
-                hs["x"] = tt(T.HX[:], T.HP[:, 0:24], T.HP[:, 24:48], OP.add, [hs["p"]])
-            else:
-                hs["a"] = tt(T.AP[:, b - 24:b], T.AI[:, b - 24:b], T.MF[:, b - 24:b], OP.mult, [hs["f"], hs["m"]])
-        else:
-            if k == 0:
-                hs["s"] = ts(T.L[:, 48:72], T.HX[:], 6144.0, None, OP.add, toks=[hs["x"]])
-            hs["m"] = ts(T.MF[:, b + 24:b + 48], T.L[:, 96 + b:120 + b], 6144.0, None, OP.subtract, toks=[arrived[1]])
-
-    for k in range(4):
-        gk = [copy_s(G(3 + k, h), T.WP[:, 0:W].indirect(lists[h]), [arrived[h]]) for h in range(2)]
+    num = T.M0[:]
+    an = [("rM", NS), ("rM", NS)]
+    dq = []
+    for k in range(5):
+        gk = [gather(5 + k, h, T.WB[:], lists[h], WBT + [an[h]]) for h in range(2)]
         m = []
         for h in range(2):
-            mm(banks[h], S("HIT"), hitc(2 + k, h), True, False, [hk[h], prev[h]])
-            m.append(mm(banks[h], S("SAP"), G(3 + k, h), False, True, [gk[h]]))
-        lists = [Ls(4 + k, h) for h in range(2)]
-        part(k, 0)
-        t0, pk0_ = scan(4 + k, 0, banks[0], m[0])
-        part(k, 1)
-        a0 = ts(lists[0], pk0_, T.COL[:, 0:1], 6144.0, OP.subtract, OP.min, toks=[t0])
-        t1, pk1_ = scan(4 + k, 1, banks[1], m[1])
-        x0 = test(3 + k, 0, lists[0], [a0])
-        a1 = ts(lists[1], pk1_, T.COL[:, 0:1], 6144.0, OP.subtract, OP.min, toks=[t1])
-        arrived, prev = [a0, a1], [t0, t1]
-        part(k, 2)
-        hk = [x0, test(3 + k, 1, lists[1], [a1])]
-    acode = [mm(banks[h], S("HIT"), hitc(6, h), True, True, [hk[h], prev[h]]) for h in range(2)]
-    hv = [copy_s(T.HV[:, 192 * h:192 * h + 192], T.WV[:, 0:W].indirect(Ls(2, h)), WVT + [hs["s"]]) for h in range(2)]
-    part(4, 0)
-    d4 = tt(T.D4[:], T.MF[:, 96:120], T.ALV[:], OP.mult, [hs["m"], ("rAL", NS)])
-    a0 = tt(T.AX[:, 0:24], T.AP[:, 0:24], T.AP[:, 24:48], OP.add, [hs["a"]])
-    part(4, 1)
-    a1 = tt(T.AX[:, 24:48], T.AP[:, 48:72], T.AP[:, 72:96], OP.add, [hs["a"]])
-    a = tt(T.AY[:], T.AX[:, 0:24], T.AX[:, 24:48], OP.add, [a0, a1])
-    asc = [scan(8, 0, banks[0], acode[0])[0]]
-    az = tt(T.AZ[:], T.AY[:], T.ALV[:], OP.mult, [a])
-    asc.append(scan(8, 1, banks[1], acode[1])[0])
-    ai = ts(T.AI[:, 96:120], both(8), T.COL[:, 6:7], None, OP.is_ge, toks=[asc[1]])
-    a = tt(T.AQ[:], T.AI[:, 96:120], T.D4[:], OP.mult, [ai, d4])
-    a = tt(T.AW[:], T.AQ[:], T.AZ[:], OP.add, [a, az])
-    asel = ts(T.L[:, 192:216], T.AW[:], 6144.0, None, OP.add, toks=[a])
-    va = copy_s(T.AV[:, 0:192], T.WV[:, 0:W].indirect(Ls(8, 0)), [asel])
-    vb = cp(T.AV[:, 192:384], T.WV[:, 0:W].indirect(Ls(8, 1)), [asel])
-    ph = compact(T.HV, T.HT, 1, 0, hv)
-    pa = compact(T.AV, T.AT, 3, 1, [va, vb])
-    wait("g", [ph, pa, pk0])
+            if k < 4:
+                m.append(spread(banks[h], 0, "AP", 5 + k, h, [gk[h], prev[h]]))
+            dm = spread(T.P1, 96 * h, "AT", 5 + k, h, [gk[h], st.get("sd", pr)])
+        if k == 0:
+            for i in range(2):
+                for h in range(2):
+                    t = gather(3 + i, h, T.WB[:], Ls(i, h), WBT, ("vv", "sv")[i][h])
+                    hm = spread(T.P6, 192 * i + 96 * h, "VT", 3 + i, h, [t, tk["al"]])
+        if k == 4:
+            break
+        o = 48 + 24 * k
+        if k < 3:
+            ni = ts(T.HN[:, o:o + 24], num, 8192.0 * (4 - k), None, OP.add, toks=an)
+        gap(2 if k < 2 else 1)
+        lists = [Ls(3 + k, h) for h in range(2)]
+        num = T.L[:, 72 + 24 * k:96 + 24 * k]
+        an, prev = [], []
+        for h in range(2):
+            t, pick = scan(3 + k, h, m[h])
+            pop(dq, 1)
+            gap(2 if k == 1 and h == 0 else 1)
+            an.append(ts(lists[h], pick, T.COL[:, 0:1], 6144.0, OP.subtract, OP.min, toks=[t]))
+            prev.append(t)
+        pop(dq, 9)
+        st["sd"] = scan2(9 + k, T.P1[:, 0:192], dm)
+        if k == 0:
+            for i in range(2):
+                st["h%d" % i] = scan2(7 + i, T.P6[:, 192 * i:192 * i + 192], hm)
+        if k > 1:
+            nk = ts(T.HX[:, 24 * k - 48:24 * k - 24], num, -6144.0, None, OP.add, toks=an)
+        if k == 3:
+            q4 = tt(T.HY[:, 0:24], T.NON[:], T.HX[:, 0:24], OP.mult, [st["no"], st["n4"]])
+            q5 = tt(T.HY[:, 24:48], T.NON[:], T.HX[:, 24:48], OP.mult, [nk])
+        else:
+            gap(1)
+        hit = tt(T.HIT[:, o:o + 24], both(9 + k), T.TAC[:], OP.is_le, [st["sd"], tk["TA"]])
+        if k < 3:
+            dq.append(lambda o=o, hit=hit, ni=ni: st.update(c=tt(T.CD[:, o:o + 24], T.HIT[:, o:o + 24], T.HN[:, o:o + 24], OP.mult, [hit, ni])))
+        if k == 0:
+            dq.append(lambda: st.update(acc=ts(T.ACC[:, 24:48], T.CD[:, 48:72], 6144.0, None, OP.max, toks=[st["c"]])))
+        elif k == 1:
+            dq.append(lambda: st.update(acc=tt(T.ACC[:, 48:72], T.ACC[:, 24:48], T.CD[:, 72:96], OP.max, [st["c"], st["acc"]])))
+        elif k == 2:
+            st["n4"] = nk
+            gap(len(hq))
+            a = tt(T.ACC[:, 72:96], T.ACC[:, 48:72], T.DW[:], OP.max, [st["acc"], ("rAL", NS)])
+            pop(dq, 1)
+            gap(1)
+            a = tt(T.ACI[:, 24:48], T.ACC[:, 72:96], T.CD[:, 96:120], OP.max, [a, st["c"]])
+            dq.append(lambda a=a: st.update(no=ts(T.NON[:], T.ACI[:, 24:48], 8192.0, None, OP.is_lt, toks=[a])))
+            dq.append(lambda a=a: st.update(s=ts(T.SEL[:, 24:48], T.ACI[:, 24:48], 8191, None, OP.bitwise_and, toks=[a])))
+        else:
+            x4 = tt(T.CD[:, 120:144], T.HIT[:, 120:144], T.HY[:, 0:24], OP.mult, [hit, q4])
+            r5 = tt(T.CD[:, 144:168], T.HIT[:, 120:144], T.HY[:, 24:48], OP.mult, [q5])
+            gap(2)
+            s4 = tt(T.FS[:, 1:48:2], T.CD[:, 120:144], T.SEL[:, 24:48], OP.add, [x4, st["s"]])
+            m5 = tt(T.FM[:, 1:48:2], T.HY[:, 24:48], T.CD[:, 144:168], OP.subtract, [r5, tk["fm0"]])
+    hv = [copy_s(T.HV[:, 192 * h:192 * h + 192], T.WV[:].indirect(Ls(7, h)), WVT + [st["hl_"]]) for h in range(2)]
+    sd = scan2(13, T.P1[:, 0:192], dm)
+    t0 = tr(T.HT[:, 0:192], T.HV[:, 0:192], [hv[0]])
+    h5 = tt(T.FS[:, 0:48:2], both(13), T.TAC[:], OP.is_le, [sd, m5])
+    t1 = tr(T.HT[:, 192:384], T.HV[:, 192:384], [hv[1]])
+    y5 = tscan(T.FC[:], T.FM[:], T.FS[:], OP.mult, OP.add, [h5, s4])
+    ph = cp(T.PK[:, 0:48:2], T.HT[:, 1::16], [t0, t1])
+    asel = cp(T.L[:, 192:216], T.FC[:, 1:48:2], [y5])
+    va = copy_s(T.AV[:, 0:192], T.WV[:].indirect(Ls(8, 0)), WVT + [asel])
+    vb = cp(T.AV[:, 192:384], T.WV[:].indirect(Ls(8, 1)), WVT + [asel])
+    t1 = tr(T.AVT[:, 192:384], T.AV[:, 192:384], [vb])
+    t0 = tr(T.AVT[:, 0:192], T.AV[:, 0:192], [va])
+    pa = cp(T.PK[:, 1:48:2], T.AVT[:, 2::16], [t0, t1])
+    wait("g", [ph, pa, tk["pk0"]])
     fused([(d, T.PK[:, 12 * d:12 * d + 16], T.LAND[:, 16 * me:16 * me + 16]) for d in others], "rA%d" % me, "xA")
     own = cp(T.LAND[:, 16 * me:16 * me + 16], T.PK[:, 12 * me:12 * me + 16], [ph, pa])
-
-    ts(T.FI[:, 0:2], T.WI[:], 31, None, OP.bitwise_and)
-    fi = ts(T.FI[:, 2:4], T.WI[:], 5, None, OP.arith_shift_right)
-    ts(T.PINT[:, 2:3], T.PC[:], 7, None, OP.bitwise_and)
-    ts(T.PINT[:, 3:4], T.PC[:], 3, None, OP.arith_shift_right)
-    pi = ts(T.PINT[:, 4:5], T.PC[:], 31, 1, OP.bitwise_and, OP.arith_shift_right)
-    ff = cp(T.FF[:], T.FI[:], [fi])
-    pf = cp(T.PF[:, 0:3], T.PINT[:, 2:5], [pi])
-    ts(T.PF[:, 3:4], T.PF[:, 0:1], 2.0, None, OP.mult, toks=[pf])
-    ts(T.PF[:, 4:5], T.PF[:, 0:1], 2.0, 1.0, OP.mult, OP.add)
-    a = ts(T.PF[:, 5:6], T.PF[:, 0:1], 32.0, T.PF[:, 1:2], OP.mult, OP.add)
-    a = ts(T.PF[:, 6:7], T.PF[:, 5:6], 16.0, None, OP.add, toks=[a, ff])
-    ts(T.C8[:], T.MOD16[:, 0:128], T.PF[:, 1:2], None, OP.is_equal, toks=[a])
-    for h in range(2):
-        fr = ts(T.FR[:, 16 * h:16 * h + 16], T.I128[:, 0:16], T.PF[:, 3 + h:4 + h], T.FF[:, h:h + 1], OP.is_equal, OP.mult)
-    for h in range(2):
-        fl = mm(T.P7[:, 64:80], T.C8[:], T.FR[:, 16 * h:16 * h + 16], h == 0, h == 1, [fr])
-    for h in range(2):
-        ts(T.QB[:, 128 * h:128 * h + 128], T.I128[:], 0.0, T.FF[:, 2 + h:3 + h], OP.mult, OP.add)
-        js = ts(T.JS[:, 256 * h:256 * h + 256], T.I256[:], T.PF[:, 5 + h:6 + h], None, OP.is_equal, toks=[c_256])
-    for h in range(2):
-        mk = mm(T.P0[:, 256:512], T.QB[:, 128 * h:128 * h + 128], T.JS[:, 256 * h:256 * h + 256], h == 0, h == 1, [js])
-    r0 = ts(T.R0[:], T.MOD16[:, 0:128], 0.0, None, OP.not_equal)
-    flu = cp(T.FL[:], T.P7[:, 64:80], [fl])
-    mask = ts(T.MASK[:], T.P0[:, 256:512], T.PF[:, 2:3], None, OP.is_equal, toks=[mk])
-    ot0 = ms(T.OT[:], 0.0)
+    pop(bg, 99)
 
     arr = [("rA%d" % r, NE) for r in others] + [own]
     tt(T.LS[:, 0:24], T.LAND[:, 0:48:2], T.LAND[:, 17:64:2], OP.add, arr)
     ls = tt(T.LS[:, 24:32], T.LAND[:, 48:64:2], T.LAND[:, 1:16:2], OP.add)
     wn = tr(T.WIN[:], T.LS[:], [ls])
-    gm = run("v", lambda: vec.tensor_tensor(T.GM[:], T.WIN[:, 0:32].indirect(T.FL[:]), T.MASK[:], OP.mult), [wn, flu, mask])
+    gm = run("v", lambda: vec.tensor_tensor(T.GM[:], T.WIN[:, 0:32].indirect(T.FL[:]), T.MASK[:], OP.mult), [wn, tk["flu"], tk["mask"]])
     t2 = tr(T.TR[:], T.GM[:], [gm])
     for h in range(2):
-        sc = run("v", lambda: vec.tensor_tensor_scan(T.SCF[:, 128 * h:128 * h + 128], T.R0[:], T.TR[:, h::2], 0.0, OP.mult, OP.add), [t2, r0])
-    o = cp(T.OT[:, 0:16], T.SCF[:, 15::16], [sc, ot0])
+        sc = tscan(T.SCF[:, 128 * h:128 * h + 128], T.R0[:], T.TR[:, h::2], OP.mult, OP.add, [t2, tk["r0"]])
+    o = cp(T.OT[:, 0:16], T.SCF[:, 15::16], [sc, tk["ot0"]])
     yt = tr(T.YT[:], T.OT[:], [o])
     for a in range(4):
         final.append(dma("y" if a % 2 == 0 else "s", T.y[2 * a:2 * a + 2, :], T.YT[32 * a:32 * a + 16, :], "y%d" % a, [yt]))

from concourse.bass import DstId, RemoteDMATransfer
from concourse.mybir import AluOpType, AxisListType, ActivationFunctionType

V = 6144
W = 6160
KEYS = 4096
INC = 1179648.0
TYP = {"P": 0, "HD": 1, "VT": 2, "AT": 3, "AP": 4}

_f, _b, _i, _u = "float32", "bfloat16", "int32", "uint16"


def _bufs():
    s = {}

    def sb(name, n, t):
        s[name] = ("sbuf", [128, n], t)
    sb("WA", W, _b); sb("WB", W, _b); sb("WV", W, _f); sb("Z8", 16, _b); sb("S0", 384, _b)
    sb("HC", 256, _i); sb("VC", 384, _i); sb("AC", 384, _i); sb("VTC", 384, _i); sb("ATC", 384, _i)
    sb("HHI", 256, _b); sb("HLO", 256, _b); sb("VHI", 384, _b); sb("VLO", 384, _b); sb("AHI", 384, _b); sb("ALO", 384, _b)
    for x in ("VT", "AT"):
        for k in range(3):
            sb("%s%d" % (x, k), 384, _b)
    sb("I128", 128, _b); sb("I256", 256, _b); sb("ZI", 128, _b); sb("MOD16", 128, _b); sb("MOD8", 192, _b); sb("OFF", 8, _b)
    sb("XQ", 256, _b); sb("AQ", 256, _b); sb("PC", 1, _i); sb("C1", 192, _f); sb("C", 192, _f)
    sb("US", 128, _b); sb("UI", 128, _b); sb("IB", 128, _b); sb("S", 1280, _b); sb("RW", 8, _f)
    sb("PINT", 8, _i); sb("COL", 4, _f); sb("EV", 4, _f)
    sb("RK", 2, _i); sb("RT", 2, _i); sb("OWNI", 2, _i); sb("OWNF", 2, _f); sb("KI", 2, _i); sb("KF", 2, _f); sb("TF", 2, _f)
    sb("O", 8, _b); sb("PR", 8, _f); sb("WI", 2, _i); sb("AB", 4, _i); sb("ABF", 4, _f); sb("LHF", 256, _f); sb("RHF", 128, _f)
    sb("LSTU", 32, _u); sb("TLF", 40, _f)
    for r in range(4):
        sb("LI%d" % r, 6, _u); sb("TC%d" % r, 14, _f)
    sb("TOC", 24, _f); sb("TAC", 24, _f)
    sb("G", 384 * 10, _b); sb("SC", 192 * 14, _f); sb("L", 24 * 9, _u); sb("N", 72, _f); sb("E0", 24, _f); sb("E1", 24, _f)
    sb("M0", 24, _u); sb("DWS", 24, _b); sb("DW", 24, _b)
    sb("HN", 168, _f); sb("HIT", 168, _f); sb("CD", 168, _f); sb("ACC", 144, _f); sb("ACI", 48, _i); sb("SEL", 48, _i)
    sb("NON", 24, _f); sb("HX", 48, _f); sb("HY", 48, _f); sb("FM", 48, _f); sb("FS", 48, _f); sb("FC", 48, _f)
    sb("HV", 384, _f); sb("HT", 384, _f); sb("PK", 56, _f); sb("AV", 384, _f); sb("AVT", 384, _f)
    sb("LAND", 64, _f); sb("LS", 32, _f); sb("WIN", 32, _f)
    sb("FI", 4, _i); sb("FF", 4, _f); sb("FR", 32, _b); sb("C8", 128, _b); sb("FL", 16, _u); sb("QB", 256, _b); sb("JS", 512, _b)
    sb("PF", 8, _f); sb("MASK", 256, _f); sb("R0", 128, _f)
    sb("GM", 256, _f); sb("TR", 256, _f); sb("SCF", 256, _f); sb("OT", 32, _f); sb("YT", 32, _f)
    for k in range(8):
        s["P%d" % k] = ("psum", [128, 512], "float32")
    return s


SCRATCH = _bufs()
LOADS = ["rk", "rt", "hd", "vp", "ap", "vt", "at", "hh", "hl", "vh", "vl", "ah", "al", "VT0", "VT1", "VT2", "AT0", "AT1", "AT2",
         "vv", "av", "y0", "y1", "y2", "y3"]
SEMAPHORES = (["sv", "ss", "st", "sg"] + ["d_" + x for x in LOADS]
              + ["r%s%d" % (k, r) for k in "LTA" for r in range(4)] + ["rM", "rAL"]
              + ["xL", "xT", "xM", "xAL", "xA"])
NE = 4
NS = 8
FA = (768, 1536)
GB, VB = (0, 384, 768), 3072
GW = (0, 640, 1280, 1920, 2560, 3200, 3840)


def rank_program(g, core, T, topo):
    me = T.rank_of(core)
    if me is None:
        return
    OP, ACT, X = AluOpType, ActivationFunctionType, AxisListType.X
    n_ranks = len(T.cores)
    nxt = (me + 1) % n_ranks
    eng = {"v": g.vector, "s": g.scalar, "t": g.tensor, "g": g, "y": g.sync}
    semof = {"v": "sv", "s": "ss", "t": "st", "g": "sg"}
    cnt = {"sv": 0, "ss": 0, "st": 0, "sg": 0}
    seen = {q: {} for q in eng}
    vec, act, pe = g.vector, g.scalar, g.tensor

    def wait(q, toks):
        need = {}
        for s, n in toks:
            need[s] = max(need.get(s, 0), n)
        for s in need:
            if seen[q].get(s, 0) < need[s]:
                eng[q].wait_ge(T.sem[s], need[s])
                seen[q][s] = need[s]

    def run(q, fn, toks=()):
        wait(q, toks)
        ins = fn()
        s = semof[q]
        ins.then_inc(T.sem[s], 1)
        cnt[s] += 1
        return (s, cnt[s])

    def dma(q, out, in_, name, toks=()):
        wait(q, toks)
        eng[q].dma_start(out, in_).then_inc(T.sem["d_" + name], 16)
        return ("d_" + name, 16)

    def ts(out, in0, s1, s2, op0, op1=None, toks=()):
        if op1 is None:
            return run("v", lambda: vec.tensor_scalar(out, in0, s1, None, op0), toks)
        return run("v", lambda: vec.tensor_scalar(out, in0, s1, s2, op0, op1), toks)

    def tt(out, a, b, op, toks=()):
        return run("v", lambda: vec.tensor_tensor(out, a, b, op), toks)

    def cp(out, in_, toks=()):
        return run("v", lambda: vec.tensor_copy(out, in_), toks)

    def tr(out, in_, toks=()):
        return run("v", lambda: vec.transpose(out, in_), toks)

    def ms(ap, c, toks=()):
        return run("v", lambda: vec.memset(ap, c), toks)

    def tscan(out, d0, d1, op0, op1, toks=()):
        return run("v", lambda: vec.tensor_tensor_scan(out, d0, d1, 0.0, op0, op1), toks)

    def mm(out, l, r, start, stop, toks=()):
        return run("t", lambda: pe.matmul(out, l, r, start, stop), toks)

    def copy_s(out, in_, toks=()):
        return run("s", lambda: act.activation(out, in_, ACT.Copy), toks)

    def iota(out, pattern, base, cm, toks=(), flag=True):
        if flag:
            return run("g", lambda: g.iota(out, pattern, base, cm, allow_small_or_imprecise_dtypes=True), toks)
        return run("g", lambda: g.iota(out, pattern, base, cm), toks)

    final = []

    def fused(pairs, sem, local):
        free, tl, tot = list(range(16)), [], 0
        for d, src, dst in sorted(pairs, key=lambda x: len(topo.engines(core, T.cores[x[0]]))):
            es = [e for e in topo.engines(core, T.cores[d]) if e in free][:NE]
            free = [e for e in free if e not in es]
            rid, pid = topo.addr(T.cores[d], core)
            tl.append(RemoteDMATransfer(dst_ids=[DstId(rid=rid, pnc=pid)], dma_engine_mask=sum(1 << e for e in es),
                                        remote_sem=T.sem[sem], srcs=[src], dsts=[dst]))
            tot += len(es)
        g.remote_dma_fused(tl, local_sem=T.sem[local])
        final.append((local, tot))

    def send(d, src, dst, sem, local):
        es = topo.engines(core, T.cores[d])[:NS]
        rid, pid = topo.addr(T.cores[d], core)
        g.remote_dma(dst, src, T.sem[sem], T.sem[local], pid, rid, sum(1 << e for e in es))
        final.append((local, NS))

    others = [(me + k) % n_ranks for k in range(1, n_ranks)]

    d_rk = dma("y", T.RK[:], T.rk[:], "rk")
    d_rt = dma("s", T.RT[:], T.rt[:], "rt")
    d_hd = dma("y", T.HC[:], T.hd[:], "hd")
    d_vp = dma("s", T.VC[:], T.vp[:], "vp")
    d_ap = dma("s", T.AC[:], T.ap[:], "ap")
    d_vt = dma("y", T.VTC[:], T.vt[:], "vt")
    d_at = dma("y", T.ATC[:], T.at[:], "at")

    c_pc = iota(T.PC[:], [[0, 1]], 0, 1, flag=False)
    c_zi = iota(T.ZI[:], [[1, 128]], 0, -1)
    c_i = iota(T.I128[:], [[1, 128]], 0, 0)
    c_off = iota(T.OFF[:], [[0, 2], [128, 4]], 0, 0)
    c_xq = [iota(T.XQ[:, 128 * q:128 * q + 128], [[-16, 8], [0, 8], [512 - 1024 * q, 2]], 512 * q, 1) for q in range(2)]
    c_m16 = iota(T.MOD16[:], [[0, 8], [1, 16]], 0, 0)
    c_m8 = iota(T.MOD8[:], [[0, 24], [1, 8]], 0, 0)

    fa, fb, fv = [], [], []
    tk, gpos, spos = {}, [0], [0]
    gjobs = [(w, l, c[i], c[i + 1]) for w, l, c in ((T.WB, fb, GB), (T.WV, fv, GW)) for i in range(len(c) - 1)]
    sjobs = []
    for win, lst, a, step_ in ((T.WA, fa, FA[1], 768), (T.WB, fb, VB, 384), (T.WV, fv, GW[-1], 384)):
        while a < V:
            n = min(step_, V - a)
            sjobs.append((win, lst, a, n))
            a += n

    def gfill(n):
        for _ in range(n):
            if gpos[0] < len(gjobs):
                win, lst, a, b = gjobs[gpos[0]]
                lst.append(iota(win[:, a:b], [[0, b - a]], 0, 0))
                gpos[0] += 1

    def sfill(n):
        for _ in range(n):
            if spos[0] < len(sjobs):
                win, lst, a, k = sjobs[spos[0]]
                if win is T.WA:
                    lst.append(copy_s(win[:, a:a + k], T.WA[:, 0:k], [z]))
                else:
                    lst.append(copy_s(win[:, a:a + k], T.S0[:, 0:k], [s0]))
                spos[0] += 1

    z = ms(T.WA[:, 0:FA[0]], 0.0)
    fa.append(z)
    sfill(sum(1 for j in sjobs if j[0] is T.WA))

    us = ts(T.US[:], T.ZI[:], 0.0, None, OP.is_gt, toks=[c_zi])
    ui = ts(T.UI[:], T.ZI[:], 0.0, None, OP.is_ge)
    ib = ts(T.IB[:], T.ZI[:], 0.0, None, OP.is_equal)
    owni = ts(T.OWNI[:], T.RK[:], 12, None, OP.arith_shift_right, toks=[d_rk])
    k1 = ts(T.KI[:], T.RK[:], 4095, None, OP.bitwise_and)
    ts(T.PINT[:, 0:1], T.PC[:], 15, None, OP.bitwise_and, toks=[c_pc])
    for k in (1, 2):
        ts(T.PINT[:, k:k + 1], T.PC[:], 15, k, OP.bitwise_and, OP.arith_shift_right)
    ownf = cp(T.OWNF[:], T.OWNI[:], [owni])
    kf = cp(T.KF[:], T.KI[:], [k1])
    pi = ts(T.PINT[:, 3:4], T.PC[:], 3, None, OP.bitwise_and)
    ts(T.PINT[:, 4:5], T.PC[:], 7, None, OP.bitwise_and)
    o0 = ts(T.O[:, 0:4], T.I128[:, 0:4], T.OWNF[:, 0:1], None, OP.is_equal, toks=[ownf, c_i])
    o1 = ts(T.O[:, 4:8], T.I128[:, 0:4], T.OWNF[:, 1:2], None, OP.is_equal)
    p, q = T.P0[:, 0:4], T.P1[:, 0:4]
    mm(p, T.IB[:], T.OFF[:, 0:4], True, False, [ib, c_off])
    mm(q, T.IB[:], T.OFF[:, 4:8], True, False)
    mm(p, T.US[:], T.O[:, 0:4], False, False, [o0])
    mm(q, T.UI[:], T.O[:, 0:4], False, False)
    mm(p, T.US[:], T.O[:, 4:8], False, True, [o1])
    pos = mm(q, T.US[:], T.O[:, 4:8], False, True)
    ts(T.EV[:, 0:1], T.PINT[:, 3:4], 0.0, 6144.0, OP.is_equal, OP.mult, toks=[pi])
    e3 = ts(T.EV[:, 1:2], T.PINT[:, 3:4], 3.0, 1048576.0, OP.is_equal, OP.mult)
    tf = cp(T.TF[:], T.RT[:], [d_rt])
    col = ts(T.COL[:, 0:1], T.PINT[:, 1:2], -INC, 7 * INC, OP.mult, OP.add)
    p8 = cp(T.COL[:, 3:4], T.PINT[:, 1:2])
    s0 = ms(T.S0[:], 0.0)
    fa.append(ms(T.WA[:, FA[0]:FA[1]], 0.0))
    smat = {}

    def S(name, q):
        k = 128 * (2 * TYP[name] + q)
        return T.S[:, k:k + 128]

    def weight(name):
        for q in range(2):
            smat[name] = ts(S(name, q), T.AQ[:, 128 * q:128 * q + 128], 8.0, T.RW[:, TYP[name]:TYP[name] + 1], OP.is_le, OP.mult, toks=[rw, aq[1]])

    tt(T.PR[:, 0:4], T.P0[:, 0:4], T.O[:, 0:4], OP.mult, [pos, o1])
    pr = tt(T.PR[:, 4:8], T.P1[:, 0:4], T.O[:, 4:8], OP.mult)
    run("v", lambda: vec.tensor_reduce(T.WI[:, 0:1], T.PR[:, 0:4], X, OP.max), [pr])
    wi = run("v", lambda: vec.tensor_reduce(T.WI[:, 1:2], T.PR[:, 4:8], X, OP.max))
    ts(T.AB[:, 0:2], T.WI[:], 15, None, OP.bitwise_and, toks=[wi])
    ab = ts(T.AB[:, 2:4], T.WI[:], 4, None, OP.arith_shift_right)
    for k, (src, v) in enumerate(((1, 0.0), (1, 1.0), (2, 1.0), (2, 2.0), (1, 6.0))):
        rw = ts(T.RW[:, k:k + 1], T.PINT[:, src:src + 1], v, None, OP.is_equal)
        if k == 3:
            abf = cp(T.ABF[:], T.AB[:], [ab])
    c1 = ts(T.C1[:], T.MOD8[:], T.COL[:, 3:4], -16000000.0, OP.is_equal, OP.mult, toks=[p8, c_m8])
    z8 = ms(T.Z8[:], 0.0)
    eb = tt(T.EV[:, 2:3], T.EV[:, 0:1], T.EV[:, 1:2], OP.add, [e3])
    for h in range(2):
        for e, val in ((0, T.KF), (1, T.TF)):
            k = 64 * h + 32 * e
            ts(T.RHF[:, k:k + 32], T.I128[:, 0:32], T.ABF[:, 2 + h:3 + h], val[:, h:h + 1], OP.is_equal, OP.mult, toks=[abf, kf, tf])
        lt = ts(T.LHF[:, 128 * h:128 * h + 128], T.MOD16[:], T.ABF[:, h:h + 1], None, OP.is_equal, toks=[c_m16])
        lst = mm(T.P7[:, 0:64], T.LHF[:, 128 * h:128 * h + 128], T.RHF[:, 64 * h:64 * h + 64], h == 0, h == 1, [lt])
    hh = cp(T.HHI[:], T.HC[:], [d_hd])
    th_ = mm(T.P4[:, 0:256], T.IB[:], T.HHI[:], True, True, [hh])
    vh = cp(T.VHI[:], T.VC[:], [d_vp])
    tv_ = mm(T.P5[:, 0:384], T.IB[:], T.VHI[:], True, True, [vh])
    fa.append(ts(T.WA[:, V:W], T.Z8[:], T.EV[:, 2:3], None, OP.add, toks=[eb, z8]))
    d_hh = dma("y", T.WA[2:128:16, 0:KEYS], T.HHI[:], "hh", [hh] + fa)
    d_vh = dma("y", T.WA[0:128:16, 0:V], T.VHI[:], "vh", [vh])
    lu = cp(T.LSTU[:], T.P7[:, 0:32], [lst])
    tl0 = cp(T.TLF[:, 8:40], T.P7[:, 32:64])
    tl1 = cp(T.TLF[:, 0:8], T.P7[:, 56:64])
    hl = tt(T.HLO[:], T.HC[:], T.P4[:, 0:256], OP.subtract, [th_])
    d_hl = dma("y", T.WA[3:128:16, 0:KEYS], T.HLO[:], "hl", [hl])
    vl = tt(T.VLO[:], T.VC[:], T.P5[:, 0:384], OP.subtract, [tv_])
    d_vl = dma("y", T.WA[1:128:16, 0:V], T.VLO[:], "vl", [vl])
    WAT = fa + [d_hh, d_hl, d_vh, d_vl]
    tk["c256"] = iota(T.I256[:], [[1, 256]], 0, 0)
    gfill(1)
    wait("g", [lu])
    fused([(d, T.LSTU[:, 8 * d:8 * d + 6], T["LI%d" % me][:]) for d in others], "rL%d" % me, "xL")
    wait("g", [tl1])
    fused([(d, T.TLF[:, 8 * d:8 * d + 14], T["TC%d" % me][:]) for d in others], "rT%d" % me, "xT")
    gfill(5)
    aq = [run("s", lambda q=q: act.activation(T.AQ[:, 128 * q:128 * q + 128], T.XQ[:, 128 * q:128 * q + 128], ACT.Abs, bias=-7.5), [c_xq[q]])
          for q in range(2)]
    cc = run("s", lambda: act.activation(T.C[:], T.C1[:], ACT.Copy, bias=INC), [c1])
    weight("HD")
    sfill(7)
    weight("P")
    ts(T.COL[:, 1:2], T.COL[:, 0:1], 6144.0, None, OP.add, toks=[col])
    cp2 = ts(T.COL[:, 2:3], T.COL[:, 0:1], 12288.0, None, OP.add)
    fb.append(ts(T.WB[:, V:W], T.Z8[:], T.EV[:, 2:3], None, OP.add))
    tk["wv"] = ms(T.WV[:, V:W], 0.0)
    for k, (m, s) in ((5, (127, 3)), (6, (31, 1))):
        ts(T.PINT[:, k:k + 1], T.PC[:], m, s, OP.bitwise_and, OP.arith_shift_right)

    big, bg, wbt, WBT = [], [], [], []

    def conv(fn, name, row, src):
        t = fn()
        tk[name] = t
        wbt.append((name, row, src, t))

    def aph():
        conv(lambda: cp(T.AHI[:], T.AC[:], [d_ap]), "ah", 12, T.AHI)
        tk["map"] = mm(T.P6[:, 0:384], T.IB[:], T.AHI[:], True, True, [tk["ah"]])

    def first(x, src, bank, d, row):
        conv(lambda: cp(T[x + "0"][:], src[:], [d]), x + "0", row, T[x + "0"])
        tk["m" + x] = mm(bank[:, 0:384], T.IB[:], T[x + "0"][:], True, True, [tk[x + "0"], hl, vl])

    def mid(x, src, bank, row):
        conv(lambda: tt(T[x + "1"][:], src[:], bank[:, 0:384], OP.subtract, [tk["m" + x]]), x + "1", row + 1, T[x + "1"])
        mm(bank[:, 0:384], T.IB[:], T[x + "0"][:], True, False, [tk[x + "1"]])
        tk["n" + x] = mm(bank[:, 0:384], T.IB[:], T[x + "1"][:], False, True)

    def last(x, src, bank, row):
        conv(lambda: tt(T[x + "2"][:], src[:], bank[:, 0:384], OP.subtract, [tk["n" + x]]), x + "2", row + 2, T[x + "2"])

    big += [aph, lambda: first("AT", T.ATC, T.P5, d_at, 8),
            lambda: conv(lambda: tt(T.ALO[:], T.AC[:], T.P6[:, 0:384], OP.subtract, [tk["map"]]), "al", 13, T.ALO),
            lambda: first("VT", T.VTC, T.P4, d_vt, 4), lambda: mid("AT", T.ATC, T.P5, 8), lambda: mid("VT", T.VTC, T.P4, 4),
            lambda: last("AT", T.ATC, T.P5, 8), lambda: last("VT", T.VTC, T.P4, 4)]
    for x in ("AP", "AT", "VT"):
        bg.append(lambda x=x: weight(x))

    def tadd(buf, r, off):
        src = T.TLF[:, 8 * me + off:8 * me + off + 6] if r == me else T["TC%d" % r][:, off:off + 6]
        tk["TO" if off else "TA"] = ts(buf[:, 6 * r:6 * r + 6], src, T.COL[:, 0:1], None, OP.add, toks=[tl1 if r == me else ("rT%d" % r, NE), col])
    for off in (8, 0):
        for r in [me] + others:
            bg.append(lambda r=r, off=off: tadd(T.TOC if off else T.TAC, r, off))
    bg.append(lambda: tk.update(fm0=ms(T.FM[:], 0.0)))
    bg.append(lambda: tk.update(pk0=ms(T.PK[:, 48:56], 0.0)))
    bg.append(lambda: ts(T.FI[:, 0:2], T.WI[:], 31, None, OP.bitwise_and))
    bg.append(lambda: tk.update(fi=ts(T.FI[:, 2:4], T.WI[:], 5, None, OP.arith_shift_right)))
    bg.append(lambda: tk.update(pf=cp(T.PF[:, 0:3], T.PINT[:, 4:7])))
    bg.append(lambda: tk.update(ff=cp(T.FF[:], T.FI[:], [tk["fi"]])))
    bg.append(lambda: ts(T.PF[:, 3:4], T.PF[:, 0:1], 2.0, None, OP.mult, toks=[tk["pf"]]))
    bg.append(lambda: ts(T.PF[:, 4:5], T.PF[:, 0:1], 2.0, 1.0, OP.mult, OP.add))
    bg.append(lambda: tk.update(p5=ts(T.PF[:, 5:6], T.PF[:, 0:1], 32.0, T.PF[:, 1:2], OP.mult, OP.add)))
    bg.append(lambda: ts(T.C8[:], T.MOD16[:], T.PF[:, 1:2], None, OP.is_equal))
    bg.append(lambda: tk.update(p6=ts(T.PF[:, 6:7], T.PF[:, 5:6], 16.0, None, OP.add, toks=[tk["p5"]])))
    for h in range(2):
        bg.append(lambda h=h: tk.update(fr=ts(T.FR[:, 16 * h:16 * h + 16], T.I128[:, 0:16], T.PF[:, 3 + h:4 + h], T.FF[:, h:h + 1],
                                              OP.is_equal, OP.mult, toks=[tk["p6"], tk["ff"]])))
    for h in range(2):
        bg.append(lambda h=h: ts(T.QB[:, 128 * h:128 * h + 128], T.I128[:], 0.0, T.FF[:, 2 + h:3 + h], OP.mult, OP.add))
        bg.append(lambda h=h: tk.update(js=ts(T.JS[:, 256 * h:256 * h + 256], T.I256[:], T.PF[:, 5 + h:6 + h], None, OP.is_equal, toks=[tk["c256"]])))

    def place():
        for h in range(2):
            tk["fl"] = mm(T.P7[:, 64:80], T.C8[:], T.FR[:, 16 * h:16 * h + 16], h == 0, h == 1, [tk["fr"], tl1])
        for h in range(2):
            tk["mk"] = mm(T.P0[:, 256:512], T.QB[:, 128 * h:128 * h + 128], T.JS[:, 256 * h:256 * h + 256], h == 0, h == 1, [tk["js"], pr])
        tk["r0"] = ts(T.R0[:], T.MOD16[:], 0.0, None, OP.not_equal)
    bg.append(place)
    bg.append(lambda: tk.update(ot0=ms(T.OT[:], 0.0)))
    bg.append(lambda: tk.update(flu=cp(T.FL[:], T.P7[:, 64:80], [tk["fl"]])))
    bg.append(lambda: tk.update(mask=ts(T.MASK[:], T.P0[:, 256:512], T.PF[:, 2:3], None, OP.is_equal, toks=[tk["mk"]])))

    def pop(jobs, n):
        for _ in range(n):
            if jobs:
                jobs.pop(0)()

    def land():
        while wbt:
            name, row, src, t = wbt.pop(0)
            WBT.append(dma("y", T.WB[row:128:16, 0:V], src[:], name, [t] + fb))

    banks = [T.P2, T.P3]

    def gather(i, h, win, lst, toks, who="s"):
        o = 384 * i + 192 * h
        if who == "s":
            return copy_s(T.G[:, o:o + 192], win.indirect(lst), toks)
        return cp(T.G[:, o:o + 192], win.indirect(lst), toks)

    def spread(bank, c, name, i, h, toks):
        o = 384 * i + 192 * h
        for q in range(2):
            t = mm(bank[:, c:c + 96], S(name, q), T.G[:, o + q:o + 192:2], q == 0, q == 1, toks + [smat[name]])
        return t

    def Ls(i, half):
        return T.L[:, 24 * i + 12 * half:24 * i + 12 * half + 12]

    def scan(i, half, tok):
        o = 192 * i + 96 * half
        t = tscan(T.SC[:, o:o + 96], T.C[:, 0:96], banks[half][:, 0:96], OP.add, OP.max, [tok, cc])
        return t, T.SC[:, o + 7:o + 96:8]

    def scan2(i, src, tok):
        return tscan(T.SC[:, 192 * i:192 * i + 192], T.C[:], src, OP.add, OP.max, [tok, cc])

    def both(i):
        return T.SC[:, 192 * i + 7:192 * i + 192:8]

    def step(i, m, lst):
        ks, ls = [], []
        for h in range(2):
            t, pick = scan(i, h, m[h])
            ks.append(t)
            pop(bg, 1)
            ls.append(lst(h, t, pick))
        return ks, ls

    fb.append(ms(T.WB[:, GB[-1]:VB], 0.0))
    pop(big, 2)
    hg = []
    for k, r in enumerate([me] + others):
        src = T.LSTU[:, 8 * me:8 * me + 6] if r == me else T["LI%d" % r][:]
        tok = lu if r == me else ("rL%d" % r, NE)
        out, inp = T.G[:, 96 * r:96 * r + 96], T.WA[:, 0:KEYS].indirect(src)
        hg.append(cp(out, inp, WAT + [tok]) if k == 3 else copy_s(out, inp, WAT + [tok]))
    m = [spread(banks[h], 0, "HD", 0, h, hg) for h in range(2)]
    sfill(1)
    pop(big, 2)
    land()
    ks, l0 = step(0, m, lambda h, t, pick: ts(Ls(0, h), pick, T.COL[:, 0:1], 6144.0, OP.subtract, OP.min, toks=[t, col]))
    ga = [gather(1, h, T.WA[:], Ls(0, h), WAT + [l0[h]]) for h in range(2)]
    m = [spread(banks[h], 0, "P", 1, h, [ga[h], ks[h]]) for h in range(2)]
    a = ts(T.N[:, 0:24], both(0), T.COL[:, 0:1], 6144.0, OP.subtract, OP.max)
    pop(big, 2)
    e0 = ts(T.E0[:], T.N[:, 0:24], T.COL[:, 1:2], None, OP.subtract, toks=[a, cp2])
    land()

    def l1_(h, t, pick):
        a = tt(T.N[:, 24 + 12 * h:36 + 12 * h], pick, T.E0[:, 12 * h:12 * h + 12], OP.add, [t, e0])
        pop(bg, 1)
        return ts(Ls(1, h), T.N[:, 24 + 12 * h:36 + 12 * h], 6144.0, None, OP.min, toks=[a])
    ks, l1 = step(1, m, l1_)
    ga = [gather(2, h, T.WA[:], Ls(1, h), [l1[h]]) for h in range(2)]
    m = [spread(banks[h], 0, "P", 2, h, [ga[h], ks[h]]) for h in range(2)]
    e1v = ts(T.E1[:], T.N[:, 24:48], 6144.0, T.COL[:, 2:3], OP.max, OP.subtract)
    pop(big, 2)
    land()

    def l2_(h, t, pick):
        a = tt(T.N[:, 48 + 12 * h:60 + 12 * h], pick, T.E1[:, 12 * h:12 * h + 12], OP.add, [t, e1v])
        pop(bg, 1)
        return cp(Ls(2, h), T.N[:, 48 + 12 * h:60 + 12 * h], [a])
    prev, l2 = step(2, m, l2_)
    wait("g", l2)
    send(nxt, T.L[:, 48:72], T.M0[:], "rM", "xM")
    sfill(99)
    gfill(99)
    d_vv = dma("y", T.WV[1:128:16, 0:V], T.vv[:], "vv", fv)
    d_av = dma("y", T.WV[2:128:16, 0:V], T.av[:], "av", fv)
    WVT = fv + [d_vv, d_av, tk["wv"]]
    pop(bg, 12)
    nn = [ts(T.HN[:, 24 * i:24 * i + 24], T.L[:, 24 * i:24 * i + 24], 8192.0 * (2 - i), None, OP.add) for i in range(2)]
    pop(bg, 2)
    st = {}

    def dead():
        dw = ts(T.DWS[:], T.ACC[:, 0:24], 8192.0, 55296.0, OP.is_ge, OP.mult, toks=[st["ha"]])
        wait("g", [dw])
        send(nxt, T.DWS[:], T.DW[:], "rAL", "xAL")
    hq = [lambda: st.update(x0=tt(T.HIT[:, 0:24], both(7), T.TOC[:], OP.is_le, [st["h0"], tk["TO"]])),
          lambda: st.update(x1=tt(T.HIT[:, 24:48], both(8), T.TOC[:], OP.is_le, [st["h1"]])),
          lambda: st.update(c0=tt(T.CD[:, 0:24], T.HIT[:, 0:24], T.HN[:, 0:24], OP.mult, [st["x0"], nn[0]])),
          lambda: st.update(c1=tt(T.CD[:, 24:48], T.HIT[:, 24:48], T.HN[:, 24:48], OP.mult, [st["x1"], nn[1]])),
          lambda: st.update(ha=tt(T.ACC[:, 0:24], T.CD[:, 0:24], T.CD[:, 24:48], OP.max, [st["c0"], st["c1"]])),
          dead,
          lambda: st.update(hm_=ts(T.ACI[:, 0:24], T.ACC[:, 0:24], 6144.0, None, OP.max)),
          lambda: st.update(hs_=ts(T.SEL[:, 0:24], T.ACI[:, 0:24], 8191, None, OP.bitwise_and, toks=[st["hm_"]])),
          lambda: st.update(hl_=cp(T.L[:, 168:192], T.SEL[:, 0:24], [st["hs_"]]))]

    def gap(n):
        for _ in range(n):
            pop(hq if hq and "h1" in st else bg, 1)

    lists = [T.M0[:, 12 * h:12 * h + 12] for h in range(2)]
    num = T.M0[:]
    an = [("rM", NS), ("rM", NS)]
    dq = []
    for k in range(5):
        gk = [gather(5 + k, h, T.WB[:], lists[h], WBT + [an[h]]) for h in range(2)]
        m = []
        for h in range(2):
            if k < 4:
                m.append(spread(banks[h], 0, "AP", 5 + k, h, [gk[h], prev[h]]))
            dm = spread(T.P1, 96 * h, "AT", 5 + k, h, [gk[h], st.get("sd", pr)])
        if k == 0:
            for i in range(2):
                for h in range(2):
                    t = gather(3 + i, h, T.WB[:], Ls(i, h), WBT, ("vv", "sv")[i][h])
                    hm = spread(T.P6, 192 * i + 96 * h, "VT", 3 + i, h, [t, tk["al"]])
        if k == 4:
            break
        o = 48 + 24 * k
        if k < 3:
            ni = ts(T.HN[:, o:o + 24], num, 8192.0 * (4 - k), None, OP.add, toks=an)
        gap(2 if k < 2 else 1)
        lists = [Ls(3 + k, h) for h in range(2)]
        num = T.L[:, 72 + 24 * k:96 + 24 * k]
        an, prev = [], []
        for h in range(2):
            t, pick = scan(3 + k, h, m[h])
            pop(dq, 1)
            gap(2 if k == 1 and h == 0 else 1)
            an.append(ts(lists[h], pick, T.COL[:, 0:1], 6144.0, OP.subtract, OP.min, toks=[t]))
            prev.append(t)
        pop(dq, 9)
        st["sd"] = scan2(9 + k, T.P1[:, 0:192], dm)
        if k == 0:
            for i in range(2):
                st["h%d" % i] = scan2(7 + i, T.P6[:, 192 * i:192 * i + 192], hm)
        if k > 1:
            nk = ts(T.HX[:, 24 * k - 48:24 * k - 24], num, -6144.0, None, OP.add, toks=an)
        if k == 3:
            q4 = tt(T.HY[:, 0:24], T.NON[:], T.HX[:, 0:24], OP.mult, [st["no"], st["n4"]])
            q5 = tt(T.HY[:, 24:48], T.NON[:], T.HX[:, 24:48], OP.mult, [nk])
        else:
            gap(1)
        hit = tt(T.HIT[:, o:o + 24], both(9 + k), T.TAC[:], OP.is_le, [st["sd"], tk["TA"]])
        if k < 3:
            dq.append(lambda o=o, hit=hit, ni=ni: st.update(c=tt(T.CD[:, o:o + 24], T.HIT[:, o:o + 24], T.HN[:, o:o + 24], OP.mult, [hit, ni])))
        if k == 0:
            dq.append(lambda: st.update(acc=ts(T.ACC[:, 24:48], T.CD[:, 48:72], 6144.0, None, OP.max, toks=[st["c"]])))
        elif k == 1:
            dq.append(lambda: st.update(acc=tt(T.ACC[:, 48:72], T.ACC[:, 24:48], T.CD[:, 72:96], OP.max, [st["c"], st["acc"]])))
        elif k == 2:
            st["n4"] = nk
            gap(len(hq))
            a = tt(T.ACC[:, 72:96], T.ACC[:, 48:72], T.DW[:], OP.max, [st["acc"], ("rAL", NS)])
            pop(dq, 1)
            gap(1)
            a = tt(T.ACI[:, 24:48], T.ACC[:, 72:96], T.CD[:, 96:120], OP.max, [a, st["c"]])
            dq.append(lambda a=a: st.update(no=ts(T.NON[:], T.ACI[:, 24:48], 8192.0, None, OP.is_lt, toks=[a])))
            dq.append(lambda a=a: st.update(s=ts(T.SEL[:, 24:48], T.ACI[:, 24:48], 8191, None, OP.bitwise_and, toks=[a])))
        else:
            x4 = tt(T.CD[:, 120:144], T.HIT[:, 120:144], T.HY[:, 0:24], OP.mult, [hit, q4])
            r5 = tt(T.CD[:, 144:168], T.HIT[:, 120:144], T.HY[:, 24:48], OP.mult, [q5])
            gap(2)
            s4 = tt(T.FS[:, 1:48:2], T.CD[:, 120:144], T.SEL[:, 24:48], OP.add, [x4, st["s"]])
            m5 = tt(T.FM[:, 1:48:2], T.HY[:, 24:48], T.CD[:, 144:168], OP.subtract, [r5, tk["fm0"]])
    hv = [copy_s(T.HV[:, 192 * h:192 * h + 192], T.WV[:].indirect(Ls(7, h)), WVT + [st["hl_"]]) for h in range(2)]
    sd = scan2(13, T.P1[:, 0:192], dm)
    t0 = tr(T.HT[:, 0:192], T.HV[:, 0:192], [hv[0]])
    h5 = tt(T.FS[:, 0:48:2], both(13), T.TAC[:], OP.is_le, [sd, m5])
    t1 = tr(T.HT[:, 192:384], T.HV[:, 192:384], [hv[1]])
    y5 = tscan(T.FC[:], T.FM[:], T.FS[:], OP.mult, OP.add, [h5, s4])
    ph = cp(T.PK[:, 0:48:2], T.HT[:, 1::16], [t0, t1])
    asel = cp(T.L[:, 192:216], T.FC[:, 1:48:2], [y5])
    va = copy_s(T.AV[:, 0:192], T.WV[:].indirect(Ls(8, 0)), WVT + [asel])
    vb = cp(T.AV[:, 192:384], T.WV[:].indirect(Ls(8, 1)), WVT + [asel])
    t1 = tr(T.AVT[:, 192:384], T.AV[:, 192:384], [vb])
    t0 = tr(T.AVT[:, 0:192], T.AV[:, 0:192], [va])
    pa = cp(T.PK[:, 1:48:2], T.AVT[:, 2::16], [t0, t1])
    wait("g", [ph, pa, tk["pk0"]])
    fused([(d, T.PK[:, 12 * d:12 * d + 16], T.LAND[:, 16 * me:16 * me + 16]) for d in others], "rA%d" % me, "xA")
    own = cp(T.LAND[:, 16 * me:16 * me + 16], T.PK[:, 12 * me:12 * me + 16], [ph, pa])
    pop(bg, 99)

    arr = [("rA%d" % r, NE) for r in others] + [own]
    tt(T.LS[:, 0:24], T.LAND[:, 0:48:2], T.LAND[:, 17:64:2], OP.add, arr)
    ls = tt(T.LS[:, 24:32], T.LAND[:, 48:64:2], T.LAND[:, 1:16:2], OP.add)
    wn = tr(T.WIN[:], T.LS[:], [ls])
    gm = run("v", lambda: vec.tensor_tensor(T.GM[:], T.WIN[:, 0:32].indirect(T.FL[:]), T.MASK[:], OP.mult), [wn, tk["flu"], tk["mask"]])
    t2 = tr(T.TR[:], T.GM[:], [gm])
    for h in range(2):
        sc = tscan(T.SCF[:, 128 * h:128 * h + 128], T.R0[:], T.TR[:, h::2], OP.mult, OP.add, [t2, tk["r0"]])
    o = cp(T.OT[:, 0:16], T.SCF[:, 15::16], [sc, tk["ot0"]])
    yt = tr(T.YT[:], T.OT[:], [o])
    for a in range(4):
        final.append(dma("y" if a % 2 == 0 else "s", T.y[2 * a:2 * a + 2, :], T.YT[32 * a:32 * a + 16, :], "y%d" % a, [yt]))
    wait("g", final + [(s, n) for s, n in cnt.items()])
